import numpy as np
import ml_dtypes


def mxq(x, axis, fmt="e4m3"):
    dtype, down = {"e4m3": (ml_dtypes.float8_e4m3fn, 7), "e5m2": (ml_dtypes.float8_e5m2, 14)}[fmt]
    v = np.moveaxis(np.asarray(x, np.float32).astype(ml_dtypes.bfloat16).astype(np.float64), axis, -1)
    blocks = v.reshape(v.shape[:-1] + (-1, 32))
    amax = np.abs(blocks).max(-1, keepdims=True)
    byte = np.maximum(np.where(amax > 0, np.frexp(amax)[1] - 1 + 127, 0) - down, 1)
    scale = np.exp2(byte - 127.0)
    codes = (blocks / scale).astype(np.float32).astype(dtype).astype(np.float64)
    return np.moveaxis((codes * scale).reshape(v.shape), -1, axis)


WIDE = False


def mx_kscale(k):
    if not WIDE:
        return np.ones(k)
    levels = np.array([10, -10, 5, -5, 0])
    if k % 512:
        return np.exp2(np.random.permutation(np.resize(levels, k // 32))).repeat(32)
    a = np.empty((k // 512, 16))
    for p in range(k // 512):
        a[p, :8] = np.random.permutation(np.resize(levels, 8))
        for g in range(8):
            far = levels[np.abs(levels - a[p, g]) >= 10]
            a[p, g + 8] = far[np.random.randint(len(far))]
    return np.exp2(a.ravel()).repeat(32)


def f64(x):
    return np.asarray(x).astype(np.float64)


def striped(idx):
    return np.tile(np.asarray(idx).reshape(-1, 16).T, (8, 1)).astype(np.uint16)


def unstriped(offs):
    return offs[:16].T.reshape(-1).astype(np.int64)


B, N, T, D, DV, NQ = 2, 512, 2048, 512, 256, 128


def setup_inputs():
    n = np.random.standard_normal
    seg = T // B
    idx = np.concatenate([b * seg + np.random.permutation(seg)[:N] for b in range(B)])
    s = mx_kscale(D)[:, None]
    u = np.ones(T)
    u[idx] = mx_kscale(B * N)
    r = np.random.uniform(0.5, 2.0, T)
    k = n((D, T)) / s
    v = n((DV, T)) / (u * r)
    return {
        "qT": (n((B, D, NQ)) * s * (0.80 / np.sqrt(D))).astype(np.float32),
        "kT": k.astype(np.float32),
        "vT": v.astype(np.float32),
        "vs": np.tile(u * r, (128, 1)).astype(np.float32),
        "offs": striped(idx),
    }


def reference(qT, kT, vT, vs, offs):
    idx = unstriped(offs)
    k = f64(kT)
    v = f64(vT)
    pick = lambda x: x[:, idx].reshape(x.shape[0], B, N).transpose(1, 0, 2)
    q = f64(qT)
    score = mxq(q, 1, "e4m3").transpose(0, 2, 1) @ mxq(pick(k), 1, "e4m3")
    p = np.square(np.maximum(score, 0.0))
    total = p.sum(-1, keepdims=True) + 1.0
    w = p * pick(f64(vs))[:, :1, :]
    y = mxq(w, 2, "e4m3") @ mxq(pick(v).transpose(0, 2, 1), 1, "e4m3")
    y = y / total
    return y

@@ -1,0 +1,390 @@
+from contextlib import ExitStack
+
+import concourse.mybir as mybir
+from concourse.masks import make_identity
+
+B, NQ, N, T, D, DV = 2, 128, 512, 2048, 512, 256
+P = 128
+PACK = 4
+SEG = T // B
+HALF = DV // 2
+
+F32 = mybir.dt.float32
+BF16 = mybir.dt.bfloat16
+U32 = mybir.dt.uint32
+U16 = mybir.dt.uint16
+U8 = mybir.dt.uint8
+FP8X4 = mybir.dt.float8_e4m3fn_x4
+COPY = mybir.ActivationFunctionType.Copy
+RELU = mybir.ActivationFunctionType.Relu
+SQUARE = mybir.ActivationFunctionType.Square
+ADD = mybir.AluOpType.add
+MAX = mybir.AluOpType.max
+MULT = mybir.AluOpType.mult
+
+FLOPS = 2 * B * NQ * N * (D + DV)
+BYTES = 4 * (B * D * NQ + D * T + DV * T + T + B * NQ * DV) + 2 * P * (B * N // 16)
+
+
+def tile_attend_relu2_seg_kernel(tc, qT, kT, vT, vs, offs, out):
+    nc = tc.nc
+    with ExitStack() as ctx:
+        keep = ctx.enter_context(tc.tile_pool(name="keep", bufs=1))
+        turn_pool = ctx.enter_context(tc.psum_pool(name="turns", bufs=4))
+        score_pool = ctx.enter_context(tc.psum_pool(name="scores", bufs=2))
+        y_pool = ctx.enter_context(tc.psum_pool(name="ys", bufs=2))
+
+        offsets = keep.tile([P, B * N // 16], U16, name="offsets")
+        vs_tab = keep.tile([P, T], F32, name="vs_tab")
+        ident = keep.tile([P, P], F32, name="ident")
+        warm = keep.tile([P, 8], F32, name="warm")
+        q_raw = keep.tile([P, B, PACK * NQ], F32, name="q_raw")
+        v_raw = keep.tile([P, 2, T], F32, name="v_raw")
+        k_raw = [[keep.tile([P, 2, SEG], F32, name="k_raw%d%d" % (u, b)) for u in range(2)] for b in range(B)]
+        k_pairs = [keep.tile([P, T, 2], BF16, name="k_pairs%d" % u, align_bytes=64) for u in range(2)]
+        q_in = keep.tile([P, B, NQ, PACK], BF16, name="q_in", align_bytes=64)
+        q_codes = keep.tile([P, B * NQ], U32, name="q_codes", align_bytes=64)
+        q_scales = keep.tile([P, B * NQ], U8, name="q_scales", align_bytes=64)
+        vs_got = keep.tile([P, B * N], F32, name="vs_got")
+        vs_cols = keep.tile([P, B * PACK], F32, name="vs_cols")
+        v_pairs = keep.tile([P, T, 2], BF16, name="v_pairs", align_bytes=64)
+        v_words = [keep.tile([P, PACK, P], U32, name="v_words%d" % b, align_bytes=64) for b in range(B)]
+        v_got = [[keep.tile([P, N], F32, name="v_got%d%d" % (b, h)) for h in range(2)] for b in range(B)]
+        v_codes = [keep.tile([P, DV], U32, name="v_codes%d" % b, align_bytes=64) for b in range(B)]
+        v_scales = [keep.tile([P, DV], U8, name="v_scales%d" % b, align_bytes=64) for b in range(B)]
+        v_in = [keep.tile([P, DV, PACK], BF16, name="v_in%d" % b, align_bytes=64) for b in range(B)]
+        k_in = [keep.tile([P, PACK, P, 2], U32, name="k_in%d" % b, align_bytes=64) for b in range(B)]
+        k_got = [keep.tile([P, 2, PACK, P], U32, name="k_got%d" % b, align_bytes=64) for b in range(B)]
+        k_codes = [keep.tile([P, N], U32, name="k_codes%d" % b, align_bytes=64) for b in range(B)]
+        k_scales = [keep.tile([P, N], U8, name="k_scales%d" % b, align_bytes=64) for b in range(B)]
+        scaled = [keep.tile([P, PACK, NQ], F32, name="scaled%d" % b) for b in range(B)]
+        shaped = [keep.tile([P, NQ, PACK], F32, name="shaped%d" % b) for b in range(B)]
+        positive = [keep.tile([P, PACK, NQ], F32, name="positive%d" % b) for b in range(B)]
+        squares = [keep.tile([P, PACK, P], F32, name="squares%d" % b) for b in range(B)]
+        w_in = [keep.tile([P, NQ, PACK], BF16, name="w_in%d" % b, align_bytes=64) for b in range(B)]
+        w_codes = [keep.tile([P, NQ], U32, name="w_codes%d" % b, align_bytes=64) for b in range(B)]
+        w_scales = [keep.tile([P, NQ], U8, name="w_scales%d" % b, align_bytes=64) for b in range(B)]
+        total = [keep.tile([P, 1], F32, name="total%d" % b) for b in range(B)]
+        total1 = [keep.tile([P, 1], F32, name="total1%d" % b) for b in range(B)]
+        recip = [keep.tile([P, 1], F32, name="recip%d" % b) for b in range(B)]
+        y_sb = [keep.tile([P, DV], F32, name="y_sb%d" % b) for b in range(B)]
+        bank = {}
+        kv = kT.rearrange("(p j) n -> p j n", j=PACK)
+
+        def listed(b):
+            return offsets[:, b * (N // 16) : (b + 1) * (N // 16)]
+
+        def load_scales():
+            nc.sync.dma_start(vs_tab[0:1, :], vs[0:1, :])
+
+        def load_queries():
+            nc.sync.dma_start(q_raw[:], qT.rearrange("b (p j) q -> p b (j q)", j=PACK))
+
+        def load_values(b, h):
+            nc.sync.dma_start(v_raw[:, h, b * SEG : (b + 1) * SEG], vT[h * P : (h + 1) * P, b * SEG : (b + 1) * SEG])
+
+        def load_keys(b, u, a0, a1):
+            nc.sync.dma_start(k_raw[b][u][:, :, a0:a1], kv[:, 2 * u : 2 * u + 2, b * SEG + a0 : b * SEG + a1])
+
+        def load_offsets():
+            nc.sync.dma_start(offsets[:], offs)
+
+        def cast_queries(b):
+            nc.scalar.activation(q_in[:, b, :, :], q_raw[:, b, :].rearrange("p (j q) -> p q j", j=PACK), COPY)
+
+        def cast_queries_gpsimd():
+            for b in range(B):
+                nc.gpsimd.tensor_scalar(
+                    q_in[:, b, :, :], q_raw[:, b, :].rearrange("p (j q) -> p q j", j=PACK), 1.0, 0.0, op0=MULT, op1=ADD
+                )
+
+        def quantize_queries():
+            nc.vector.quantize_mx(
+                out=q_codes[:].bitcast(FP8X4), scales=q_scales[:], in_=q_in[:].rearrange("p b q j -> p (b q j)")
+            )
+
+        def gather_scales():
+            nc.vector.tensor_copy(vs_got[:], vs_tab[:].indirect(offsets[:]))
+
+        def turn(key, source):
+            turned = turn_pool.tile([P, PACK, P], F32, name="turned")
+            for t in range(PACK):
+                nc.tensor.transpose(turned[:, t, :], source(t), ident[:])
+            bank[key] = turned
+
+        def turn_scales():
+            turned = turn_pool.tile([P, PACK, P], F32, name="turned")
+            flat = turned[:].rearrange("s t e -> s (t e)")
+            for k in range(B * PACK):
+                b, t = divmod(k, PACK)
+                nc.tensor.transpose(flat[:, 2 * k : 2 * k + P], vs_got[:, b * N + t : (b + 1) * N : PACK], ident[:])
+            bank["vs"] = flat
+
+        def take_scales(engine):
+            source = bank["vs"][:, 0 : 2 * B * PACK : 2]
+            if engine == "S":
+                nc.scalar.activation(vs_cols[:], source, COPY)
+            else:
+                nc.vector.tensor_copy(vs_cols[:], source)
+
+        def load_value_tokens(b, a0, a1):
+            n0, n1 = b * SEG + a0, b * SEG + a1
+            nc.sync.dma_start(v_raw[:, :, n0:n1], vT.rearrange("(h p) n -> p h n", h=2)[:, :, n0:n1])
+
+        def cast_values(b, a0, a1, engine):
+            dst = v_pairs[:, b * SEG + a0 : b * SEG + a1, :]
+            source = v_raw[:, :, b * SEG + a0 : b * SEG + a1].rearrange("p h n -> p n h")
+            if engine == "S":
+                nc.scalar.activation(dst, source, COPY)
+            else:
+                nc.vector.tensor_copy(dst, source)
+
+        def gather_value_words(b):
+            words = v_pairs[:].rearrange("p n e -> p (n e)").bitcast(U32)
+            window = words[:, 0:SEG] if b == 0 else words
+            nc.vector.tensor_copy(v_words[b][:].rearrange("p t s -> p s t"), window.indirect(listed(b)))
+
+        def turn_value_words(b):
+            turn(("v", b), lambda t: v_words[b][:, t, :].bitcast(F32))
+
+        def settle_value_words(b, h, engine):
+            pairs = bank[("v", b)][:].rearrange("s t p -> s (t p)").bitcast(BF16)
+            pairs = pairs.rearrange("s (t p h) -> s h p t", t=PACK, h=2)
+            if h is None:
+                target, source = v_in[b][:].rearrange("s (h p) t -> s h p t", h=2), pairs
+            else:
+                target, source = v_in[b][:, h * HALF : (h + 1) * HALF, :], pairs[:, h, :, :]
+            if engine == "S":
+                nc.scalar.copy(target, source)
+            else:
+                nc.vector.tensor_copy(target, source)
+
+        def gather_values(b, h):
+            window = v_raw[:, h, 0:SEG] if b == 0 else v_raw[:, h, :]
+            nc.vector.tensor_copy(v_got[b][h][:], window.indirect(listed(b)))
+
+        def turn_values(b, h):
+            turn(("v", b, h), lambda t: v_got[b][h][:, t:N:PACK])
+
+        def settle_values(b, h, e0, e1, engine):
+            target = v_in[b][:, h * HALF + e0 : h * HALF + e1, :]
+            source = bank[("v", b, h)][:, :, e0:e1].rearrange("s t e -> s e t")
+            if engine == "S":
+                nc.scalar.activation(target, source, COPY)
+            else:
+                nc.vector.tensor_copy(target, source)
+
+        def quantize_values(b, e0, e1):
+            nc.vector.quantize_mx(
+                out=v_codes[b][:, e0:e1].bitcast(FP8X4),
+                scales=v_scales[b][:, e0:e1],
+                in_=v_in[b][:, e0:e1, :].rearrange("s e t -> s (e t)"),
+            )
+
+        def cast_keys(b, u, a0, a1, engine):
+            dst = k_pairs[u][:, b * SEG + a0 : b * SEG + a1, :]
+            source = k_raw[b][u][:, :, a0:a1].rearrange("p e n -> p n e")
+            if engine == "S":
+                nc.scalar.activation(dst, source, COPY)
+            else:
+                nc.vector.tensor_copy(dst, source)
+
+        def gather_keys(b, u):
+            words = k_pairs[u][:].rearrange("p n e -> p (n e)").bitcast(U32)
+            window = words[:, 0:SEG] if b == 0 else words
+            nc.vector.tensor_copy(k_in[b][:, :, :, u].rearrange("p t s -> p s t"), window.indirect(listed(b)))
+
+        def gather_keys_apart(b, u):
+            words = k_pairs[u][:].rearrange("p n e -> p (n e)").bitcast(U32)
+            window = words[:, 0:SEG] if b == 0 else words
+            nc.vector.tensor_copy(k_got[b][:, u, :, :].rearrange("p t s -> p s t"), window.indirect(listed(b)))
+
+        def lay_keys(b, engine):
+            target = k_in[b][:].rearrange("p t s u -> p (t s) u")
+            source = k_got[b][:].rearrange("p u t s -> p (t s) u")
+            if engine == "V":
+                nc.vector.tensor_copy(target, source)
+            else:
+                nc.gpsimd.tensor_copy(target, source)
+
+        def quantize_keys(b):
+            nc.vector.quantize_mx(
+                out=k_codes[b][:].bitcast(FP8X4),
+                scales=k_scales[b][:],
+                in_=k_in[b][:].rearrange("p t s u -> p (t s u)").bitcast(BF16),
+            )
+
+        def score(b):
+            scores = score_pool.tile([P, PACK, NQ], F32, name="scores")
+            for t in range(PACK):
+                nc.tensor.matmul_mx(
+                    out=scores[:, t, :],
+                    lhsT=k_codes[b][:, t * P : (t + 1) * P].bitcast(FP8X4),
+                    lhsT_scale=k_scales[b][:, t * P : (t + 1) * P],
+                    rhs=q_codes[:, b * NQ : (b + 1) * NQ].bitcast(FP8X4),
+                    rhs_scale=q_scales[:, b * NQ : (b + 1) * NQ],
+                    start=True,
+                    stop=True,
+                )
+            bank[("s", b)] = scores
+
+        def relu(b):
+            nc.scalar.activation(positive[b][:], bank[("s", b)][:], RELU)
+
+        def scale_scores(b, t):
+            nc.scalar.activation(scaled[b][:, t, :], bank[("s", b)][:, t, :], COPY, scale=vs_cols[:, b * PACK + t : b * PACK + t + 1])
+
+        def square(b, engine):
+            if engine == "S":
+                nc.scalar.activation(scaled[b][:], positive[b][:], SQUARE)
+            elif engine == "G":
+                nc.gpsimd.tensor_tensor(scaled[b][:], positive[b][:], positive[b][:], MULT)
+            else:
+                nc.vector.scalar_tensor_tensor(
+                    out=scaled[b][:], in0=bank[("s", b)][:], scalar=0.0, in1=positive[b][:], op0=MAX, op1=MULT
+                )
+
+        def spread(b):
+            return vs_cols[:, b * PACK : (b + 1) * PACK].unsqueeze(1).to_broadcast([P, NQ, PACK])
+
+        def by_query(tile):
+            return tile[:].rearrange("s t q -> s q t")
+
+        def scale_positive(b):
+            nc.vector.scalar_tensor_tensor(
+                out=shaped[b][:], in0=by_query(bank[("s", b)]), scalar=0.0, in1=spread(b), op0=MAX, op1=MULT
+            )
+
+        def weigh(b, form):
+            if form == "v":
+                nc.vector.scalar_tensor_tensor(
+                    out=w_in[b][:], in0=by_query(bank[("s", b)]), scalar=0.0, in1=shaped[b][:], op0=MAX, op1=MULT
+                )
+            elif form == "z":
+                nc.vector.scalar_tensor_tensor(
+                    out=w_in[b][:], in0=by_query(bank[("s", b)]), scalar=0.0, in1=by_query(scaled[b]), op0=MAX, op1=MULT
+                )
+            elif form in ("g", "G"):
+                nc.gpsimd.tensor_tensor(w_in[b][:], by_query(scaled[b]), spread(b), MULT)
+            else:
+                nc.vector.tensor_tensor(w_in[b][:], by_query(scaled[b]), spread(b), MULT)
+
+        def quantize_weights(b):
+            nc.vector.quantize_mx(
+                out=w_codes[b][:].bitcast(FP8X4), scales=w_scales[b][:], in_=w_in[b][:].rearrange("s q t -> s (q t)")
+            )
+
+        def turn_positive(b):
+            turn(("p", b), lambda t: positive[b][:, t, :])
+
+        def sum_weights(b):
+            nc.scalar.activation(squares[b][:], bank[("p", b)][:], SQUARE, accum_out=total[b][:])
+
+        def add_one(b):
+            nc.gpsimd.tensor_scalar(total1[b][:], total[b][:], 1.0, None, op0=ADD)
+
+        def invert_total(b):
+            nc.vector.reciprocal(recip[b][:], total1[b][:])
+
+        def multiply_values(b, e0, e1):
+            y = y_pool.tile([P, DV], F32, name="y")
+            nc.tensor.matmul_mx(
+                out=y[:, 0 : e1 - e0],
+                lhsT=w_codes[b][:].bitcast(FP8X4),
+                lhsT_scale=w_scales[b][:],
+                rhs=v_codes[b][:, e0:e1].bitcast(FP8X4),
+                rhs_scale=v_scales[b][:, e0:e1],
+                start=True,
+                stop=True,
+            )
+            bank[("y", b, e0)] = y
+
+        def settle_output(b, e0, e1):
+            nc.scalar.activation(y_sb[b][:, e0:e1], bank[("y", b, e0)][:, 0 : e1 - e0], COPY, scale=recip[b][:])
+
+        def store_output(b, e0, e1):
+            nc.scalar.dma_start(out[b][:, e0:e1], y_sb[b][:, e0:e1])
+
+        nc.vector.memset(warm[:], 0.0)
+        nc.scalar.activation(warm[:, 4:8], warm[:, 0:4], SQUARE)
+        nc.gpsimd.memset(vs_tab[:, 0:1280], 0.0)
+        nc.vector.memset(vs_tab[:, 1280:T], 0.0)
+        load_offsets()
+        load_keys(0, 0, 0, 512)
+        make_identity(nc, ident[:])
+        load_scales()
+        load_keys(0, 0, 512, 1024)
+        load_keys(0, 1, 384, 1024)
+        cast_keys(0, 0, 0, 512, "S")
+        gather_scales()
+        load_keys(0, 1, 0, 384)
+        load_keys(1, 1, 0, 256)
+        cast_keys(0, 0, 512, 1024, "S")
+        load_keys(1, 0, 384, 1024)
+        cast_keys(0, 1, 384, 784, "S")
+        cast_keys(0, 1, 784, 1024, "V")
+        turn_scales()
+        load_keys(1, 0, 0, 384)
+        gather_keys_apart(0, 0)
+        cast_keys(0, 1, 0, 384, "S")
+        load_keys(1, 1, 256, 512)
+        take_scales("V")
+        load_keys(1, 1, 512, 1024)
+        cast_keys(1, 1, 0, 256, "S")
+        gather_keys_apart(0, 1)
+        load_queries()
+        cast_keys(1, 0, 384, 1024, "S")
+        cast_keys(1, 0, 144, 384, "V")
+        lay_keys(0, "V")
+        quantize_keys(0)
+        load_value_tokens(0, 0, 640)
+        cast_keys(1, 0, 0, 144, "S")
+        load_value_tokens(0, 640, 1024)
+        cast_keys(1, 1, 256, 512, "V")
+        gather_keys_apart(1, 0)
+        cast_queries_gpsimd()
+        load_values(1, 1)
+        cast_keys(1, 1, 512, 1024, "S")
+        load_values(1, 0)
+        cast_values(0, 0, 640, "S")
+        gather_keys_apart(1, 1)
+        quantize_queries()
+        lay_keys(1, "V")
+        quantize_keys(1)
+        score(0)
+        cast_values(0, 640, 1024, "S")
+        gather_values(1, 1)
+        score(1)
+        relu(0)
+        gather_value_words(0)
+        relu(1)
+        square(0, "G")
+        turn_positive(0)
+        turn_values(1, 1)
+        sum_weights(0)
+        turn_positive(1)
+        gather_values(1, 0)
+        turn_value_words(0)
+        square(1, "S")
+        add_one(0)
+        weigh(0, "G")
+        settle_values(1, 1, 0, 64, "S")
+        weigh(1, "p")
+        turn_values(1, 0)
+        settle_value_words(0, None, "S")
+        invert_total(0)
+        settle_values(1, 1, 64, 128, "V")
+        quantize_weights(1)
+        quantize_weights(0)
+        settle_values(1, 0, 0, 128, "S")
+        quantize_values(0, 0, DV)
+        sum_weights(1)
+        quantize_values(1, 0, 256)
+        multiply_values(0, 0, 256)
+        multiply_values(1, 0, 256)
+        settle_output(0, 0, 256)
+        add_one(1)
+        invert_total(1)
+        store_output(0, 0, 256)
+        settle_output(1, 0, 256)
+        store_output(1, 0, 256)

@@ -18,9 +18,10 @@ FP8X4 = mybir.dt.float8_e4m3fn_x4
 COPY = mybir.ActivationFunctionType.Copy
 RELU = mybir.ActivationFunctionType.Relu
 SQUARE = mybir.ActivationFunctionType.Square
-ADD = mybir.AluOpType.add
 MAX = mybir.AluOpType.max
 MULT = mybir.AluOpType.mult
+ADD = mybir.AluOpType.add
+POW = mybir.AluOpType.pow
 
 FLOPS = 2 * B * NQ * N * (D + DV)
 BYTES = 4 * (B * D * NQ + D * T + DV * T + T + B * NQ * DV) + 2 * P * (B * N // 16)
@@ -39,34 +40,32 @@ def tile_attend_relu2_seg_kernel(tc, qT, kT, vT, vs, offs, out):
         ident = keep.tile([P, P], F32, name="ident")
         warm = keep.tile([P, 8], F32, name="warm")
         q_raw = keep.tile([P, B, PACK * NQ], F32, name="q_raw")
-        v_raw = keep.tile([P, 2, T], F32, name="v_raw")
-        k_raw = [[keep.tile([P, 2, SEG], F32, name="k_raw%d%d" % (u, b)) for u in range(2)] for b in range(B)]
-        k_pairs = [keep.tile([P, T, 2], BF16, name="k_pairs%d" % u, align_bytes=64) for u in range(2)]
         q_in = keep.tile([P, B, NQ, PACK], BF16, name="q_in", align_bytes=64)
         q_codes = keep.tile([P, B * NQ], U32, name="q_codes", align_bytes=64)
         q_scales = keep.tile([P, B * NQ], U8, name="q_scales", align_bytes=64)
         vs_got = keep.tile([P, B * N], F32, name="vs_got")
         vs_cols = keep.tile([P, B * PACK], F32, name="vs_cols")
-        v_pairs = keep.tile([P, T, 2], BF16, name="v_pairs", align_bytes=64)
-        v_words = [keep.tile([P, PACK, P], U32, name="v_words%d" % b, align_bytes=64) for b in range(B)]
-        v_got = [[keep.tile([P, N], F32, name="v_got%d%d" % (b, h)) for h in range(2)] for b in range(B)]
-        v_codes = [keep.tile([P, DV], U32, name="v_codes%d" % b, align_bytes=64) for b in range(B)]
-        v_scales = [keep.tile([P, DV], U8, name="v_scales%d" % b, align_bytes=64) for b in range(B)]
-        v_in = [keep.tile([P, DV, PACK], BF16, name="v_in%d" % b, align_bytes=64) for b in range(B)]
-        k_in = [keep.tile([P, PACK, P, 2], U32, name="k_in%d" % b, align_bytes=64) for b in range(B)]
-        k_got = [keep.tile([P, 2, PACK, P], U32, name="k_got%d" % b, align_bytes=64) for b in range(B)]
+        k_raw = [[keep.tile([P, 2, SEG], F32, name="k_raw%d%d" % (b, u)) for u in range(2)] for b in range(B)]
+        k_pairs = [keep.tile([P, T, 2], BF16, name="k_pairs%d" % u, align_bytes=64) for u in range(2)]
+        k_got = [keep.tile([P, 2, N], U32, name="k_got%d" % b, align_bytes=64) for b in range(B)]
+        k_in = [keep.tile([P, N, 2], U32, name="k_in%d" % b, align_bytes=64) for b in range(B)]
         k_codes = [keep.tile([P, N], U32, name="k_codes%d" % b, align_bytes=64) for b in range(B)]
         k_scales = [keep.tile([P, N], U8, name="k_scales%d" % b, align_bytes=64) for b in range(B)]
-        scaled = [keep.tile([P, PACK, NQ], F32, name="scaled%d" % b) for b in range(B)]
-        shaped = [keep.tile([P, NQ, PACK], F32, name="shaped%d" % b) for b in range(B)]
-        positive = [keep.tile([P, PACK, NQ], F32, name="positive%d" % b) for b in range(B)]
-        squares = [keep.tile([P, PACK, P], F32, name="squares%d" % b) for b in range(B)]
-        w_in = [keep.tile([P, NQ, PACK], BF16, name="w_in%d" % b, align_bytes=64) for b in range(B)]
-        w_codes = [keep.tile([P, NQ], U32, name="w_codes%d" % b, align_bytes=64) for b in range(B)]
-        w_scales = [keep.tile([P, NQ], U8, name="w_scales%d" % b, align_bytes=64) for b in range(B)]
-        total = [keep.tile([P, 1], F32, name="total%d" % b) for b in range(B)]
-        total1 = [keep.tile([P, 1], F32, name="total1%d" % b) for b in range(B)]
-        recip = [keep.tile([P, 1], F32, name="recip%d" % b) for b in range(B)]
+        v0_raw = [keep.tile([P, SEG], F32, name="v0_raw%d" % h, align_bytes=64) for h in range(2)]
+        v0_got = [keep.tile([P, N], BF16, name="v0_got%d" % h, align_bytes=64) for h in range(2)]
+        v1_raw = keep.tile([P, 2, SEG], F32, name="v1_raw")
+        v1_pairs = keep.tile([P, T, 2], BF16, name="v1_pairs", align_bytes=64)
+        v1_got = keep.tile([P, PACK, P], U32, name="v1_got", align_bytes=64)
+        v_in = keep.tile([P, B * DV, PACK], BF16, name="v_in", align_bytes=64)
+        v_codes = keep.tile([P, B * DV], U32, name="v_codes", align_bytes=64)
+        v_scales = keep.tile([P, B * DV], U8, name="v_scales", align_bytes=64)
+        w_codes = keep.tile([P, B * NQ], U32, name="w_codes", align_bytes=64)
+        w_scales = keep.tile([P, B * NQ], U8, name="w_scales", align_bytes=64)
+        minus_one = keep.tile([P, B], F32, name="minus_one")
+        positive = []
+        squares = [keep.tile([P, N + 8], F32, name="squares%d" % b) for b in range(B)]
+        total = keep.tile([P, B], F32, name="total")
+        recip = keep.tile([P, B], F32, name="recip")
         y_sb = [keep.tile([P, DV], F32, name="y_sb%d" % b) for b in range(B)]
         bank = {}
         kv = kT.rearrange("(p j) n -> p j n", j=PACK)
@@ -74,317 +73,261 @@ def tile_attend_relu2_seg_kernel(tc, qT, kT, vT, vs, offs, out):
         def listed(b):
             return offsets[:, b * (N // 16) : (b + 1) * (N // 16)]
 
-        def load_scales():
-            nc.sync.dma_start(vs_tab[0:1, :], vs[0:1, :])
+        def words(pairs):
+            return pairs[:].rearrange("p n e -> p (n e)").bitcast(U32)
+
+        def copy_on(engine, target, source):
+            if engine == "S":
+                nc.scalar.activation(target, source, COPY)
+            else:
+                nc.vector.tensor_copy(target, source)
 
         def load_queries():
             nc.sync.dma_start(q_raw[:], qT.rearrange("b (p j) q -> p b (j q)", j=PACK))
 
-        def load_values(b, h):
-            nc.sync.dma_start(v_raw[:, h, b * SEG : (b + 1) * SEG], vT[h * P : (h + 1) * P, b * SEG : (b + 1) * SEG])
-
         def load_keys(b, u, a0, a1):
             nc.sync.dma_start(k_raw[b][u][:, :, a0:a1], kv[:, 2 * u : 2 * u + 2, b * SEG + a0 : b * SEG + a1])
 
-        def load_offsets():
-            nc.sync.dma_start(offsets[:], offs)
+        def load_values0(h):
+            nc.sync.dma_start(v0_raw[h][:], vT[h * P : (h + 1) * P, 0:SEG])
 
-        def cast_queries(b):
-            nc.scalar.activation(q_in[:, b, :, :], q_raw[:, b, :].rearrange("p (j q) -> p q j", j=PACK), COPY)
+        def load_values1(a0, a1):
+            nc.sync.dma_start(v1_raw[:, :, a0:a1], vT.rearrange("(h p) n -> p h n", h=2)[:, :, SEG + a0 : SEG + a1])
 
-        def cast_queries_gpsimd():
-            for b in range(B):
-                nc.gpsimd.tensor_scalar(
-                    q_in[:, b, :, :], q_raw[:, b, :].rearrange("p (j q) -> p q j", j=PACK), 1.0, 0.0, op0=MULT, op1=ADD
-                )
+        def cast_queries(engine):
+            source = q_raw[:].rearrange("p b (j q) -> p b q j", j=PACK)
+            if engine == "G":
+                nc.gpsimd.tensor_scalar(q_in[:], source, 1.0, 0.0, op0=MULT, op1=ADD)
+            else:
+                copy_on(engine, q_in[:], source)
+
+        def quantize(codes, scales, source):
+            nc.vector.quantize_mx(out=codes.bitcast(FP8X4), scales=scales, in_=source)
 
         def quantize_queries():
-            nc.vector.quantize_mx(
-                out=q_codes[:].bitcast(FP8X4), scales=q_scales[:], in_=q_in[:].rearrange("p b q j -> p (b q j)")
-            )
+            quantize(q_codes[:], q_scales[:], q_in[:].rearrange("p b q j -> p (b q j)"))
 
         def gather_scales():
             nc.vector.tensor_copy(vs_got[:], vs_tab[:].indirect(offsets[:]))
 
-        def turn(key, source):
+        def turn(key, count, source):
             turned = turn_pool.tile([P, PACK, P], F32, name="turned")
-            for t in range(PACK):
+            for t in range(count):
                 nc.tensor.transpose(turned[:, t, :], source(t), ident[:])
             bank[key] = turned
 
         def turn_scales():
             turned = turn_pool.tile([P, PACK, P], F32, name="turned")
             flat = turned[:].rearrange("s t e -> s (t e)")
-            for k in range(B * PACK):
+            for k in reversed(range(B * PACK)):
                 b, t = divmod(k, PACK)
                 nc.tensor.transpose(flat[:, 2 * k : 2 * k + P], vs_got[:, b * N + t : (b + 1) * N : PACK], ident[:])
             bank["vs"] = flat
 
         def take_scales(engine):
-            source = bank["vs"][:, 0 : 2 * B * PACK : 2]
+            copy_on(engine, vs_cols[:], bank["vs"][:, P - 1 : P - 1 + 2 * B * PACK : 2])
+
+        def cast_keys(b, u, a0, a1, engine):
+            copy_on(engine, k_pairs[u][:, b * SEG + a0 : b * SEG + a1, :], k_raw[b][u][:, :, a0:a1].rearrange("p e n -> p n e"))
+
+        def gather_keys(b, u):
+            nc.vector.tensor_copy(k_got[b][:, u, :], words(k_pairs[u])[:, 0 : (b + 1) * SEG].indirect(listed(b)))
+
+        def lay_keys(b, engine):
+            source = k_got[b][:].rearrange("p u n -> p n u")
             if engine == "S":
-                nc.scalar.activation(vs_cols[:], source, COPY)
+                nc.scalar.copy(k_in[b][:], source)
             else:
-                nc.vector.tensor_copy(vs_cols[:], source)
+                nc.vector.tensor_copy(k_in[b][:], source)
 
-        def load_value_tokens(b, a0, a1):
-            n0, n1 = b * SEG + a0, b * SEG + a1
-            nc.sync.dma_start(v_raw[:, :, n0:n1], vT.rearrange("(h p) n -> p h n", h=2)[:, :, n0:n1])
+        def quantize_keys(b):
+            quantize(k_codes[b][:], k_scales[b][:], k_in[b][:].rearrange("p n u -> p (n u)").bitcast(BF16))
 
-        def cast_values(b, a0, a1, engine):
-            dst = v_pairs[:, b * SEG + a0 : b * SEG + a1, :]
-            source = v_raw[:, :, b * SEG + a0 : b * SEG + a1].rearrange("p h n -> p n h")
+        def score(b):
+            scores = score_pool.tile([P, N], F32, name="scores")
+            nc.tensor.matmul_mx(
+                out=scores[:],
+                lhsT=q_codes[:, b * NQ : (b + 1) * NQ].bitcast(FP8X4),
+                lhsT_scale=q_scales[:, b * NQ : (b + 1) * NQ],
+                rhs=k_codes[b][:].bitcast(FP8X4),
+                rhs_scale=k_scales[b][:],
+                start=True,
+                stop=True,
+            )
+            bank[("s", b)] = scores
+
+        def place_positive(tag):
+            held = keep.tile([P, 2, SEG], F32, name=tag)
+            for b in range(B):
+                positive.append(held[:, b, :])
+                nc.gpsimd.memset(held[:, b, N : N + 1], 1.0)
+
+        def relu(b, engine):
+            target = positive[b][:, 0:N].rearrange("q (t s) -> q t s", t=PACK)
+            source = bank[("s", b)][:].rearrange("q (s t) -> q t s", t=PACK)
             if engine == "S":
-                nc.scalar.activation(dst, source, COPY)
+                nc.scalar.activation(target, source, RELU)
             else:
-                nc.vector.tensor_copy(dst, source)
+                nc.vector.tensor_scalar(target, source, 0.0, None, op0=MAX)
 
-        def gather_value_words(b):
-            words = v_pairs[:].rearrange("p n e -> p (n e)").bitcast(U32)
-            window = words[:, 0:SEG] if b == 0 else words
-            nc.vector.tensor_copy(v_words[b][:].rearrange("p t s -> p s t"), window.indirect(listed(b)))
-
-        def turn_value_words(b):
-            turn(("v", b), lambda t: v_words[b][:, t, :].bitcast(F32))
-
-        def settle_value_words(b, h, engine):
-            pairs = bank[("v", b)][:].rearrange("s t p -> s (t p)").bitcast(BF16)
-            pairs = pairs.rearrange("s (t p h) -> s h p t", t=PACK, h=2)
-            if h is None:
-                target, source = v_in[b][:].rearrange("s (h p) t -> s h p t", h=2), pairs
+        def square(b, engine):
+            source = positive[b][:, 0 : N + 1]
+            if engine == "S":
+                nc.scalar.activation(squares[b][:, 0 : N + 1], source, SQUARE, accum_out=total[:, b : b + 1])
             else:
-                target, source = v_in[b][:, h * HALF : (h + 1) * HALF, :], pairs[:, h, :, :]
+                nc.vector.scalar_tensor_tensor(
+                    out=squares[b][:, 0 : N + 1], in0=source, scalar=0.0, in1=source, op0=MAX, op1=MULT,
+                    accum_out=total[:, b : b + 1],
+                )
+
+        def turn_squares(b):
+            turn(("p", b), PACK, lambda t: squares[b][:, t * P : (t + 1) * P])
+
+        def weigh(b):
+            spread = vs_cols[:, b * PACK : (b + 1) * PACK].unsqueeze(1).to_broadcast([P, NQ, PACK])
+            nc.vector.tensor_tensor(bank["w"][:, b * NQ : (b + 1) * NQ, :], bank[("p", b)][:].rearrange("s t q -> s q t"), spread, MULT)
+
+        def place_weights(tag):
+            bank["w"] = keep.tile([P, B * NQ, PACK], BF16, name=tag, align_bytes=64)
+
+        def quantize_weights(c0, c1):
+            quantize(w_codes[:, c0:c1], w_scales[:, c0:c1], bank["w"][:, c0:c1, :].rearrange("s c t -> s (c t)"))
+
+        def quantize_values(c0, c1):
+            quantize(v_codes[:, c0:c1], v_scales[:, c0:c1], v_in[:, c0:c1, :].rearrange("s c t -> s (c t)"))
+
+        def invert_totals(engine):
+            if engine == "G":
+                nc.gpsimd.tensor_tensor(recip[:], total[:], minus_one[:], POW)
+            else:
+                nc.vector.reciprocal(recip[:], total[:])
+
+        def cast_values1(a0, a1, engine):
+            copy_on(engine, v1_pairs[:, SEG + a0 : SEG + a1, :], v1_raw[:, :, a0:a1].rearrange("p h n -> p n h"))
+
+        def gather_values1():
+            nc.vector.tensor_copy(v1_got[:].rearrange("p t s -> p s t"), words(v1_pairs).indirect(listed(1)))
+
+        def turn_values1():
+            turn(("v", 1), PACK, lambda t: v1_got[:, t, :].bitcast(F32))
+
+        def settle_values1(h0, h1, engine):
+            pairs = bank[("v", 1)][:].rearrange("s t p -> s (t p)").bitcast(BF16)
+            source = pairs.rearrange("s (t p h) -> s h p t", t=PACK, h=2)[:, h0:h1, :, :]
+            target = v_in[:, DV : 2 * DV, :].rearrange("s (h p) t -> s h p t", h=2)[:, h0:h1, :, :]
             if engine == "S":
                 nc.scalar.copy(target, source)
             else:
                 nc.vector.tensor_copy(target, source)
 
-        def gather_values(b, h):
-            window = v_raw[:, h, 0:SEG] if b == 0 else v_raw[:, h, :]
-            nc.vector.tensor_copy(v_got[b][h][:], window.indirect(listed(b)))
+        def gather_values0(h):
+            nc.vector.tensor_copy(v0_got[h][:], v0_raw[h][:].indirect(listed(0)))
 
-        def turn_values(b, h):
-            turn(("v", b, h), lambda t: v_got[b][h][:, t:N:PACK])
+        def turn_values0(h):
+            turn(("v", 0, h), 2, lambda u: v0_got[h][:].bitcast(F32)[:, u : N // 2 : 2])
 
-        def settle_values(b, h, e0, e1, engine):
-            target = v_in[b][:, h * HALF + e0 : h * HALF + e1, :]
-            source = bank[("v", b, h)][:, :, e0:e1].rearrange("s t e -> s e t")
+        def settle_values0(h, engine):
+            target = v_in[:, h * HALF : (h + 1) * HALF, :].rearrange("s e t -> s (e t)").bitcast(F32)
+            target = target.rearrange("s (e u) -> s e u", u=2)
+            source = bank[("v", 0, h)][:, 0:2, :].rearrange("s u e -> s e u")
             if engine == "S":
-                nc.scalar.activation(target, source, COPY)
+                nc.scalar.copy(target, source)
             else:
                 nc.vector.tensor_copy(target, source)
-
-        def quantize_values(b, e0, e1):
-            nc.vector.quantize_mx(
-                out=v_codes[b][:, e0:e1].bitcast(FP8X4),
-                scales=v_scales[b][:, e0:e1],
-                in_=v_in[b][:, e0:e1, :].rearrange("s e t -> s (e t)"),
-            )
-
-        def cast_keys(b, u, a0, a1, engine):
-            dst = k_pairs[u][:, b * SEG + a0 : b * SEG + a1, :]
-            source = k_raw[b][u][:, :, a0:a1].rearrange("p e n -> p n e")
-            if engine == "S":
-                nc.scalar.activation(dst, source, COPY)
-            else:
-                nc.vector.tensor_copy(dst, source)
-
-        def gather_keys(b, u):
-            words = k_pairs[u][:].rearrange("p n e -> p (n e)").bitcast(U32)
-            window = words[:, 0:SEG] if b == 0 else words
-            nc.vector.tensor_copy(k_in[b][:, :, :, u].rearrange("p t s -> p s t"), window.indirect(listed(b)))
-
-        def gather_keys_apart(b, u):
-            words = k_pairs[u][:].rearrange("p n e -> p (n e)").bitcast(U32)
-            window = words[:, 0:SEG] if b == 0 else words
-            nc.vector.tensor_copy(k_got[b][:, u, :, :].rearrange("p t s -> p s t"), window.indirect(listed(b)))
-
-        def lay_keys(b, engine):
-            target = k_in[b][:].rearrange("p t s u -> p (t s) u")
-            source = k_got[b][:].rearrange("p u t s -> p (t s) u")
-            if engine == "V":
-                nc.vector.tensor_copy(target, source)
-            else:
-                nc.gpsimd.tensor_copy(target, source)
-
-        def quantize_keys(b):
-            nc.vector.quantize_mx(
-                out=k_codes[b][:].bitcast(FP8X4),
-                scales=k_scales[b][:],
-                in_=k_in[b][:].rearrange("p t s u -> p (t s u)").bitcast(BF16),
-            )
-
-        def score(b):
-            scores = score_pool.tile([P, PACK, NQ], F32, name="scores")
-            for t in range(PACK):
-                nc.tensor.matmul_mx(
-                    out=scores[:, t, :],
-                    lhsT=k_codes[b][:, t * P : (t + 1) * P].bitcast(FP8X4),
-                    lhsT_scale=k_scales[b][:, t * P : (t + 1) * P],
-                    rhs=q_codes[:, b * NQ : (b + 1) * NQ].bitcast(FP8X4),
-                    rhs_scale=q_scales[:, b * NQ : (b + 1) * NQ],
-                    start=True,
-                    stop=True,
-                )
-            bank[("s", b)] = scores
-
-        def relu(b):
-            nc.scalar.activation(positive[b][:], bank[("s", b)][:], RELU)
-
-        def scale_scores(b, t):
-            nc.scalar.activation(scaled[b][:, t, :], bank[("s", b)][:, t, :], COPY, scale=vs_cols[:, b * PACK + t : b * PACK + t + 1])
-
-        def square(b, engine):
-            if engine == "S":
-                nc.scalar.activation(scaled[b][:], positive[b][:], SQUARE)
-            elif engine == "G":
-                nc.gpsimd.tensor_tensor(scaled[b][:], positive[b][:], positive[b][:], MULT)
-            else:
-                nc.vector.scalar_tensor_tensor(
-                    out=scaled[b][:], in0=bank[("s", b)][:], scalar=0.0, in1=positive[b][:], op0=MAX, op1=MULT
-                )
-
-        def spread(b):
-            return vs_cols[:, b * PACK : (b + 1) * PACK].unsqueeze(1).to_broadcast([P, NQ, PACK])
-
-        def by_query(tile):
-            return tile[:].rearrange("s t q -> s q t")
-
-        def scale_positive(b):
-            nc.vector.scalar_tensor_tensor(
-                out=shaped[b][:], in0=by_query(bank[("s", b)]), scalar=0.0, in1=spread(b), op0=MAX, op1=MULT
-            )
-
-        def weigh(b, form):
-            if form == "v":
-                nc.vector.scalar_tensor_tensor(
-                    out=w_in[b][:], in0=by_query(bank[("s", b)]), scalar=0.0, in1=shaped[b][:], op0=MAX, op1=MULT
-                )
-            elif form == "z":
-                nc.vector.scalar_tensor_tensor(
-                    out=w_in[b][:], in0=by_query(bank[("s", b)]), scalar=0.0, in1=by_query(scaled[b]), op0=MAX, op1=MULT
-                )
-            elif form in ("g", "G"):
-                nc.gpsimd.tensor_tensor(w_in[b][:], by_query(scaled[b]), spread(b), MULT)
-            else:
-                nc.vector.tensor_tensor(w_in[b][:], by_query(scaled[b]), spread(b), MULT)
-
-        def quantize_weights(b):
-            nc.vector.quantize_mx(
-                out=w_codes[b][:].bitcast(FP8X4), scales=w_scales[b][:], in_=w_in[b][:].rearrange("s q t -> s (q t)")
-            )
-
-        def turn_positive(b):
-            turn(("p", b), lambda t: positive[b][:, t, :])
-
-        def sum_weights(b):
-            nc.scalar.activation(squares[b][:], bank[("p", b)][:], SQUARE, accum_out=total[b][:])
-
-        def add_one(b):
-            nc.gpsimd.tensor_scalar(total1[b][:], total[b][:], 1.0, None, op0=ADD)
-
-        def invert_total(b):
-            nc.vector.reciprocal(recip[b][:], total1[b][:])
 
         def multiply_values(b, e0, e1):
             y = y_pool.tile([P, DV], F32, name="y")
             nc.tensor.matmul_mx(
                 out=y[:, 0 : e1 - e0],
-                lhsT=w_codes[b][:].bitcast(FP8X4),
-                lhsT_scale=w_scales[b][:],
-                rhs=v_codes[b][:, e0:e1].bitcast(FP8X4),
-                rhs_scale=v_scales[b][:, e0:e1],
+                lhsT=w_codes[:, b * NQ : (b + 1) * NQ].bitcast(FP8X4),
+                lhsT_scale=w_scales[:, b * NQ : (b + 1) * NQ],
+                rhs=v_codes[:, b * DV + e0 : b * DV + e1].bitcast(FP8X4),
+                rhs_scale=v_scales[:, b * DV + e0 : b * DV + e1],
                 start=True,
                 stop=True,
             )
             bank[("y", b, e0)] = y
 
-        def settle_output(b, e0, e1):
-            nc.scalar.activation(y_sb[b][:, e0:e1], bank[("y", b, e0)][:, 0 : e1 - e0], COPY, scale=recip[b][:])
+        def settle_output(b, e0, e1, engine):
+            source = bank[("y", b, e0)][:, 0 : e1 - e0]
+            if engine == "S":
+                nc.scalar.activation(y_sb[b][:, e0:e1], source, COPY, scale=recip[:, b : b + 1])
+            else:
+                nc.vector.tensor_scalar(y_sb[b][:, e0:e1], source, recip[:, b : b + 1], None, op0=MULT)
 
-        def store_output(b, e0, e1):
-            nc.scalar.dma_start(out[b][:, e0:e1], y_sb[b][:, e0:e1])
+        def store_output(b, e0, e1, queue):
+            queue.dma_start(out[b][:, e0:e1], y_sb[b][:, e0:e1])
 
-        nc.vector.memset(warm[:], 0.0)
+        nc.gpsimd.memset(warm[:], 0.0)
+        nc.gpsimd.memset(vs_tab[0 : P - 1, 0:768], 0.0)
+        nc.vector.memset(vs_tab[0 : P - 1, 768:T], 0.0)
+        nc.vector.memset(words(v1_pairs)[:, 0:SEG], 0)
         nc.scalar.activation(warm[:, 4:8], warm[:, 0:4], SQUARE)
-        nc.gpsimd.memset(vs_tab[:, 0:1280], 0.0)
-        nc.vector.memset(vs_tab[:, 1280:T], 0.0)
-        load_offsets()
-        load_keys(0, 0, 0, 512)
+        nc.sync.dma_start(offsets[:], offs)
+        nc.sync.dma_start(vs_tab[P - 1 : P, :], vs[0:1, :])
         make_identity(nc, ident[:])
-        load_scales()
-        load_keys(0, 0, 512, 1024)
-        load_keys(0, 1, 384, 1024)
-        cast_keys(0, 0, 0, 512, "S")
-        gather_scales()
-        load_keys(0, 1, 0, 384)
-        load_keys(1, 1, 0, 256)
-        cast_keys(0, 0, 512, 1024, "S")
-        load_keys(1, 0, 384, 1024)
-        cast_keys(0, 1, 384, 784, "S")
-        cast_keys(0, 1, 784, 1024, "V")
-        turn_scales()
-        load_keys(1, 0, 0, 384)
-        gather_keys_apart(0, 0)
-        cast_keys(0, 1, 0, 384, "S")
-        load_keys(1, 1, 256, 512)
-        take_scales("V")
-        load_keys(1, 1, 512, 1024)
-        cast_keys(1, 1, 0, 256, "S")
-        gather_keys_apart(0, 1)
+
+        for b in range(B):
+            for u in range(2):
+                for a in (0, 512):
+                    load_keys(b, u, a, a + 512)
         load_queries()
-        cast_keys(1, 0, 384, 1024, "S")
-        cast_keys(1, 0, 144, 384, "V")
+        load_values1(0, 512)
+        load_values1(512, 1024)
+        load_values0(0)
+        load_values0(1)
+        gather_scales()
+        turn_scales()
+        cast_keys(0, 0, 0, 512, "S")
+        cast_keys(0, 0, 512, 1024, "S")
+        gather_keys(0, 0)
+        take_scales("V")
+        cast_keys(0, 1, 0, 512, "S")
+        cast_keys(0, 1, 512, 1024, "V")
+        gather_keys(0, 1)
+        cast_keys(1, 0, 0, 512, "S")
+        cast_keys(1, 0, 512, 1024, "S")
         lay_keys(0, "V")
+        gather_keys(1, 0)
         quantize_keys(0)
-        load_value_tokens(0, 0, 640)
-        cast_keys(1, 0, 0, 144, "S")
-        load_value_tokens(0, 640, 1024)
-        cast_keys(1, 1, 256, 512, "V")
-        gather_keys_apart(1, 0)
-        cast_queries_gpsimd()
-        load_values(1, 1)
-        cast_keys(1, 1, 512, 1024, "S")
-        load_values(1, 0)
-        cast_values(0, 0, 640, "S")
-        gather_keys_apart(1, 1)
-        quantize_queries()
+        cast_keys(1, 1, 0, 512, "S")
+        cast_keys(1, 1, 512, 768, "S")
+        cast_keys(1, 1, 768, 1024, "V")
+        gather_keys(1, 1)
+        cast_queries("V")
         lay_keys(1, "V")
-        quantize_keys(1)
+        quantize_queries()
         score(0)
-        cast_values(0, 640, 1024, "S")
-        gather_values(1, 1)
+        quantize_keys(1)
         score(1)
-        relu(0)
-        gather_value_words(0)
-        relu(1)
-        square(0, "G")
-        turn_positive(0)
-        turn_values(1, 1)
-        sum_weights(0)
-        turn_positive(1)
-        gather_values(1, 0)
-        turn_value_words(0)
+        cast_values1(0, 512, "S")
+        cast_values1(512, 1024, "S")
+        place_positive("v1_raw")
+        relu(0, "S")
+        square(0, "S")
+        turn_squares(0)
+        relu(1, "S")
         square(1, "S")
-        add_one(0)
-        weigh(0, "G")
-        settle_values(1, 1, 0, 64, "S")
-        weigh(1, "p")
-        turn_values(1, 0)
-        settle_value_words(0, None, "S")
-        invert_total(0)
-        settle_values(1, 1, 64, 128, "V")
-        quantize_weights(1)
-        quantize_weights(0)
-        settle_values(1, 0, 0, 128, "S")
-        quantize_values(0, 0, DV)
-        sum_weights(1)
-        quantize_values(1, 0, 256)
-        multiply_values(0, 0, 256)
-        multiply_values(1, 0, 256)
-        settle_output(0, 0, 256)
-        add_one(1)
-        invert_total(1)
-        store_output(0, 0, 256)
-        settle_output(1, 0, 256)
-        store_output(1, 0, 256)
+        turn_squares(1)
+        invert_totals("V")
+        gather_values1()
+        turn_values1()
+        gather_values0(0)
+        turn_values0(0)
+        gather_values0(1)
+        turn_values0(1)
+        settle_values1(0, 2, "S")
+        settle_values0(0, "S")
+        settle_values0(1, "S")
+        place_weights("v0_raw1")
+        weigh(0)
+        weigh(1)
+        quantize_values(DV, 2 * DV)
+        quantize_weights(0, B * NQ)
+        quantize_values(0, DV)
+        multiply_values(1, 0, DV)
+        multiply_values(0, 0, DV)
+        settle_output(1, 0, DV, "S")
+        store_output(1, 0, DV, nc.sync)
+        settle_output(0, 0, DV, "S")
+        store_output(0, 0, DV, nc.scalar)

@@ -31,9 +31,7 @@ def tile_attend_relu2_seg_kernel(tc, qT, kT, vT, vs, offs, out):
     nc = tc.nc
     with ExitStack() as ctx:
         keep = ctx.enter_context(tc.tile_pool(name="keep", bufs=1))
-        turn_pool = ctx.enter_context(tc.psum_pool(name="turns", bufs=4))
-        score_pool = ctx.enter_context(tc.psum_pool(name="scores", bufs=2))
-        y_pool = ctx.enter_context(tc.psum_pool(name="ys", bufs=2))
+        psum = ctx.enter_context(tc.psum_pool(name="psum", bufs=1))
 
         offsets = keep.tile([P, B * N // 16], U16, name="offsets")
         vs_tab = keep.tile([P, T], F32, name="vs_tab")
@@ -44,27 +42,27 @@ def tile_attend_relu2_seg_kernel(tc, qT, kT, vT, vs, offs, out):
         q_codes = keep.tile([P, B * NQ], U32, name="q_codes", align_bytes=64)
         q_scales = keep.tile([P, B * NQ], U8, name="q_scales", align_bytes=64)
         vs_got = keep.tile([P, B * N], F32, name="vs_got")
-        vs_cols = keep.tile([P, B * PACK], F32, name="vs_cols")
         k_raw = [[keep.tile([P, 2, SEG], F32, name="k_raw%d%d" % (b, u)) for u in range(2)] for b in range(B)]
         k_pairs = [keep.tile([P, T, 2], BF16, name="k_pairs%d" % u, align_bytes=64) for u in range(2)]
         k_got = [keep.tile([P, 2, N], U32, name="k_got%d" % b, align_bytes=64) for b in range(B)]
         k_in = [keep.tile([P, N, 2], U32, name="k_in%d" % b, align_bytes=64) for b in range(B)]
         k_codes = [keep.tile([P, N], U32, name="k_codes%d" % b, align_bytes=64) for b in range(B)]
         k_scales = [keep.tile([P, N], U8, name="k_scales%d" % b, align_bytes=64) for b in range(B)]
-        v0_raw = [keep.tile([P, SEG], F32, name="v0_raw%d" % h, align_bytes=64) for h in range(2)]
+        v0_raw = [keep.tile([P, SEG], F32, name="v0_raw%d" % h) for h in range(2)]
         v0_got = [keep.tile([P, N], BF16, name="v0_got%d" % h, align_bytes=64) for h in range(2)]
-        v1_raw = keep.tile([P, 2, SEG], F32, name="v1_raw")
+        v1_raw = keep.tile([P, 2, SEG], F32, name="v1_raw", align_bytes=64)
         v1_pairs = keep.tile([P, T, 2], BF16, name="v1_pairs", align_bytes=64)
         v1_got = keep.tile([P, PACK, P], U32, name="v1_got", align_bytes=64)
-        v_in = keep.tile([P, B * DV, PACK], BF16, name="v_in", align_bytes=64)
-        v_codes = keep.tile([P, B * DV], U32, name="v_codes", align_bytes=64)
-        v_scales = keep.tile([P, B * DV], U8, name="v_scales", align_bytes=64)
-        w_codes = keep.tile([P, B * NQ], U32, name="w_codes", align_bytes=64)
-        w_scales = keep.tile([P, B * NQ], U8, name="w_scales", align_bytes=64)
+        late_in = keep.tile([P, B * NQ + DV, PACK], BF16, name="late_in", align_bytes=64)
+        late_codes = keep.tile([P, B * (NQ + DV)], U32, name="late_codes", align_bytes=64)
+        late_scales = keep.tile([P, B * (NQ + DV)], U8, name="late_scales", align_bytes=64)
+        w_at = [0, NQ]
+        v_at = [B * NQ + DV, B * NQ]
         minus_one = keep.tile([P, B], F32, name="minus_one")
         positive = []
-        squares = [keep.tile([P, N + 8], F32, name="squares%d" % b) for b in range(B)]
+        squares = [keep.tile([P, N], F32, name="squares%d" % b) for b in range(B)]
         total = keep.tile([P, B], F32, name="total")
+        total_and_one = keep.tile([P, B], F32, name="total_and_one")
         recip = keep.tile([P, B], F32, name="recip")
         y_sb = [keep.tile([P, DV], F32, name="y_sb%d" % b) for b in range(B)]
         bank = {}
@@ -110,14 +108,14 @@ def tile_attend_relu2_seg_kernel(tc, qT, kT, vT, vs, offs, out):
         def gather_scales():
             nc.vector.tensor_copy(vs_got[:], vs_tab[:].indirect(offsets[:]))
 
-        def turn(key, count, source):
-            turned = turn_pool.tile([P, PACK, P], F32, name="turned")
+        def turn(key, tag, count, source):
+            turned = psum.tile([P, PACK, P], F32, name=tag)
             for t in range(count):
                 nc.tensor.transpose(turned[:, t, :], source(t), ident[:])
             bank[key] = turned
 
         def turn_scales():
-            turned = turn_pool.tile([P, PACK, P], F32, name="turned")
+            turned = psum.tile([P, PACK, P], F32, name="turn_v00")
             flat = turned[:].rearrange("s t e -> s (t e)")
             for k in reversed(range(B * PACK)):
                 b, t = divmod(k, PACK)
@@ -125,7 +123,8 @@ def tile_attend_relu2_seg_kernel(tc, qT, kT, vT, vs, offs, out):
             bank["vs"] = flat
 
         def take_scales(engine):
-            copy_on(engine, vs_cols[:], bank["vs"][:, P - 1 : P - 1 + 2 * B * PACK : 2])
+            bank["cols"] = keep.tile([P, B * PACK], F32, name="k_raw00")
+            copy_on(engine, bank["cols"][:], bank["vs"][:, P - 1 : P - 1 + 2 * B * PACK : 2])
 
         def cast_keys(b, u, a0, a1, engine):
             copy_on(engine, k_pairs[u][:, b * SEG + a0 : b * SEG + a1, :], k_raw[b][u][:, :, a0:a1].rearrange("p e n -> p n e"))
@@ -144,7 +143,7 @@ def tile_attend_relu2_seg_kernel(tc, qT, kT, vT, vs, offs, out):
             quantize(k_codes[b][:], k_scales[b][:], k_in[b][:].rearrange("p n u -> p (n u)").bitcast(BF16))
 
         def score(b):
-            scores = score_pool.tile([P, N], F32, name="scores")
+            scores = psum.tile([P, N], F32, name="product%d" % b)
             nc.tensor.matmul_mx(
                 out=scores[:],
                 lhsT=q_codes[:, b * NQ : (b + 1) * NQ].bitcast(FP8X4),
@@ -157,10 +156,9 @@ def tile_attend_relu2_seg_kernel(tc, qT, kT, vT, vs, offs, out):
             bank[("s", b)] = scores
 
         def place_positive(tag):
-            held = keep.tile([P, 2, SEG], F32, name=tag)
+            held = keep.tile([P, B, N], F32, name=tag, align_bytes=64)
             for b in range(B):
                 positive.append(held[:, b, :])
-                nc.gpsimd.memset(held[:, b, N : N + 1], 1.0)
 
         def relu(b, engine):
             target = positive[b][:, 0:N].rearrange("q (t s) -> q t s", t=PACK)
@@ -171,36 +169,32 @@ def tile_attend_relu2_seg_kernel(tc, qT, kT, vT, vs, offs, out):
                 nc.vector.tensor_scalar(target, source, 0.0, None, op0=MAX)
 
         def square(b, engine):
-            source = positive[b][:, 0 : N + 1]
+            source = positive[b]
             if engine == "S":
-                nc.scalar.activation(squares[b][:, 0 : N + 1], source, SQUARE, accum_out=total[:, b : b + 1])
+                nc.scalar.activation(squares[b][:], source, SQUARE, accum_out=total[:, b : b + 1])
             else:
                 nc.vector.scalar_tensor_tensor(
-                    out=squares[b][:, 0 : N + 1], in0=source, scalar=0.0, in1=source, op0=MAX, op1=MULT,
+                    out=squares[b][:], in0=source, scalar=0.0, in1=source, op0=MAX, op1=MULT,
                     accum_out=total[:, b : b + 1],
                 )
 
         def turn_squares(b):
-            turn(("p", b), PACK, lambda t: squares[b][:, t * P : (t + 1) * P])
+            turn(("p", b), "turn_p%d" % b, PACK, lambda t: squares[b][:, t * P : (t + 1) * P])
 
         def weigh(b):
-            spread = vs_cols[:, b * PACK : (b + 1) * PACK].unsqueeze(1).to_broadcast([P, NQ, PACK])
-            nc.vector.tensor_tensor(bank["w"][:, b * NQ : (b + 1) * NQ, :], bank[("p", b)][:].rearrange("s t q -> s q t"), spread, MULT)
+            spread = bank["cols"][:, b * PACK : (b + 1) * PACK].unsqueeze(1).to_broadcast([P, NQ, PACK])
+            nc.vector.tensor_tensor(late_in[:, w_at[b] : w_at[b] + NQ, :], bank[("p", b)][:].rearrange("s t q -> s q t"), spread, MULT)
 
-        def place_weights(tag):
-            bank["w"] = keep.tile([P, B * NQ, PACK], BF16, name=tag, align_bytes=64)
-
-        def quantize_weights(c0, c1):
-            quantize(w_codes[:, c0:c1], w_scales[:, c0:c1], bank["w"][:, c0:c1, :].rearrange("s c t -> s (c t)"))
-
-        def quantize_values(c0, c1):
-            quantize(v_codes[:, c0:c1], v_scales[:, c0:c1], v_in[:, c0:c1, :].rearrange("s c t -> s (c t)"))
+        def quantize_late(c0, c1):
+            quantize(late_codes[:, c0:c1], late_scales[:, c0:c1], late_in[:, c0:c1, :].rearrange("s c t -> s (c t)"))
 
         def invert_totals(engine):
             if engine == "G":
-                nc.gpsimd.tensor_tensor(recip[:], total[:], minus_one[:], POW)
+                nc.gpsimd.tensor_scalar(total_and_one[:], total[:], 1.0, 1.0, op0=MULT, op1=ADD)
+                nc.gpsimd.tensor_tensor(recip[:], total_and_one[:], minus_one[:], POW)
             else:
-                nc.vector.reciprocal(recip[:], total[:])
+                nc.vector.tensor_scalar(total_and_one[:], total[:], 1.0, None, op0=ADD)
+                nc.vector.reciprocal(recip[:], total_and_one[:])
 
         def cast_values1(a0, a1, engine):
             copy_on(engine, v1_pairs[:, SEG + a0 : SEG + a1, :], v1_raw[:, :, a0:a1].rearrange("p h n -> p n h"))
@@ -209,12 +203,12 @@ def tile_attend_relu2_seg_kernel(tc, qT, kT, vT, vs, offs, out):
             nc.vector.tensor_copy(v1_got[:].rearrange("p t s -> p s t"), words(v1_pairs).indirect(listed(1)))
 
         def turn_values1():
-            turn(("v", 1), PACK, lambda t: v1_got[:, t, :].bitcast(F32))
+            turn(("v", 1), "turn_v1", PACK, lambda t: v1_got[:, t, :].bitcast(F32))
 
         def settle_values1(h0, h1, engine):
             pairs = bank[("v", 1)][:].rearrange("s t p -> s (t p)").bitcast(BF16)
             source = pairs.rearrange("s (t p h) -> s h p t", t=PACK, h=2)[:, h0:h1, :, :]
-            target = v_in[:, DV : 2 * DV, :].rearrange("s (h p) t -> s h p t", h=2)[:, h0:h1, :, :]
+            target = late_in[:, v_at[1] : v_at[1] + DV, :].rearrange("s (h p) t -> s h p t", h=2)[:, h0:h1, :, :]
             if engine == "S":
                 nc.scalar.copy(target, source)
             else:
@@ -224,10 +218,17 @@ def tile_attend_relu2_seg_kernel(tc, qT, kT, vT, vs, offs, out):
             nc.vector.tensor_copy(v0_got[h][:], v0_raw[h][:].indirect(listed(0)))
 
         def turn_values0(h):
-            turn(("v", 0, h), 2, lambda u: v0_got[h][:].bitcast(F32)[:, u : N // 2 : 2])
+            turn(("v", 0, h), "turn_v00", 2, lambda u: v0_got[h][:].bitcast(F32)[:, u : N // 2 : 2])
+
+        def place_values0(tag):
+            bank["v0_in"] = keep.tile([P, DV, PACK], BF16, name=tag, align_bytes=64)
+
+        def quantize_values0(e0, e1):
+            c0, c1 = v_at[0] + e0, v_at[0] + e1
+            quantize(late_codes[:, c0:c1], late_scales[:, c0:c1], bank["v0_in"][:, e0:e1, :].rearrange("s c t -> s (c t)"))
 
         def settle_values0(h, engine):
-            target = v_in[:, h * HALF : (h + 1) * HALF, :].rearrange("s e t -> s (e t)").bitcast(F32)
+            target = bank["v0_in"][:, h * HALF : (h + 1) * HALF, :].rearrange("s e t -> s (e t)").bitcast(F32)
             target = target.rearrange("s (e u) -> s e u", u=2)
             source = bank[("v", 0, h)][:, 0:2, :].rearrange("s u e -> s e u")
             if engine == "S":
@@ -235,14 +236,14 @@ def tile_attend_relu2_seg_kernel(tc, qT, kT, vT, vs, offs, out):
             else:
                 nc.vector.tensor_copy(target, source)
 
-        def multiply_values(b, e0, e1):
-            y = y_pool.tile([P, DV], F32, name="y")
+        def multiply_values(b, e0, e1, tag):
+            y = psum.tile([P, DV], F32, name=tag)
             nc.tensor.matmul_mx(
                 out=y[:, 0 : e1 - e0],
-                lhsT=w_codes[:, b * NQ : (b + 1) * NQ].bitcast(FP8X4),
-                lhsT_scale=w_scales[:, b * NQ : (b + 1) * NQ],
-                rhs=v_codes[:, b * DV + e0 : b * DV + e1].bitcast(FP8X4),
-                rhs_scale=v_scales[:, b * DV + e0 : b * DV + e1],
+                lhsT=late_codes[:, w_at[b] : w_at[b] + NQ].bitcast(FP8X4),
+                lhsT_scale=late_scales[:, w_at[b] : w_at[b] + NQ],
+                rhs=late_codes[:, v_at[b] + e0 : v_at[b] + e1].bitcast(FP8X4),
+                rhs_scale=late_scales[:, v_at[b] + e0 : v_at[b] + e1],
                 start=True,
                 stop=True,
             )
@@ -259,8 +260,7 @@ def tile_attend_relu2_seg_kernel(tc, qT, kT, vT, vs, offs, out):
             queue.dma_start(out[b][:, e0:e1], y_sb[b][:, e0:e1])
 
         nc.gpsimd.memset(warm[:], 0.0)
-        nc.gpsimd.memset(vs_tab[0 : P - 1, 0:768], 0.0)
-        nc.vector.memset(vs_tab[0 : P - 1, 768:T], 0.0)
+        nc.vector.memset(vs_tab[0 : P - 1, :], 0.0)
         nc.vector.memset(words(v1_pairs)[:, 0:SEG], 0)
         nc.scalar.activation(warm[:, 4:8], warm[:, 0:4], SQUARE)
         nc.sync.dma_start(offsets[:], offs)
@@ -279,26 +279,27 @@ def tile_attend_relu2_seg_kernel(tc, qT, kT, vT, vs, offs, out):
         gather_scales()
         turn_scales()
         cast_keys(0, 0, 0, 512, "S")
-        cast_keys(0, 0, 512, 1024, "S")
+        cast_keys(0, 0, 512, 1024, "V")
         gather_keys(0, 0)
         take_scales("V")
         cast_keys(0, 1, 0, 512, "S")
-        cast_keys(0, 1, 512, 1024, "V")
+        cast_keys(0, 1, 512, 768, "S")
+        cast_keys(0, 1, 768, 1024, "V")
         gather_keys(0, 1)
         cast_keys(1, 0, 0, 512, "S")
         cast_keys(1, 0, 512, 1024, "S")
         lay_keys(0, "V")
-        gather_keys(1, 0)
         quantize_keys(0)
+        gather_keys(1, 0)
         cast_keys(1, 1, 0, 512, "S")
         cast_keys(1, 1, 512, 768, "S")
         cast_keys(1, 1, 768, 1024, "V")
         gather_keys(1, 1)
-        cast_queries("V")
+        cast_queries("S")
         lay_keys(1, "V")
+        quantize_keys(1)
         quantize_queries()
         score(0)
-        quantize_keys(1)
         score(1)
         cast_values1(0, 512, "S")
         cast_values1(512, 1024, "S")
@@ -309,24 +310,23 @@ def tile_attend_relu2_seg_kernel(tc, qT, kT, vT, vs, offs, out):
         relu(1, "S")
         square(1, "S")
         turn_squares(1)
-        invert_totals("V")
         gather_values1()
         turn_values1()
         gather_values0(0)
         turn_values0(0)
         gather_values0(1)
+        place_values0("v1_raw")
+        settle_values0(0, "S")
         turn_values0(1)
         settle_values1(0, 2, "S")
-        settle_values0(0, "S")
         settle_values0(1, "S")
-        place_weights("v0_raw1")
         weigh(0)
         weigh(1)
-        quantize_values(DV, 2 * DV)
-        quantize_weights(0, B * NQ)
-        quantize_values(0, DV)
-        multiply_values(1, 0, DV)
-        multiply_values(0, 0, DV)
+        invert_totals("V")
+        quantize_late(0, 512)
+        quantize_values0(0, DV)
+        multiply_values(1, 0, DV, "product0")
+        multiply_values(0, 0, DV, "product1")
         settle_output(1, 0, DV, "S")
         store_output(1, 0, DV, nc.sync)
         settle_output(0, 0, DV, "S")

@@ -21,7 +21,6 @@ SQUARE = mybir.ActivationFunctionType.Square
 MAX = mybir.AluOpType.max
 MULT = mybir.AluOpType.mult
 ADD = mybir.AluOpType.add
-POW = mybir.AluOpType.pow
 
 FLOPS = 2 * B * NQ * N * (D + DV)
 BYTES = 4 * (B * D * NQ + D * T + DV * T + T + B * NQ * DV) + 2 * P * (B * N // 16)
@@ -36,7 +35,6 @@ def tile_attend_relu2_seg_kernel(tc, qT, kT, vT, vs, offs, out):
         offsets = keep.tile([P, B * N // 16], U16, name="offsets")
         vs_tab = keep.tile([P, T], F32, name="vs_tab")
         ident = keep.tile([P, P], F32, name="ident")
-        warm = keep.tile([P, 8], F32, name="warm")
         q_raw = keep.tile([P, B, PACK * NQ], F32, name="q_raw")
         q_in = keep.tile([P, B, NQ, PACK], BF16, name="q_in", align_bytes=64)
         q_codes = keep.tile([P, B * NQ], U32, name="q_codes", align_bytes=64)
@@ -58,13 +56,11 @@ def tile_attend_relu2_seg_kernel(tc, qT, kT, vT, vs, offs, out):
         late_scales = keep.tile([P, B * (NQ + DV)], U8, name="late_scales", align_bytes=64)
         w_at = [0, NQ]
         v_at = [B * NQ + DV, B * NQ]
-        minus_one = keep.tile([P, B], F32, name="minus_one")
         positive = []
-        squares = [keep.tile([P, N], F32, name="squares%d" % b) for b in range(B)]
+        squares = [keep.tile([P, N + 16], F32, name="squares%d" % b) for b in range(B)]
         total = keep.tile([P, B], F32, name="total")
-        total_and_one = keep.tile([P, B], F32, name="total_and_one")
         recip = keep.tile([P, B], F32, name="recip")
-        y_sb = [keep.tile([P, DV], F32, name="y_sb%d" % b) for b in range(B)]
+        y_sb = [keep.tile([P, DV], F32, name="y_sb%d" % b, align_bytes=64) for b in range(B)]
         bank = {}
         kv = kT.rearrange("(p j) n -> p j n", j=PACK)
 
@@ -83,8 +79,8 @@ def tile_attend_relu2_seg_kernel(tc, qT, kT, vT, vs, offs, out):
         def load_queries():
             nc.sync.dma_start(q_raw[:], qT.rearrange("b (p j) q -> p b (j q)", j=PACK))
 
-        def load_keys(b, u, a0, a1):
-            nc.sync.dma_start(k_raw[b][u][:, :, a0:a1], kv[:, 2 * u : 2 * u + 2, b * SEG + a0 : b * SEG + a1])
+        def load_keys(b, u, a0, a1, queue):
+            queue.dma_start(k_raw[b][u][:, :, a0:a1], kv[:, 2 * u : 2 * u + 2, b * SEG + a0 : b * SEG + a1])
 
         def load_values0(h):
             nc.sync.dma_start(v0_raw[h][:], vT[h * P : (h + 1) * P, 0:SEG])
@@ -156,7 +152,8 @@ def tile_attend_relu2_seg_kernel(tc, qT, kT, vT, vs, offs, out):
             bank[("s", b)] = scores
 
         def place_positive(tag):
-            held = keep.tile([P, B, N], F32, name=tag, align_bytes=64)
+            held = keep.tile([P, B, N + 16], F32, name=tag, align_bytes=64)
+            nc.gpsimd.memset(held[:, :, N : N + 1], 1.0)
             for b in range(B):
                 positive.append(held[:, b, :])
 
@@ -169,12 +166,12 @@ def tile_attend_relu2_seg_kernel(tc, qT, kT, vT, vs, offs, out):
                 nc.vector.tensor_scalar(target, source, 0.0, None, op0=MAX)
 
         def square(b, engine):
-            source = positive[b]
+            source = positive[b][:, 0 : N + 1]
             if engine == "S":
-                nc.scalar.activation(squares[b][:], source, SQUARE, accum_out=total[:, b : b + 1])
+                nc.scalar.activation(squares[b][:, 0 : N + 1], source, SQUARE, accum_out=total[:, b : b + 1])
             else:
                 nc.vector.scalar_tensor_tensor(
-                    out=squares[b][:], in0=source, scalar=0.0, in1=source, op0=MAX, op1=MULT,
+                    out=squares[b][:, 0 : N + 1], in0=source, scalar=0.0, in1=source, op0=MAX, op1=MULT,
                     accum_out=total[:, b : b + 1],
                 )
 
@@ -188,13 +185,8 @@ def tile_attend_relu2_seg_kernel(tc, qT, kT, vT, vs, offs, out):
         def quantize_late(c0, c1):
             quantize(late_codes[:, c0:c1], late_scales[:, c0:c1], late_in[:, c0:c1, :].rearrange("s c t -> s (c t)"))
 
-        def invert_totals(engine):
-            if engine == "G":
-                nc.gpsimd.tensor_scalar(total_and_one[:], total[:], 1.0, 1.0, op0=MULT, op1=ADD)
-                nc.gpsimd.tensor_tensor(recip[:], total_and_one[:], minus_one[:], POW)
-            else:
-                nc.vector.tensor_scalar(total_and_one[:], total[:], 1.0, None, op0=ADD)
-                nc.vector.reciprocal(recip[:], total_and_one[:])
+        def invert_totals():
+            nc.vector.reciprocal(recip[:], total[:])
 
         def cast_values1(a0, a1, engine):
             copy_on(engine, v1_pairs[:, SEG + a0 : SEG + a1, :], v1_raw[:, :, a0:a1].rearrange("p h n -> p n h"))
@@ -259,18 +251,17 @@ def tile_attend_relu2_seg_kernel(tc, qT, kT, vT, vs, offs, out):
         def store_output(b, e0, e1, queue):
             queue.dma_start(out[b][:, e0:e1], y_sb[b][:, e0:e1])
 
-        nc.gpsimd.memset(warm[:], 0.0)
+        load_keys(0, 0, 0, 512, nc.scalar)
         nc.vector.memset(vs_tab[0 : P - 1, :], 0.0)
         nc.vector.memset(words(v1_pairs)[:, 0:SEG], 0)
-        nc.scalar.activation(warm[:, 4:8], warm[:, 0:4], SQUARE)
         nc.sync.dma_start(offsets[:], offs)
         nc.sync.dma_start(vs_tab[P - 1 : P, :], vs[0:1, :])
         make_identity(nc, ident[:])
 
-        for b in range(B):
-            for u in range(2):
-                for a in (0, 512):
-                    load_keys(b, u, a, a + 512)
+        load_keys(0, 0, 512, 1024, nc.sync)
+        for b, u in ((0, 1), (1, 0), (1, 1)):
+            for a in (0, 512):
+                load_keys(b, u, a, a + 512, nc.sync)
         load_queries()
         load_values1(0, 512)
         load_values1(512, 1024)
@@ -302,7 +293,8 @@ def tile_attend_relu2_seg_kernel(tc, qT, kT, vT, vs, offs, out):
         score(0)
         score(1)
         cast_values1(0, 512, "S")
-        cast_values1(512, 1024, "S")
+        cast_values1(512, 768, "S")
+        cast_values1(768, 1024, "V")
         place_positive("v1_raw")
         relu(0, "S")
         square(0, "S")
@@ -322,12 +314,16 @@ def tile_attend_relu2_seg_kernel(tc, qT, kT, vT, vs, offs, out):
         settle_values0(1, "S")
         weigh(0)
         weigh(1)
-        invert_totals("V")
+        invert_totals()
+        quantize_values0(0, HALF)
         quantize_late(0, 512)
-        quantize_values0(0, DV)
+        quantize_values0(HALF, DV)
         multiply_values(1, 0, DV, "product0")
-        multiply_values(0, 0, DV, "product1")
+        multiply_values(0, 0, HALF, "product1")
+        multiply_values(0, HALF, DV, "turn_p0")
         settle_output(1, 0, DV, "S")
         store_output(1, 0, DV, nc.sync)
-        settle_output(0, 0, DV, "S")
-        store_output(0, 0, DV, nc.scalar)
+        settle_output(0, 0, HALF, "V")
+        store_output(0, 0, HALF, nc.sync)
+        settle_output(0, HALF, DV, "S")
+        store_output(0, HALF, DV, nc.scalar)

@@ -16,6 +16,7 @@ U16 = mybir.dt.uint16
 U8 = mybir.dt.uint8
 FP8X4 = mybir.dt.float8_e4m3fn_x4
 COPY = mybir.ActivationFunctionType.Copy
+IDENTITY = mybir.ActivationFunctionType.Identity
 RELU = mybir.ActivationFunctionType.Relu
 SQUARE = mybir.ActivationFunctionType.Square
 MAX = mybir.AluOpType.max
@@ -57,10 +58,11 @@ def tile_attend_relu2_seg_kernel(tc, qT, kT, vT, vs, offs, out):
         w_at = [0, NQ]
         v_at = [B * NQ + DV, B * NQ]
         positive = []
-        squares = [keep.tile([P, N + 16], F32, name="squares%d" % b) for b in range(B)]
+        squares = [keep.tile([P, N], F32, name="squares%d" % b) for b in range(B)]
         total = keep.tile([P, B], F32, name="total")
+        total_and_one = keep.tile([P, B], F32, name="total_and_one")
         recip = keep.tile([P, B], F32, name="recip")
-        y_sb = [keep.tile([P, DV], F32, name="y_sb%d" % b, align_bytes=64) for b in range(B)]
+        y_sb = [keep.tile([P, DV], F32, name="y_sb%d" % b) for b in range(B)]
         bank = {}
         kv = kT.rearrange("(p j) n -> p j n", j=PACK)
 
@@ -152,8 +154,7 @@ def tile_attend_relu2_seg_kernel(tc, qT, kT, vT, vs, offs, out):
             bank[("s", b)] = scores
 
         def place_positive(tag):
-            held = keep.tile([P, B, N + 16], F32, name=tag, align_bytes=64)
-            nc.gpsimd.memset(held[:, :, N : N + 1], 1.0)
+            held = keep.tile([P, B, N], F32, name=tag, align_bytes=64)
             for b in range(B):
                 positive.append(held[:, b, :])
 
@@ -166,12 +167,12 @@ def tile_attend_relu2_seg_kernel(tc, qT, kT, vT, vs, offs, out):
                 nc.vector.tensor_scalar(target, source, 0.0, None, op0=MAX)
 
         def square(b, engine):
-            source = positive[b][:, 0 : N + 1]
+            source = positive[b]
             if engine == "S":
-                nc.scalar.activation(squares[b][:, 0 : N + 1], source, SQUARE, accum_out=total[:, b : b + 1])
+                nc.scalar.activation(squares[b][:], source, SQUARE, accum_out=total[:, b : b + 1])
             else:
                 nc.vector.scalar_tensor_tensor(
-                    out=squares[b][:, 0 : N + 1], in0=source, scalar=0.0, in1=source, op0=MAX, op1=MULT,
+                    out=squares[b][:], in0=source, scalar=0.0, in1=source, op0=MAX, op1=MULT,
                     accum_out=total[:, b : b + 1],
                 )
 
@@ -185,8 +186,14 @@ def tile_attend_relu2_seg_kernel(tc, qT, kT, vT, vs, offs, out):
         def quantize_late(c0, c1):
             quantize(late_codes[:, c0:c1], late_scales[:, c0:c1], late_in[:, c0:c1, :].rearrange("s c t -> s (c t)"))
 
+        def add_one(engine):
+            if engine == "S":
+                nc.scalar.activation(total_and_one[:], total[:], IDENTITY, bias=1.0)
+            else:
+                nc.vector.tensor_scalar(total_and_one[:], total[:], 1.0, None, op0=ADD)
+
         def invert_totals():
-            nc.vector.reciprocal(recip[:], total[:])
+            nc.vector.reciprocal(recip[:], total_and_one[:])
 
         def cast_values1(a0, a1, engine):
             copy_on(engine, v1_pairs[:, SEG + a0 : SEG + a1, :], v1_raw[:, :, a0:a1].rearrange("p h n -> p n h"))
@@ -251,11 +258,11 @@ def tile_attend_relu2_seg_kernel(tc, qT, kT, vT, vs, offs, out):
         def store_output(b, e0, e1, queue):
             queue.dma_start(out[b][:, e0:e1], y_sb[b][:, e0:e1])
 
-        load_keys(0, 0, 0, 512, nc.scalar)
+        load_keys(0, 0, 0, 512, nc.sync)
         nc.vector.memset(vs_tab[0 : P - 1, :], 0.0)
         nc.vector.memset(words(v1_pairs)[:, 0:SEG], 0)
         nc.sync.dma_start(offsets[:], offs)
-        nc.sync.dma_start(vs_tab[P - 1 : P, :], vs[0:1, :])
+        nc.scalar.dma_start(vs_tab[P - 1 : P, :], vs[0:1, :])
         make_identity(nc, ident[:])
 
         load_keys(0, 0, 512, 1024, nc.sync)
@@ -270,12 +277,11 @@ def tile_attend_relu2_seg_kernel(tc, qT, kT, vT, vs, offs, out):
         gather_scales()
         turn_scales()
         cast_keys(0, 0, 0, 512, "S")
-        cast_keys(0, 0, 512, 1024, "V")
+        cast_keys(0, 0, 512, 1024, "S")
         gather_keys(0, 0)
         take_scales("V")
         cast_keys(0, 1, 0, 512, "S")
-        cast_keys(0, 1, 512, 768, "S")
-        cast_keys(0, 1, 768, 1024, "V")
+        cast_keys(0, 1, 512, 1024, "S")
         gather_keys(0, 1)
         cast_keys(1, 0, 0, 512, "S")
         cast_keys(1, 0, 512, 1024, "S")
@@ -313,17 +319,14 @@ def tile_attend_relu2_seg_kernel(tc, qT, kT, vT, vs, offs, out):
         settle_values1(0, 2, "S")
         settle_values0(1, "S")
         weigh(0)
+        add_one("V")
         weigh(1)
         invert_totals()
-        quantize_values0(0, HALF)
         quantize_late(0, 512)
-        quantize_values0(HALF, DV)
+        quantize_values0(0, DV)
         multiply_values(1, 0, DV, "product0")
-        multiply_values(0, 0, HALF, "product1")
-        multiply_values(0, HALF, DV, "turn_p0")
+        multiply_values(0, 0, DV, "product1")
         settle_output(1, 0, DV, "S")
         store_output(1, 0, DV, nc.sync)
-        settle_output(0, 0, HALF, "V")
-        store_output(0, 0, HALF, nc.sync)
-        settle_output(0, HALF, DV, "S")
-        store_output(0, HALF, DV, nc.scalar)
+        settle_output(0, 0, DV, "S")
+        store_output(0, 0, DV, nc.scalar)

@@ -7,7 +7,9 @@ B, NQ, N, T, D, DV = 2, 128, 512, 2048, 512, 256
 P = 128
 PACK = 4
 SEG = T // B
+CHUNK = SEG // 2
 HALF = DV // 2
+LIST_ROWS = 16
 
 F32 = mybir.dt.float32
 BF16 = mybir.dt.bfloat16
@@ -16,15 +18,13 @@ U16 = mybir.dt.uint16
 U8 = mybir.dt.uint8
 FP8X4 = mybir.dt.float8_e4m3fn_x4
 COPY = mybir.ActivationFunctionType.Copy
-IDENTITY = mybir.ActivationFunctionType.Identity
 RELU = mybir.ActivationFunctionType.Relu
 SQUARE = mybir.ActivationFunctionType.Square
-MAX = mybir.AluOpType.max
 MULT = mybir.AluOpType.mult
 ADD = mybir.AluOpType.add
 
 FLOPS = 2 * B * NQ * N * (D + DV)
-BYTES = 4 * (B * D * NQ + D * T + DV * T + T + B * NQ * DV) + 2 * P * (B * N // 16)
+BYTES = 4 * (B * D * NQ + D * T + DV * T + T + B * NQ * DV) + 2 * P * (B * N // LIST_ROWS)
 
 
 def tile_attend_relu2_seg_kernel(tc, qT, kT, vT, vs, offs, out):
@@ -33,7 +33,7 @@ def tile_attend_relu2_seg_kernel(tc, qT, kT, vT, vs, offs, out):
         keep = ctx.enter_context(tc.tile_pool(name="keep", bufs=1))
         psum = ctx.enter_context(tc.psum_pool(name="psum", bufs=1))
 
-        offsets = keep.tile([P, B * N // 16], U16, name="offsets")
+        offsets = keep.tile([P, B * N // LIST_ROWS], U16, name="offsets")
         vs_tab = keep.tile([P, T], F32, name="vs_tab")
         ident = keep.tile([P, P], F32, name="ident")
         q_raw = keep.tile([P, B, PACK * NQ], F32, name="q_raw")
@@ -52,281 +52,179 @@ def tile_attend_relu2_seg_kernel(tc, qT, kT, vT, vs, offs, out):
         v1_raw = keep.tile([P, 2, SEG], F32, name="v1_raw", align_bytes=64)
         v1_pairs = keep.tile([P, T, 2], BF16, name="v1_pairs", align_bytes=64)
         v1_got = keep.tile([P, PACK, P], U32, name="v1_got", align_bytes=64)
-        late_in = keep.tile([P, B * NQ + DV, PACK], BF16, name="late_in", align_bytes=64)
-        late_codes = keep.tile([P, B * (NQ + DV)], U32, name="late_codes", align_bytes=64)
-        late_scales = keep.tile([P, B * (NQ + DV)], U8, name="late_scales", align_bytes=64)
+        joint = B * NQ + DV
         w_at = [0, NQ]
-        v_at = [B * NQ + DV, B * NQ]
-        positive = []
+        v_at = [joint, B * NQ]
+        joint_in = keep.tile([P, joint, PACK], BF16, name="joint_in", align_bytes=64)
+        second_codes = keep.tile([P, B * (NQ + DV)], U32, name="second_codes", align_bytes=64)
+        second_scales = keep.tile([P, B * (NQ + DV)], U8, name="second_scales", align_bytes=64)
         squares = [keep.tile([P, N], F32, name="squares%d" % b) for b in range(B)]
         total = keep.tile([P, B], F32, name="total")
         total_and_one = keep.tile([P, B], F32, name="total_and_one")
         recip = keep.tile([P, B], F32, name="recip")
         y_sb = [keep.tile([P, DV], F32, name="y_sb%d" % b) for b in range(B)]
-        bank = {}
-        kv = kT.rearrange("(p j) n -> p j n", j=PACK)
+        key_rows = kT.rearrange("(p j) n -> p j n", j=PACK)
+        value_rows = vT.rearrange("(h p) n -> p h n", h=2)
 
         def listed(b):
-            return offsets[:, b * (N // 16) : (b + 1) * (N // 16)]
+            return offsets[:, b * (N // LIST_ROWS) : (b + 1) * (N // LIST_ROWS)]
 
         def words(pairs):
             return pairs[:].rearrange("p n e -> p (n e)").bitcast(U32)
 
-        def copy_on(engine, target, source):
-            if engine == "S":
-                nc.scalar.activation(target, source, COPY)
-            else:
-                nc.vector.tensor_copy(target, source)
-
-        def load_queries():
-            nc.sync.dma_start(q_raw[:], qT.rearrange("b (p j) q -> p b (j q)", j=PACK))
-
-        def load_keys(b, u, a0, a1, queue):
-            queue.dma_start(k_raw[b][u][:, :, a0:a1], kv[:, 2 * u : 2 * u + 2, b * SEG + a0 : b * SEG + a1])
-
-        def load_values0(h):
-            nc.sync.dma_start(v0_raw[h][:], vT[h * P : (h + 1) * P, 0:SEG])
-
-        def load_values1(a0, a1):
-            nc.sync.dma_start(v1_raw[:, :, a0:a1], vT.rearrange("(h p) n -> p h n", h=2)[:, :, SEG + a0 : SEG + a1])
-
-        def cast_queries(engine):
-            source = q_raw[:].rearrange("p b (j q) -> p b q j", j=PACK)
-            if engine == "G":
-                nc.gpsimd.tensor_scalar(q_in[:], source, 1.0, 0.0, op0=MULT, op1=ADD)
-            else:
-                copy_on(engine, q_in[:], source)
-
         def quantize(codes, scales, source):
             nc.vector.quantize_mx(out=codes.bitcast(FP8X4), scales=scales, in_=source)
 
-        def quantize_queries():
-            quantize(q_codes[:], q_scales[:], q_in[:].rearrange("p b q j -> p (b q j)"))
-
-        def gather_scales():
-            nc.vector.tensor_copy(vs_got[:], vs_tab[:].indirect(offsets[:]))
-
-        def turn(key, tag, count, source):
+        def turn(tag, count, source):
             turned = psum.tile([P, PACK, P], F32, name=tag)
             for t in range(count):
                 nc.tensor.transpose(turned[:, t, :], source(t), ident[:])
-            bank[key] = turned
+            return turned
 
-        def turn_scales():
-            turned = psum.tile([P, PACK, P], F32, name="turn_v00")
-            flat = turned[:].rearrange("s t e -> s (t e)")
-            for k in reversed(range(B * PACK)):
-                b, t = divmod(k, PACK)
-                nc.tensor.transpose(flat[:, 2 * k : 2 * k + P], vs_got[:, b * N + t : (b + 1) * N : PACK], ident[:])
-            bank["vs"] = flat
+        def load_keys(b, u, a0, a1):
+            nc.sync.dma_start(k_raw[b][u][:, :, a0:a1], key_rows[:, 2 * u : 2 * u + 2, b * SEG + a0 : b * SEG + a1])
 
-        def take_scales(engine):
-            bank["cols"] = keep.tile([P, B * PACK], F32, name="k_raw00")
-            copy_on(engine, bank["cols"][:], bank["vs"][:, P - 1 : P - 1 + 2 * B * PACK : 2])
-
-        def cast_keys(b, u, a0, a1, engine):
-            copy_on(engine, k_pairs[u][:, b * SEG + a0 : b * SEG + a1, :], k_raw[b][u][:, :, a0:a1].rearrange("p e n -> p n e"))
+        def key_chunk(b, u, c):
+            a0, a1 = c * CHUNK, (c + 1) * CHUNK
+            return k_pairs[u][:, b * SEG + a0 : b * SEG + a1, :], k_raw[b][u][:, :, a0:a1].rearrange("p e n -> p n e")
 
         def gather_keys(b, u):
             nc.vector.tensor_copy(k_got[b][:, u, :], words(k_pairs[u])[:, 0 : (b + 1) * SEG].indirect(listed(b)))
 
-        def lay_keys(b, engine):
-            source = k_got[b][:].rearrange("p u n -> p n u")
-            if engine == "S":
-                nc.scalar.copy(k_in[b][:], source)
-            else:
-                nc.vector.tensor_copy(k_in[b][:], source)
-
-        def quantize_keys(b):
+        def lay_and_quantize_keys(b):
+            nc.vector.tensor_copy(k_in[b][:], k_got[b][:].rearrange("p u n -> p n u"))
             quantize(k_codes[b][:], k_scales[b][:], k_in[b][:].rearrange("p n u -> p (n u)").bitcast(BF16))
 
-        def score(b):
-            scores = psum.tile([P, N], F32, name="product%d" % b)
+        def product(tag, width, left_codes, left_scales, right_codes, right_scales):
+            sums = psum.tile([P, width], F32, name=tag)
             nc.tensor.matmul_mx(
-                out=scores[:],
-                lhsT=q_codes[:, b * NQ : (b + 1) * NQ].bitcast(FP8X4),
-                lhsT_scale=q_scales[:, b * NQ : (b + 1) * NQ],
-                rhs=k_codes[b][:].bitcast(FP8X4),
-                rhs_scale=k_scales[b][:],
+                out=sums[:],
+                lhsT=left_codes.bitcast(FP8X4),
+                lhsT_scale=left_scales,
+                rhs=right_codes.bitcast(FP8X4),
+                rhs_scale=right_scales,
                 start=True,
                 stop=True,
             )
-            bank[("s", b)] = scores
+            return sums
 
-        def place_positive(tag):
-            held = keep.tile([P, B, N], F32, name=tag, align_bytes=64)
-            for b in range(B):
-                positive.append(held[:, b, :])
-
-        def relu(b, engine):
-            target = positive[b][:, 0:N].rearrange("q (t s) -> q t s", t=PACK)
-            source = bank[("s", b)][:].rearrange("q (s t) -> q t s", t=PACK)
-            if engine == "S":
-                nc.scalar.activation(target, source, RELU)
-            else:
-                nc.vector.tensor_scalar(target, source, 0.0, None, op0=MAX)
-
-        def square(b, engine):
-            source = positive[b]
-            if engine == "S":
-                nc.scalar.activation(squares[b][:], source, SQUARE, accum_out=total[:, b : b + 1])
-            else:
-                nc.vector.scalar_tensor_tensor(
-                    out=squares[b][:], in0=source, scalar=0.0, in1=source, op0=MAX, op1=MULT,
-                    accum_out=total[:, b : b + 1],
-                )
-
-        def turn_squares(b):
-            turn(("p", b), "turn_p%d" % b, PACK, lambda t: squares[b][:, t * P : (t + 1) * P])
-
-        def weigh(b):
-            spread = bank["cols"][:, b * PACK : (b + 1) * PACK].unsqueeze(1).to_broadcast([P, NQ, PACK])
-            nc.vector.tensor_tensor(late_in[:, w_at[b] : w_at[b] + NQ, :], bank[("p", b)][:].rearrange("s t q -> s q t"), spread, MULT)
-
-        def quantize_late(c0, c1):
-            quantize(late_codes[:, c0:c1], late_scales[:, c0:c1], late_in[:, c0:c1, :].rearrange("s c t -> s (c t)"))
-
-        def add_one(engine):
-            if engine == "S":
-                nc.scalar.activation(total_and_one[:], total[:], IDENTITY, bias=1.0)
-            else:
-                nc.vector.tensor_scalar(total_and_one[:], total[:], 1.0, None, op0=ADD)
-
-        def invert_totals():
-            nc.vector.reciprocal(recip[:], total_and_one[:])
-
-        def cast_values1(a0, a1, engine):
-            copy_on(engine, v1_pairs[:, SEG + a0 : SEG + a1, :], v1_raw[:, :, a0:a1].rearrange("p h n -> p n h"))
-
-        def gather_values1():
-            nc.vector.tensor_copy(v1_got[:].rearrange("p t s -> p s t"), words(v1_pairs).indirect(listed(1)))
-
-        def turn_values1():
-            turn(("v", 1), "turn_v1", PACK, lambda t: v1_got[:, t, :].bitcast(F32))
-
-        def settle_values1(h0, h1, engine):
-            pairs = bank[("v", 1)][:].rearrange("s t p -> s (t p)").bitcast(BF16)
-            source = pairs.rearrange("s (t p h) -> s h p t", t=PACK, h=2)[:, h0:h1, :, :]
-            target = late_in[:, v_at[1] : v_at[1] + DV, :].rearrange("s (h p) t -> s h p t", h=2)[:, h0:h1, :, :]
-            if engine == "S":
-                nc.scalar.copy(target, source)
-            else:
-                nc.vector.tensor_copy(target, source)
+        def weigh(b, turned_squares, scale_cols):
+            spread = scale_cols[:, b * PACK : (b + 1) * PACK].unsqueeze(1).to_broadcast([P, NQ, PACK])
+            nc.vector.tensor_tensor(
+                joint_in[:, w_at[b] : w_at[b] + NQ, :], turned_squares[:].rearrange("s t q -> s q t"), spread, MULT
+            )
 
         def gather_values0(h):
             nc.vector.tensor_copy(v0_got[h][:], v0_raw[h][:].indirect(listed(0)))
 
         def turn_values0(h):
-            turn(("v", 0, h), "turn_v00", 2, lambda u: v0_got[h][:].bitcast(F32)[:, u : N // 2 : 2])
+            return turn("shared_turn", 2, lambda u: v0_got[h][:].bitcast(F32)[:, u : N // 2 : 2])
 
-        def place_values0(tag):
-            bank["v0_in"] = keep.tile([P, DV, PACK], BF16, name=tag, align_bytes=64)
+        def settle_values0(h, turned, v0_in):
+            target = v0_in[:, h * HALF : (h + 1) * HALF, :].rearrange("s e t -> s (e t)").bitcast(F32)
+            nc.scalar.copy(target.rearrange("s (e u) -> s e u", u=2), turned[:, 0:2, :].rearrange("s u e -> s e u"))
 
-        def quantize_values0(e0, e1):
-            c0, c1 = v_at[0] + e0, v_at[0] + e1
-            quantize(late_codes[:, c0:c1], late_scales[:, c0:c1], bank["v0_in"][:, e0:e1, :].rearrange("s c t -> s (c t)"))
-
-        def settle_values0(h, engine):
-            target = bank["v0_in"][:, h * HALF : (h + 1) * HALF, :].rearrange("s e t -> s (e t)").bitcast(F32)
-            target = target.rearrange("s (e u) -> s e u", u=2)
-            source = bank[("v", 0, h)][:, 0:2, :].rearrange("s u e -> s e u")
-            if engine == "S":
-                nc.scalar.copy(target, source)
-            else:
-                nc.vector.tensor_copy(target, source)
-
-        def multiply_values(b, e0, e1, tag):
-            y = psum.tile([P, DV], F32, name=tag)
-            nc.tensor.matmul_mx(
-                out=y[:, 0 : e1 - e0],
-                lhsT=late_codes[:, w_at[b] : w_at[b] + NQ].bitcast(FP8X4),
-                lhsT_scale=late_scales[:, w_at[b] : w_at[b] + NQ],
-                rhs=late_codes[:, v_at[b] + e0 : v_at[b] + e1].bitcast(FP8X4),
-                rhs_scale=late_scales[:, v_at[b] + e0 : v_at[b] + e1],
-                start=True,
-                stop=True,
-            )
-            bank[("y", b, e0)] = y
-
-        def settle_output(b, e0, e1, engine):
-            source = bank[("y", b, e0)][:, 0 : e1 - e0]
-            if engine == "S":
-                nc.scalar.activation(y_sb[b][:, e0:e1], source, COPY, scale=recip[:, b : b + 1])
-            else:
-                nc.vector.tensor_scalar(y_sb[b][:, e0:e1], source, recip[:, b : b + 1], None, op0=MULT)
-
-        def store_output(b, e0, e1, queue):
-            queue.dma_start(out[b][:, e0:e1], y_sb[b][:, e0:e1])
-
-        load_keys(0, 0, 0, 512, nc.sync)
         nc.vector.memset(vs_tab[0 : P - 1, :], 0.0)
         nc.vector.memset(words(v1_pairs)[:, 0:SEG], 0)
         nc.sync.dma_start(offsets[:], offs)
-        nc.scalar.dma_start(vs_tab[P - 1 : P, :], vs[0:1, :])
+        nc.sync.dma_start(vs_tab[P - 1 : P, :], vs[0:1, :])
         make_identity(nc, ident[:])
 
-        load_keys(0, 0, 512, 1024, nc.sync)
-        for b, u in ((0, 1), (1, 0), (1, 1)):
-            for a in (0, 512):
-                load_keys(b, u, a, a + 512, nc.sync)
-        load_queries()
-        load_values1(0, 512)
-        load_values1(512, 1024)
-        load_values0(0)
-        load_values0(1)
-        gather_scales()
-        turn_scales()
-        cast_keys(0, 0, 0, 512, "S")
-        cast_keys(0, 0, 512, 1024, "S")
+        for u in range(2):
+            load_keys(0, u, 0, SEG)
+        for u in range(2):
+            for c in range(2):
+                load_keys(1, u, c * CHUNK, (c + 1) * CHUNK)
+        nc.sync.dma_start(q_raw[:], qT.rearrange("b (p j) q -> p b (j q)", j=PACK))
+        for c in range(2):
+            a0, a1 = c * CHUNK, (c + 1) * CHUNK
+            nc.sync.dma_start(v1_raw[:, :, a0:a1], value_rows[:, :, SEG + a0 : SEG + a1])
+        for h in range(2):
+            nc.sync.dma_start(v0_raw[h][:], vT[h * P : (h + 1) * P, 0:SEG])
+
+        nc.vector.tensor_copy(vs_got[:], vs_tab[:].indirect(offsets[:]))
+        turned_scales = psum.tile([P, PACK, P], F32, name="shared_turn")
+        turned_flat = turned_scales[:].rearrange("s t e -> s (t e)")
+        for k in reversed(range(B * PACK)):
+            b, t = divmod(k, PACK)
+            nc.tensor.transpose(turned_flat[:, 2 * k : 2 * k + P], vs_got[:, b * N + t : (b + 1) * N : PACK], ident[:])
+
+        nc.scalar.activation(*key_chunk(0, 0, 0), COPY)
+        nc.vector.tensor_copy(*key_chunk(0, 0, 1))
         gather_keys(0, 0)
-        take_scales("V")
-        cast_keys(0, 1, 0, 512, "S")
-        cast_keys(0, 1, 512, 1024, "S")
+        scale_cols = keep.tile([P, B * PACK], F32, name="k_raw00")
+        nc.vector.tensor_copy(scale_cols[:], turned_flat[:, P - 1 : P - 1 + 2 * B * PACK : 2])
+        nc.scalar.activation(*key_chunk(0, 1, 0), COPY)
+        nc.vector.tensor_copy(*key_chunk(0, 1, 1))
         gather_keys(0, 1)
-        cast_keys(1, 0, 0, 512, "S")
-        cast_keys(1, 0, 512, 1024, "S")
-        lay_keys(0, "V")
-        quantize_keys(0)
+
+        for c in range(2):
+            nc.scalar.activation(*key_chunk(1, 0, c), COPY)
+        lay_and_quantize_keys(0)
         gather_keys(1, 0)
-        cast_keys(1, 1, 0, 512, "S")
-        cast_keys(1, 1, 512, 768, "S")
-        cast_keys(1, 1, 768, 1024, "V")
+        for c in range(2):
+            nc.scalar.activation(*key_chunk(1, 1, c), COPY)
         gather_keys(1, 1)
-        cast_queries("S")
-        lay_keys(1, "V")
-        quantize_keys(1)
-        quantize_queries()
-        score(0)
-        score(1)
-        cast_values1(0, 512, "S")
-        cast_values1(512, 768, "S")
-        cast_values1(768, 1024, "V")
-        place_positive("v1_raw")
-        relu(0, "S")
-        square(0, "S")
-        turn_squares(0)
-        relu(1, "S")
-        square(1, "S")
-        turn_squares(1)
-        gather_values1()
-        turn_values1()
+        nc.scalar.activation(q_in[:], q_raw[:].rearrange("p b (j q) -> p b q j", j=PACK), COPY)
+        lay_and_quantize_keys(1)
+        quantize(q_codes[:], q_scales[:], q_in[:].rearrange("p b q j -> p (b q j)"))
+
+        scores = []
+        for b in range(B):
+            queries = slice(b * NQ, (b + 1) * NQ)
+            scores.append(
+                product("product%d" % b, N, q_codes[:, queries], q_scales[:, queries], k_codes[b][:], k_scales[b][:])
+            )
+
+        for c in range(2):
+            a0, a1 = c * CHUNK, (c + 1) * CHUNK
+            nc.scalar.activation(
+                v1_pairs[:, SEG + a0 : SEG + a1, :], v1_raw[:, :, a0:a1].rearrange("p h n -> p n h"), COPY
+            )
+
+        positive = keep.tile([P, B, N], F32, name="v1_raw", align_bytes=64)
+        turned_squares = []
+        for b in range(B):
+            nc.scalar.activation(
+                positive[:, b, :].rearrange("q (t s) -> q t s", t=PACK),
+                scores[b][:].rearrange("q (s t) -> q t s", t=PACK),
+                RELU,
+            )
+            nc.scalar.activation(squares[b][:], positive[:, b, :], SQUARE, accum_out=total[:, b : b + 1])
+            turned_squares.append(turn("turn_p%d" % b, PACK, lambda t: squares[b][:, t * P : (t + 1) * P]))
+
+        nc.vector.tensor_copy(v1_got[:].rearrange("p t s -> p s t"), words(v1_pairs).indirect(listed(1)))
+        turned_v1 = turn("turn_v1", PACK, lambda t: v1_got[:, t, :].bitcast(F32))
+
         gather_values0(0)
-        turn_values0(0)
+        turned_v0 = turn_values0(0)
         gather_values0(1)
-        place_values0("v1_raw")
-        settle_values0(0, "S")
-        turn_values0(1)
-        settle_values1(0, 2, "S")
-        settle_values0(1, "S")
-        weigh(0)
-        add_one("V")
-        weigh(1)
-        invert_totals()
-        quantize_late(0, 512)
-        quantize_values0(0, DV)
-        multiply_values(1, 0, DV, "product0")
-        multiply_values(0, 0, DV, "product1")
-        settle_output(1, 0, DV, "S")
-        store_output(1, 0, DV, nc.sync)
-        settle_output(0, 0, DV, "S")
-        store_output(0, 0, DV, nc.scalar)
+        v0_in = keep.tile([P, DV, PACK], BF16, name="v1_raw", align_bytes=64)
+        settle_values0(0, turned_v0, v0_in)
+        turned_v0 = turn_values0(1)
+        v1_halves = turned_v1[:].rearrange("s t p -> s (t p)").bitcast(BF16)
+        nc.scalar.copy(
+            joint_in[:, v_at[1] : v_at[1] + DV, :].rearrange("s (h p) t -> s h p t", h=2),
+            v1_halves.rearrange("s (t p h) -> s h p t", t=PACK, h=2),
+        )
+        settle_values0(1, turned_v0, v0_in)
+
+        weigh(0, turned_squares[0], scale_cols)
+        nc.vector.tensor_scalar(total_and_one[:], total[:], 1.0, None, op0=ADD)
+        weigh(1, turned_squares[1], scale_cols)
+        nc.vector.reciprocal(recip[:], total_and_one[:])
+        quantize(second_codes[:, 0:joint], second_scales[:, 0:joint], joint_in[:].rearrange("s c t -> s (c t)"))
+        v0_cols = slice(v_at[0], v_at[0] + DV)
+        quantize(second_codes[:, v0_cols], second_scales[:, v0_cols], v0_in[:].rearrange("s c t -> s (c t)"))
+
+        order = (1, 0)
+        sums = {}
+        for place, b in enumerate(order):
+            w_cols, v_cols = slice(w_at[b], w_at[b] + NQ), slice(v_at[b], v_at[b] + DV)
+            sums[b] = product(
+                "product%d" % place, DV,
+                second_codes[:, w_cols], second_scales[:, w_cols], second_codes[:, v_cols], second_scales[:, v_cols],
+            )
+        for b, queue in zip(order, (nc.sync, nc.scalar)):
+            nc.scalar.activation(y_sb[b][:], sums[b][:], COPY, scale=recip[:, b : b + 1])
+            queue.dma_start(out[b], y_sb[b][:])

@@ -18,10 +18,10 @@ U16 = mybir.dt.uint16
 U8 = mybir.dt.uint8
 FP8X4 = mybir.dt.float8_e4m3fn_x4
 COPY = mybir.ActivationFunctionType.Copy
+IDENTITY = mybir.ActivationFunctionType.Identity
 RELU = mybir.ActivationFunctionType.Relu
 SQUARE = mybir.ActivationFunctionType.Square
 MULT = mybir.AluOpType.mult
-ADD = mybir.AluOpType.add
 
 FLOPS = 2 * B * NQ * N * (D + DV)
 BYTES = 4 * (B * D * NQ + D * T + DV * T + T + B * NQ * DV) + 2 * P * (B * N // LIST_ROWS)
@@ -41,21 +41,21 @@ def tile_attend_relu2_seg_kernel(tc, qT, kT, vT, vs, offs, out):
         q_codes = keep.tile([P, B * NQ], U32, name="q_codes", align_bytes=64)
         q_scales = keep.tile([P, B * NQ], U8, name="q_scales", align_bytes=64)
         vs_got = keep.tile([P, B * N], F32, name="vs_got")
-        k_raw = [[keep.tile([P, 2, SEG], F32, name="k_raw%d%d" % (b, u)) for u in range(2)] for b in range(B)]
-        k_pairs = [keep.tile([P, T, 2], BF16, name="k_pairs%d" % u, align_bytes=64) for u in range(2)]
+        k0_raw = [keep.tile([P, 2, SEG], F32, name="k0_raw%d" % u) for u in range(2)]
+        k1_raw = [[keep.tile([P, 2, CHUNK], F32, name="k1_raw%d%d" % (u, c)) for c in range(2)] for u in range(2)]
+        k_pairs = [keep.tile([P, 2 * T], BF16, name="k_pairs%d" % u, align_bytes=64) for u in range(2)]
         k_got = [keep.tile([P, 2, N], U32, name="k_got%d" % b, align_bytes=64) for b in range(B)]
         k_in = [keep.tile([P, N, 2], U32, name="k_in%d" % b, align_bytes=64) for b in range(B)]
         k_codes = [keep.tile([P, N], U32, name="k_codes%d" % b, align_bytes=64) for b in range(B)]
         k_scales = [keep.tile([P, N], U8, name="k_scales%d" % b, align_bytes=64) for b in range(B)]
         v0_raw = [keep.tile([P, SEG], F32, name="v0_raw%d" % h) for h in range(2)]
         v0_got = [keep.tile([P, N], BF16, name="v0_got%d" % h, align_bytes=64) for h in range(2)]
-        v1_raw = keep.tile([P, 2, SEG], F32, name="v1_raw", align_bytes=64)
-        v1_pairs = keep.tile([P, T, 2], BF16, name="v1_pairs", align_bytes=64)
+        v1_raw = [keep.tile([P, 2, CHUNK], F32, name="v1_raw%d" % c, align_bytes=64) for c in range(2)]
+        v1_pairs = keep.tile([P, 2 * T], BF16, name="v1_pairs", align_bytes=64)
         v1_got = keep.tile([P, PACK, P], U32, name="v1_got", align_bytes=64)
-        joint = B * NQ + DV
-        w_at = [0, NQ]
-        v_at = [joint, B * NQ]
-        joint_in = keep.tile([P, joint, PACK], BF16, name="joint_in", align_bytes=64)
+        early = DV + NQ + HALF
+        w_at = [2 * DV + NQ, DV]
+        v_at = [DV + NQ, 0]
         second_codes = keep.tile([P, B * (NQ + DV)], U32, name="second_codes", align_bytes=64)
         second_scales = keep.tile([P, B * (NQ + DV)], U8, name="second_scales", align_bytes=64)
         squares = [keep.tile([P, N], F32, name="squares%d" % b) for b in range(B)]
@@ -70,7 +70,18 @@ def tile_attend_relu2_seg_kernel(tc, qT, kT, vT, vs, offs, out):
             return offsets[:, b * (N // LIST_ROWS) : (b + 1) * (N // LIST_ROWS)]
 
         def words(pairs):
-            return pairs[:].rearrange("p n e -> p (n e)").bitcast(U32)
+            return pairs[:].bitcast(U32)
+
+        def cast_views(pairs, first, raw, a0, a1):
+            target = pairs[:, 2 * (first + a0) : 2 * (first + a1)].rearrange("p (n e) -> p n e", e=2)
+            return target, raw[:, :, a0:a1].rearrange("p e n -> p n e")
+
+        def share_cast(pairs, first, raw, cut, width):
+            nc.scalar.activation(*cast_views(pairs, first, raw, 0, cut), COPY)
+            nc.vector.tensor_copy(*cast_views(pairs, first, raw, cut, width))
+
+        def scalar_cast(pairs, first, raw):
+            nc.scalar.activation(*cast_views(pairs, first, raw, 0, CHUNK), COPY)
 
         def quantize(codes, scales, source):
             nc.vector.quantize_mx(out=codes.bitcast(FP8X4), scales=scales, in_=source)
@@ -81,19 +92,19 @@ def tile_attend_relu2_seg_kernel(tc, qT, kT, vT, vs, offs, out):
                 nc.tensor.transpose(turned[:, t, :], source(t), ident[:])
             return turned
 
-        def load_keys(b, u, a0, a1):
-            nc.sync.dma_start(k_raw[b][u][:, :, a0:a1], key_rows[:, 2 * u : 2 * u + 2, b * SEG + a0 : b * SEG + a1])
+        def gather_keys(b, u, n0, n1):
+            entries = listed(b)[:, n0 // LIST_ROWS : n1 // LIST_ROWS]
+            nc.vector.tensor_copy(k_got[b][:, u, n0:n1], words(k_pairs[u])[:, 0 : (b + 1) * SEG].indirect(entries))
 
-        def key_chunk(b, u, c):
-            a0, a1 = c * CHUNK, (c + 1) * CHUNK
-            return k_pairs[u][:, b * SEG + a0 : b * SEG + a1, :], k_raw[b][u][:, :, a0:a1].rearrange("p e n -> p n e")
-
-        def gather_keys(b, u):
-            nc.vector.tensor_copy(k_got[b][:, u, :], words(k_pairs[u])[:, 0 : (b + 1) * SEG].indirect(listed(b)))
-
-        def lay_and_quantize_keys(b):
-            nc.vector.tensor_copy(k_in[b][:], k_got[b][:].rearrange("p u n -> p n u"))
-            quantize(k_codes[b][:], k_scales[b][:], k_in[b][:].rearrange("p n u -> p (n u)").bitcast(BF16))
+        def finish_keys(b):
+            halves = [(0, N // 2), (N // 2, N)]
+            for n0, n1 in halves:
+                gather_keys(b, 1, n0, n1)
+            for n0, n1 in halves:
+                nc.vector.tensor_copy(k_in[b][:, n0:n1, :], k_got[b][:, :, n0:n1].rearrange("p u n -> p n u"))
+            for n0, n1 in halves:
+                laid = k_in[b][:, n0:n1, :].rearrange("p n u -> p (n u)").bitcast(BF16)
+                quantize(k_codes[b][:, n0:n1], k_scales[b][:, n0:n1], laid)
 
         def product(tag, width, left_codes, left_scales, right_codes, right_scales):
             sums = psum.tile([P, width], F32, name=tag)
@@ -108,11 +119,9 @@ def tile_attend_relu2_seg_kernel(tc, qT, kT, vT, vs, offs, out):
             )
             return sums
 
-        def weigh(b, turned_squares, scale_cols):
+        def weigh(b, target, turned_squares, scale_cols):
             spread = scale_cols[:, b * PACK : (b + 1) * PACK].unsqueeze(1).to_broadcast([P, NQ, PACK])
-            nc.vector.tensor_tensor(
-                joint_in[:, w_at[b] : w_at[b] + NQ, :], turned_squares[:].rearrange("s t q -> s q t"), spread, MULT
-            )
+            nc.vector.tensor_tensor(target, turned_squares[:].rearrange("s t q -> s q t"), spread, MULT)
 
         def gather_values0(h):
             nc.vector.tensor_copy(v0_got[h][:], v0_raw[h][:].indirect(listed(0)))
@@ -120,25 +129,26 @@ def tile_attend_relu2_seg_kernel(tc, qT, kT, vT, vs, offs, out):
         def turn_values0(h):
             return turn("shared_turn", 2, lambda u: v0_got[h][:].bitcast(F32)[:, u : N // 2 : 2])
 
-        def settle_values0(h, turned, v0_in):
-            target = v0_in[:, h * HALF : (h + 1) * HALF, :].rearrange("s e t -> s (e t)").bitcast(F32)
-            nc.scalar.copy(target.rearrange("s (e u) -> s e u", u=2), turned[:, 0:2, :].rearrange("s u e -> s e u"))
+        def settle_values0(target, turned):
+            pairs = target.rearrange("s e t -> s (e t)").bitcast(F32)
+            nc.scalar.copy(pairs.rearrange("s (e u) -> s e u", u=2), turned[:, 0:2, :].rearrange("s u e -> s e u"))
 
         nc.vector.memset(vs_tab[0 : P - 1, :], 0.0)
-        nc.vector.memset(words(v1_pairs)[:, 0:SEG], 0)
         nc.sync.dma_start(offsets[:], offs)
         nc.sync.dma_start(vs_tab[P - 1 : P, :], vs[0:1, :])
         make_identity(nc, ident[:])
+        nc.gpsimd.memset(words(v1_pairs)[:, 0:SEG], 0)
 
         for u in range(2):
-            load_keys(0, u, 0, SEG)
+            nc.sync.dma_start(k0_raw[u][:], key_rows[:, 2 * u : 2 * u + 2, 0:SEG])
         for u in range(2):
             for c in range(2):
-                load_keys(1, u, c * CHUNK, (c + 1) * CHUNK)
+                a0 = SEG + c * CHUNK
+                nc.sync.dma_start(k1_raw[u][c][:], key_rows[:, 2 * u : 2 * u + 2, a0 : a0 + CHUNK])
         nc.sync.dma_start(q_raw[:], qT.rearrange("b (p j) q -> p b (j q)", j=PACK))
         for c in range(2):
-            a0, a1 = c * CHUNK, (c + 1) * CHUNK
-            nc.sync.dma_start(v1_raw[:, :, a0:a1], value_rows[:, :, SEG + a0 : SEG + a1])
+            a0 = SEG + c * CHUNK
+            nc.sync.dma_start(v1_raw[c][:], value_rows[:, :, a0 : a0 + CHUNK])
         for h in range(2):
             nc.sync.dma_start(v0_raw[h][:], vT[h * P : (h + 1) * P, 0:SEG])
 
@@ -149,49 +159,44 @@ def tile_attend_relu2_seg_kernel(tc, qT, kT, vT, vs, offs, out):
             b, t = divmod(k, PACK)
             nc.tensor.transpose(turned_flat[:, 2 * k : 2 * k + P], vs_got[:, b * N + t : (b + 1) * N : PACK], ident[:])
 
-        nc.scalar.activation(*key_chunk(0, 0, 0), COPY)
-        nc.vector.tensor_copy(*key_chunk(0, 0, 1))
-        gather_keys(0, 0)
-        scale_cols = keep.tile([P, B * PACK], F32, name="k_raw00")
+        share_cast(k_pairs[0], 0, k0_raw[0], SEG // 4, SEG)
+        gather_keys(0, 0, 0, N)
+        share_cast(k_pairs[1], 0, k0_raw[1], SEG // 2, SEG)
+        scale_cols = keep.tile([P, B * PACK], F32, name="k0_raw1")
         nc.vector.tensor_copy(scale_cols[:], turned_flat[:, P - 1 : P - 1 + 2 * B * PACK : 2])
-        nc.scalar.activation(*key_chunk(0, 1, 0), COPY)
-        nc.vector.tensor_copy(*key_chunk(0, 1, 1))
-        gather_keys(0, 1)
+        finish_keys(0)
 
         for c in range(2):
-            nc.scalar.activation(*key_chunk(1, 0, c), COPY)
-        lay_and_quantize_keys(0)
-        gather_keys(1, 0)
+            scalar_cast(k_pairs[0], SEG + c * CHUNK, k1_raw[0][c])
+        gather_keys(1, 0, 0, N)
         for c in range(2):
-            nc.scalar.activation(*key_chunk(1, 1, c), COPY)
-        gather_keys(1, 1)
+            scalar_cast(k_pairs[1], SEG + c * CHUNK, k1_raw[1][c])
         nc.scalar.activation(q_in[:], q_raw[:].rearrange("p b (j q) -> p b q j", j=PACK), COPY)
-        lay_and_quantize_keys(1)
+        finish_keys(1)
         quantize(q_codes[:], q_scales[:], q_in[:].rearrange("p b q j -> p (b q j)"))
 
-        scores = []
-        for b in range(B):
+        order = (1, 0)
+        scores = {}
+        for b in order:
             queries = slice(b * NQ, (b + 1) * NQ)
-            scores.append(
-                product("product%d" % b, N, q_codes[:, queries], q_scales[:, queries], k_codes[b][:], k_scales[b][:])
+            scores[b] = product(
+                "product%d" % b, N, q_codes[:, queries], q_scales[:, queries], k_codes[b][:], k_scales[b][:]
             )
 
         for c in range(2):
-            a0, a1 = c * CHUNK, (c + 1) * CHUNK
-            nc.scalar.activation(
-                v1_pairs[:, SEG + a0 : SEG + a1, :], v1_raw[:, :, a0:a1].rearrange("p h n -> p n h"), COPY
-            )
+            scalar_cast(v1_pairs, SEG + c * CHUNK, v1_raw[c])
 
-        positive = keep.tile([P, B, N], F32, name="v1_raw", align_bytes=64)
-        turned_squares = []
-        for b in range(B):
+        positive = keep.tile([P, B, N], F32, name="v1_raw1", align_bytes=64)
+        for b in order:
             nc.scalar.activation(
                 positive[:, b, :].rearrange("q (t s) -> q t s", t=PACK),
                 scores[b][:].rearrange("q (s t) -> q t s", t=PACK),
                 RELU,
             )
+        turned_squares = {}
+        for b in order:
             nc.scalar.activation(squares[b][:], positive[:, b, :], SQUARE, accum_out=total[:, b : b + 1])
-            turned_squares.append(turn("turn_p%d" % b, PACK, lambda t: squares[b][:, t * P : (t + 1) * P]))
+            turned_squares[b] = turn("turn_p%d" % b, PACK, lambda t: squares[b][:, t * P : (t + 1) * P])
 
         nc.vector.tensor_copy(v1_got[:].rearrange("p t s -> p s t"), words(v1_pairs).indirect(listed(1)))
         turned_v1 = turn("turn_v1", PACK, lambda t: v1_got[:, t, :].bitcast(F32))
@@ -199,30 +204,32 @@ def tile_attend_relu2_seg_kernel(tc, qT, kT, vT, vs, offs, out):
         gather_values0(0)
         turned_v0 = turn_values0(0)
         gather_values0(1)
-        v0_in = keep.tile([P, DV, PACK], BF16, name="v1_raw", align_bytes=64)
-        settle_values0(0, turned_v0, v0_in)
+        early_flat = keep.tile([P, early * PACK], BF16, name="v1_raw1", align_bytes=64)
+        late_flat = keep.tile([P, (HALF + NQ) * PACK], BF16, name="late_flat", align_bytes=64)
+        early_in = early_flat[:].rearrange("s (c t) -> s c t", t=PACK)
+        late_in = late_flat[:].rearrange("s (c t) -> s c t", t=PACK)
+        settle_values0(early_in[:, v_at[0] : v_at[0] + HALF, :], turned_v0)
         turned_v0 = turn_values0(1)
         v1_halves = turned_v1[:].rearrange("s t p -> s (t p)").bitcast(BF16)
         nc.scalar.copy(
-            joint_in[:, v_at[1] : v_at[1] + DV, :].rearrange("s (h p) t -> s h p t", h=2),
+            early_in[:, v_at[1] : v_at[1] + DV, :].rearrange("s (h p) t -> s h p t", h=2),
             v1_halves.rearrange("s (t p h) -> s h p t", t=PACK, h=2),
         )
-        settle_values0(1, turned_v0, v0_in)
+        settle_values0(late_in[:, 0:HALF, :], turned_v0)
+        nc.scalar.activation(total_and_one[:], total[:], IDENTITY, bias=1.0)
 
-        weigh(0, turned_squares[0], scale_cols)
-        nc.vector.tensor_scalar(total_and_one[:], total[:], 1.0, None, op0=ADD)
-        weigh(1, turned_squares[1], scale_cols)
+        weigh(1, early_in[:, w_at[1] : w_at[1] + NQ, :], turned_squares[1], scale_cols)
+        weigh(0, late_in[:, HALF : HALF + NQ, :], turned_squares[0], scale_cols)
         nc.vector.reciprocal(recip[:], total_and_one[:])
-        quantize(second_codes[:, 0:joint], second_scales[:, 0:joint], joint_in[:].rearrange("s c t -> s (c t)"))
-        v0_cols = slice(v_at[0], v_at[0] + DV)
-        quantize(second_codes[:, v0_cols], second_scales[:, v0_cols], v0_in[:].rearrange("s c t -> s (c t)"))
+        quantize(second_codes[:, 0:early], second_scales[:, 0:early], early_flat[:])
+        late = slice(early, B * (NQ + DV))
+        quantize(second_codes[:, late], second_scales[:, late], late_flat[:])
 
-        order = (1, 0)
         sums = {}
-        for place, b in enumerate(order):
+        for b in order:
             w_cols, v_cols = slice(w_at[b], w_at[b] + NQ), slice(v_at[b], v_at[b] + DV)
             sums[b] = product(
-                "product%d" % place, DV,
+                "product%d" % b, DV,
                 second_codes[:, w_cols], second_scales[:, w_cols], second_codes[:, v_cols], second_scales[:, v_cols],
             )
         for b, queue in zip(order, (nc.sync, nc.scalar)):

@@ -41,7 +41,8 @@ def tile_attend_relu2_seg_kernel(tc, qT, kT, vT, vs, offs, out):
         q_codes = keep.tile([P, B * NQ], U32, name="q_codes", align_bytes=64)
         q_scales = keep.tile([P, B * NQ], U8, name="q_scales", align_bytes=64)
         vs_got = keep.tile([P, B * N], F32, name="vs_got")
-        k0_raw = [keep.tile([P, 2, SEG], F32, name="k0_raw%d" % u) for u in range(2)]
+        first_raw = [keep.tile([P, 2, CHUNK], F32, name="first_raw%d" % c) for c in range(2)]
+        second_raw = keep.tile([P, 2, SEG], F32, name="second_raw")
         k1_raw = [[keep.tile([P, 2, CHUNK], F32, name="k1_raw%d%d" % (u, c)) for c in range(2)] for u in range(2)]
         k_pairs = [keep.tile([P, 2 * T], BF16, name="k_pairs%d" % u, align_bytes=64) for u in range(2)]
         k_got = [keep.tile([P, 2, N], U32, name="k_got%d" % b, align_bytes=64) for b in range(B)]
@@ -139,8 +140,9 @@ def tile_attend_relu2_seg_kernel(tc, qT, kT, vT, vs, offs, out):
         make_identity(nc, ident[:])
         nc.gpsimd.memset(words(v1_pairs)[:, 0:SEG], 0)
 
-        for u in range(2):
-            nc.sync.dma_start(k0_raw[u][:], key_rows[:, 2 * u : 2 * u + 2, 0:SEG])
+        for c in range(2):
+            nc.sync.dma_start(first_raw[c][:], key_rows[:, 0:2, c * CHUNK : (c + 1) * CHUNK])
+        nc.sync.dma_start(second_raw[:], key_rows[:, 2:4, 0:SEG])
         for u in range(2):
             for c in range(2):
                 a0 = SEG + c * CHUNK
@@ -159,10 +161,11 @@ def tile_attend_relu2_seg_kernel(tc, qT, kT, vT, vs, offs, out):
             b, t = divmod(k, PACK)
             nc.tensor.transpose(turned_flat[:, 2 * k : 2 * k + P], vs_got[:, b * N + t : (b + 1) * N : PACK], ident[:])
 
-        share_cast(k_pairs[0], 0, k0_raw[0], SEG // 4, SEG)
+        scalar_cast(k_pairs[0], 0, first_raw[0])
+        share_cast(k_pairs[0], CHUNK, first_raw[1], CHUNK // 4, CHUNK)
         gather_keys(0, 0, 0, N)
-        share_cast(k_pairs[1], 0, k0_raw[1], SEG // 2, SEG)
-        scale_cols = keep.tile([P, B * PACK], F32, name="k0_raw1")
+        share_cast(k_pairs[1], 0, second_raw, SEG // 2, SEG)
+        scale_cols = keep.tile([P, B * PACK], F32, name="second_raw")
         nc.vector.tensor_copy(scale_cols[:], turned_flat[:, P - 1 : P - 1 + 2 * B * PACK : 2])
         finish_keys(0)
 

@@ -7,7 +7,6 @@ B, NQ, N, T, D, DV = 2, 128, 512, 2048, 512, 256
 P = 128
 PACK = 4
 SEG = T // B
-CHUNK = SEG // 2
 HALF = DV // 2
 LIST_ROWS = 16
 
@@ -22,6 +21,7 @@ IDENTITY = mybir.ActivationFunctionType.Identity
 RELU = mybir.ActivationFunctionType.Relu
 SQUARE = mybir.ActivationFunctionType.Square
 MULT = mybir.AluOpType.mult
+ADD = mybir.AluOpType.add
 
 FLOPS = 2 * B * NQ * N * (D + DV)
 BYTES = 4 * (B * D * NQ + D * T + DV * T + T + B * NQ * DV) + 2 * P * (B * N // LIST_ROWS)
@@ -35,82 +35,72 @@ def tile_attend_relu2_seg_kernel(tc, qT, kT, vT, vs, offs, out):
 
         offsets = keep.tile([P, B * N // LIST_ROWS], U16, name="offsets")
         vs_tab = keep.tile([P, T], F32, name="vs_tab")
+        vs_got = keep.tile([P, B * N], F32, name="vs_got")
         ident = keep.tile([P, P], F32, name="ident")
         q_raw = keep.tile([P, B, PACK * NQ], F32, name="q_raw")
-        q_in = keep.tile([P, B, NQ, PACK], BF16, name="q_in", align_bytes=64)
+        q_in = keep.tile([P, B * NQ * PACK], BF16, name="q_in", align_bytes=64)
         q_codes = keep.tile([P, B * NQ], U32, name="q_codes", align_bytes=64)
         q_scales = keep.tile([P, B * NQ], U8, name="q_scales", align_bytes=64)
-        vs_got = keep.tile([P, B * N], F32, name="vs_got")
-        first_raw = [keep.tile([P, 2, CHUNK], F32, name="first_raw%d" % c) for c in range(2)]
-        second_raw = keep.tile([P, 2, SEG], F32, name="second_raw")
-        k1_raw = [[keep.tile([P, 2, CHUNK], F32, name="k1_raw%d%d" % (u, c)) for c in range(2)] for u in range(2)]
-        k_pairs = [keep.tile([P, 2 * T], BF16, name="k_pairs%d" % u, align_bytes=64) for u in range(2)]
-        k_got = [keep.tile([P, 2, N], U32, name="k_got%d" % b, align_bytes=64) for b in range(B)]
-        k_in = [keep.tile([P, N, 2], U32, name="k_in%d" % b, align_bytes=64) for b in range(B)]
+        k_tab = [keep.tile([P, T], F32, name="k_tab%d" % t) for t in range(PACK)]
+        k_in = [keep.tile([P, N * PACK], BF16, name="k_in%d" % b, align_bytes=64) for b in range(B)]
         k_codes = [keep.tile([P, N], U32, name="k_codes%d" % b, align_bytes=64) for b in range(B)]
         k_scales = [keep.tile([P, N], U8, name="k_scales%d" % b, align_bytes=64) for b in range(B)]
-        v0_raw = [keep.tile([P, SEG], F32, name="v0_raw%d" % h) for h in range(2)]
-        v0_got = [keep.tile([P, N], BF16, name="v0_got%d" % h, align_bytes=64) for h in range(2)]
-        v1_raw = [keep.tile([P, 2, CHUNK], F32, name="v1_raw%d" % c, align_bytes=64) for c in range(2)]
-        v1_pairs = keep.tile([P, 2 * T], BF16, name="v1_pairs", align_bytes=64)
-        v1_got = keep.tile([P, PACK, P], U32, name="v1_got", align_bytes=64)
-        early = DV + NQ + HALF
-        w_at = [2 * DV + NQ, DV]
-        v_at = [DV + NQ, 0]
-        second_codes = keep.tile([P, B * (NQ + DV)], U32, name="second_codes", align_bytes=64)
-        second_scales = keep.tile([P, B * (NQ + DV)], U8, name="second_scales", align_bytes=64)
-        squares = [keep.tile([P, N], F32, name="squares%d" % b) for b in range(B)]
-        total = keep.tile([P, B], F32, name="total")
-        total_and_one = keep.tile([P, B], F32, name="total_and_one")
-        recip = keep.tile([P, B], F32, name="recip")
+        v_tab = [[keep.tile([P, (b + 1) * SEG], F32, name="v_tab%d%d" % (b, h)) for h in range(2)] for b in range(B)]
+        wide = NQ + DV
+        second_codes = [keep.tile([P, wide], U32, name="second_codes%d" % b, align_bytes=64) for b in range(B)]
+        second_scales = [keep.tile([P, wide], U8, name="second_scales%d" % b, align_bytes=64) for b in range(B)]
+        squares = [keep.tile([P, N], F32, name="squares%d" % b, align_bytes=64) for b in range(B)]
+        total = [keep.tile([P, 2], F32, name="total%d" % b) for b in range(B)]
+        total_and_one = [keep.tile([P, 1], F32, name="total_and_one%d" % b) for b in range(B)]
+        recip = [keep.tile([P, 1], F32, name="recip%d" % b) for b in range(B)]
         y_sb = [keep.tile([P, DV], F32, name="y_sb%d" % b) for b in range(B)]
+
+        shared = ctx.enter_context(tc.tile_pool(name="shared", bufs=1))
+        work = shared.tile([P, 20 * P], F32, name="work", offset=0, align_bytes=64)
+
+        def blocks(a0, a1):
+            return work[:, a0 * P : a1 * P]
+
+        planes = [blocks(4, 20), blocks(0, 16)]
+        positive = [[blocks(14, 18)], None]
+        v_got = [[None, None], [None, None]]
+        scale_cols = [None]
+        w_in = [None, None]
+
+        def later(name, kib, shape, dtype):
+            return shared.tile(shape, dtype, name=name, offset=kib * 512, align_bytes=64)
+
         key_rows = kT.rearrange("(p j) n -> p j n", j=PACK)
-        value_rows = vT.rearrange("(h p) n -> p h n", h=2)
 
-        def listed(b):
-            return offsets[:, b * (N // LIST_ROWS) : (b + 1) * (N // LIST_ROWS)]
+        def gather(on_scalar, target, window, b, n0, n1):
+            first = (b * N + n0) // LIST_ROWS
+            picked = window.indirect(offsets[:, first : first + (n1 - n0) // LIST_ROWS])
+            if on_scalar:
+                nc.scalar.activation(target, picked, COPY)
+            else:
+                nc.vector.tensor_copy(target, picked)
 
-        def words(pairs):
-            return pairs[:].bitcast(U32)
+        def gather_keys(on_scalar, b, t, n0=0, n1=N):
+            gather(on_scalar, planes[b][:, t * N + n0 : t * N + n1], k_tab[t][:, 0 : (b + 1) * SEG], b, n0, n1)
 
-        def cast_views(pairs, first, raw, a0, a1):
-            target = pairs[:, 2 * (first + a0) : 2 * (first + a1)].rearrange("p (n e) -> p n e", e=2)
-            return target, raw[:, :, a0:a1].rearrange("p e n -> p n e")
-
-        def share_cast(pairs, first, raw, cut, width):
-            nc.scalar.activation(*cast_views(pairs, first, raw, 0, cut), COPY)
-            nc.vector.tensor_copy(*cast_views(pairs, first, raw, cut, width))
-
-        def scalar_cast(pairs, first, raw):
-            nc.scalar.activation(*cast_views(pairs, first, raw, 0, CHUNK), COPY)
+        def gather_values(on_scalar, b, h, n0=0, n1=N):
+            gather(on_scalar, v_got[b][h][:, n0:n1], v_tab[b][h][:], b, n0, n1)
 
         def quantize(codes, scales, source):
             nc.vector.quantize_mx(out=codes.bitcast(FP8X4), scales=scales, in_=source)
 
-        def turn(tag, count, source):
-            turned = psum.tile([P, PACK, P], F32, name=tag)
-            for t in range(count):
-                nc.tensor.transpose(turned[:, t, :], source(t), ident[:])
-            return turned
-
-        def gather_keys(b, u, n0, n1):
-            entries = listed(b)[:, n0 // LIST_ROWS : n1 // LIST_ROWS]
-            nc.vector.tensor_copy(k_got[b][:, u, n0:n1], words(k_pairs[u])[:, 0 : (b + 1) * SEG].indirect(entries))
-
         def finish_keys(b):
-            halves = [(0, N // 2), (N // 2, N)]
-            for n0, n1 in halves:
-                gather_keys(b, 1, n0, n1)
-            for n0, n1 in halves:
-                nc.vector.tensor_copy(k_in[b][:, n0:n1, :], k_got[b][:, :, n0:n1].rearrange("p u n -> p n u"))
-            for n0, n1 in halves:
-                laid = k_in[b][:, n0:n1, :].rearrange("p n u -> p (n u)").bitcast(BF16)
-                quantize(k_codes[b][:, n0:n1], k_scales[b][:, n0:n1], laid)
+            laid = k_in[b][:].rearrange("p (r s t) -> p s t r", r=PACK, t=PACK)
+            rows = planes[b].rearrange("p (t s r) -> p s t r", t=PACK, r=PACK)
+            for r0 in (0, 2):
+                nc.vector.tensor_copy(laid[:, :, :, r0 : r0 + 2], rows[:, :, :, r0 : r0 + 2])
+            for n0 in (0, N // 2):
+                n1 = n0 + N // 2
+                quantize(k_codes[b][:, n0:n1], k_scales[b][:, n0:n1], k_in[b][:, n0 * PACK : n1 * PACK])
 
-        def product(tag, width, left_codes, left_scales, right_codes, right_scales):
-            sums = psum.tile([P, width], F32, name=tag)
+        def product(sums, left_codes, left_scales, right_codes, right_scales):
             nc.tensor.matmul_mx(
-                out=sums[:],
+                out=sums,
                 lhsT=left_codes.bitcast(FP8X4),
                 lhsT_scale=left_scales,
                 rhs=right_codes.bitcast(FP8X4),
@@ -118,123 +108,147 @@ def tile_attend_relu2_seg_kernel(tc, qT, kT, vT, vs, offs, out):
                 start=True,
                 stop=True,
             )
-            return sums
 
-        def weigh(b, target, turned_squares, scale_cols):
-            spread = scale_cols[:, b * PACK : (b + 1) * PACK].unsqueeze(1).to_broadcast([P, NQ, PACK])
-            nc.vector.tensor_tensor(target, turned_squares[:].rearrange("s t q -> s q t"), spread, MULT)
+        def score(b):
+            parts = b + 1
+            width = N // parts
+            banks = []
+            for i in range(parts):
+                sums = psum.tile([P, width], F32, name="product%d" % i)
+                cols = slice(i * width, (i + 1) * width)
+                product(sums[:], q_codes[:, b * NQ : (b + 1) * NQ], q_scales[:, b * NQ : (b + 1) * NQ], k_codes[b][:, cols], k_scales[b][:, cols])
+                banks.append(sums)
+            return banks
 
-        def gather_values0(h):
-            nc.vector.tensor_copy(v0_got[h][:], v0_raw[h][:].indirect(listed(0)))
+        def relu(b, banks):
+            for i, sums in enumerate(banks):
+                nc.scalar.activation(positive[b][i], sums[:], RELU)
 
-        def turn_values0(h):
-            return turn("shared_turn", 2, lambda u: v0_got[h][:].bitcast(F32)[:, u : N // 2 : 2])
+        def square_and_turn(b, banks):
+            width = N // len(banks)
+            for i in range(len(banks)):
+                cols = slice(i * width, (i + 1) * width)
+                nc.scalar.activation(squares[b][:, cols], positive[b][i], SQUARE, accum_out=total[b][:, i : i + 1])
+            turned = psum.tile([P, PACK, P], F32, name="turn_p%d" % b)
+            for t in range(PACK):
+                nc.tensor.transpose(turned[:, t, :], squares[b][:, t * P : (t + 1) * P], ident[:])
+            return turned
 
-        def settle_values0(target, turned):
-            pairs = target.rearrange("s e t -> s (e t)").bitcast(F32)
-            nc.scalar.copy(pairs.rearrange("s (e u) -> s e u", u=2), turned[:, 0:2, :].rearrange("s u e -> s e u"))
+        def weigh(b, turned):
+            target = w_in[b].rearrange("s (q t) -> s q t", t=PACK)
+            spread = scale_cols[0][:, b * PACK : (b + 1) * PACK].unsqueeze(1).to_broadcast([P, NQ, PACK])
+            nc.vector.tensor_tensor(target, turned[:].rearrange("s t q -> s q t"), spread, MULT)
+
+        def turn_values(b, h, turned):
+            for u in range(2):
+                nc.tensor.transpose(turned[:, u, :], v_got[b][h][:].bitcast(F32)[:, u : N // 2 : 2], ident[:])
+
+        def finish(b, queue):
+            sums = psum.tile([P, DV], F32, name="product%d" % b)
+            product(
+                sums[:],
+                second_codes[b][:, DV:wide], second_scales[b][:, DV:wide],
+                second_codes[b][:, 0:DV], second_scales[b][:, 0:DV],
+            )
+            nc.scalar.activation(y_sb[b][:], sums[:], COPY, scale=recip[b][:])
+            queue.dma_start(out[b], y_sb[b][:])
 
         nc.vector.memset(vs_tab[0 : P - 1, :], 0.0)
         nc.sync.dma_start(offsets[:], offs)
         nc.sync.dma_start(vs_tab[P - 1 : P, :], vs[0:1, :])
         make_identity(nc, ident[:])
-        nc.gpsimd.memset(words(v1_pairs)[:, 0:SEG], 0)
-
-        for c in range(2):
-            nc.sync.dma_start(first_raw[c][:], key_rows[:, 0:2, c * CHUNK : (c + 1) * CHUNK])
-        nc.sync.dma_start(second_raw[:], key_rows[:, 2:4, 0:SEG])
-        for u in range(2):
-            for c in range(2):
-                a0 = SEG + c * CHUNK
-                nc.sync.dma_start(k1_raw[u][c][:], key_rows[:, 2 * u : 2 * u + 2, a0 : a0 + CHUNK])
-        nc.sync.dma_start(q_raw[:], qT.rearrange("b (p j) q -> p b (j q)", j=PACK))
-        for c in range(2):
-            a0 = SEG + c * CHUNK
-            nc.sync.dma_start(v1_raw[c][:], value_rows[:, :, a0 : a0 + CHUNK])
         for h in range(2):
-            nc.sync.dma_start(v0_raw[h][:], vT[h * P : (h + 1) * P, 0:SEG])
+            nc.gpsimd.memset(v_tab[1][h][:, 0:SEG], 0.0)
 
-        nc.vector.tensor_copy(vs_got[:], vs_tab[:].indirect(offsets[:]))
-        turned_scales = psum.tile([P, PACK, P], F32, name="shared_turn")
+        for t in range(PACK):
+            nc.sync.dma_start(k_tab[t][:, 0:SEG], key_rows[:, t, 0:SEG])
+        nc.sync.dma_start(q_raw[:], qT.rearrange("b (p j) q -> p b (j q)", j=PACK))
+        for t in range(PACK):
+            nc.sync.dma_start(k_tab[t][:, SEG:T], key_rows[:, t, SEG:T])
+        for b in range(B):
+            for h in range(2):
+                nc.sync.dma_start(v_tab[b][h][:, b * SEG : (b + 1) * SEG], vT[h * P : (h + 1) * P, b * SEG : (b + 1) * SEG])
+
+        gather(False, vs_got[:, 0:N].rearrange("p (t s) -> p s t", t=PACK), vs_tab[:], 0, 0, N)
+        gather(True, vs_got[:, N : B * N], vs_tab[:], 1, 0, N)
+        turned_scales = psum.tile([P, PACK, P], F32, name="turn_scales")
         turned_flat = turned_scales[:].rearrange("s t e -> s (t e)")
         for k in reversed(range(B * PACK)):
             b, t = divmod(k, PACK)
-            nc.tensor.transpose(turned_flat[:, 2 * k : 2 * k + P], vs_got[:, b * N + t : (b + 1) * N : PACK], ident[:])
+            source = vs_got[:, N + t : B * N : PACK] if b else vs_got[:, t * P : (t + 1) * P]
+            nc.tensor.transpose(turned_flat[:, 2 * k : 2 * k + P], source, ident[:])
 
-        scalar_cast(k_pairs[0], 0, first_raw[0])
-        share_cast(k_pairs[0], CHUNK, first_raw[1], CHUNK // 4, CHUNK)
-        gather_keys(0, 0, 0, N)
-        share_cast(k_pairs[1], 0, second_raw, SEG // 2, SEG)
-        scale_cols = keep.tile([P, B * PACK], F32, name="second_raw")
-        nc.vector.tensor_copy(scale_cols[:], turned_flat[:, P - 1 : P - 1 + 2 * B * PACK : 2])
-        finish_keys(0)
-
-        for c in range(2):
-            scalar_cast(k_pairs[0], SEG + c * CHUNK, k1_raw[0][c])
-        gather_keys(1, 0, 0, N)
-        for c in range(2):
-            scalar_cast(k_pairs[1], SEG + c * CHUNK, k1_raw[1][c])
-        nc.scalar.activation(q_in[:], q_raw[:].rearrange("p b (j q) -> p b q j", j=PACK), COPY)
-        finish_keys(1)
-        quantize(q_codes[:], q_scales[:], q_in[:].rearrange("p b q j -> p (b q j)"))
-
-        order = (1, 0)
-        scores = {}
-        for b in order:
-            queries = slice(b * NQ, (b + 1) * NQ)
-            scores[b] = product(
-                "product%d" % b, N, q_codes[:, queries], q_scales[:, queries], k_codes[b][:], k_scales[b][:]
-            )
-
-        for c in range(2):
-            scalar_cast(v1_pairs, SEG + c * CHUNK, v1_raw[c])
-
-        positive = keep.tile([P, B, N], F32, name="v1_raw1", align_bytes=64)
-        for b in order:
-            nc.scalar.activation(
-                positive[:, b, :].rearrange("q (t s) -> q t s", t=PACK),
-                scores[b][:].rearrange("q (s t) -> q t s", t=PACK),
-                RELU,
-            )
-        turned_squares = {}
-        for b in order:
-            nc.scalar.activation(squares[b][:], positive[:, b, :], SQUARE, accum_out=total[:, b : b + 1])
-            turned_squares[b] = turn("turn_p%d" % b, PACK, lambda t: squares[b][:, t * P : (t + 1) * P])
-
-        nc.vector.tensor_copy(v1_got[:].rearrange("p t s -> p s t"), words(v1_pairs).indirect(listed(1)))
-        turned_v1 = turn("turn_v1", PACK, lambda t: v1_got[:, t, :].bitcast(F32))
-
-        gather_values0(0)
-        turned_v0 = turn_values0(0)
-        gather_values0(1)
-        early_flat = keep.tile([P, early * PACK], BF16, name="v1_raw1", align_bytes=64)
-        late_flat = keep.tile([P, (HALF + NQ) * PACK], BF16, name="late_flat", align_bytes=64)
-        early_in = early_flat[:].rearrange("s (c t) -> s c t", t=PACK)
-        late_in = late_flat[:].rearrange("s (c t) -> s c t", t=PACK)
-        settle_values0(early_in[:, v_at[0] : v_at[0] + HALF, :], turned_v0)
-        turned_v0 = turn_values0(1)
-        v1_halves = turned_v1[:].rearrange("s t p -> s (t p)").bitcast(BF16)
-        nc.scalar.copy(
-            early_in[:, v_at[1] : v_at[1] + DV, :].rearrange("s (h p) t -> s h p t", h=2),
-            v1_halves.rearrange("s (t p h) -> s h p t", t=PACK, h=2),
+        gather_keys(False, 0, 0)
+        gather_keys(True, 0, 1)
+        gather_keys(False, 0, 2)
+        gather_keys(False, 0, 3, 0, N // 2)
+        gather_keys(True, 0, 3, N // 2, N)
+        nc.scalar.activation(
+            q_in[:].rearrange("p (b q j) -> p b q j", b=B, j=PACK),
+            q_raw[:].rearrange("p b (j q) -> p b q j", j=PACK),
+            COPY,
         )
-        settle_values0(late_in[:, 0:HALF, :], turned_v0)
-        nc.scalar.activation(total_and_one[:], total[:], IDENTITY, bias=1.0)
+        finish_keys(0)
+        quantize(q_codes[:], q_scales[:], q_in[:])
+        scores0 = score(0)
+        scale_cols[0] = keep.tile([P, B * PACK], F32, name="k_in0", align_bytes=64)
+        nc.vector.tensor_copy(scale_cols[0][:], turned_flat[:, P - 1 : P - 1 + 2 * B * PACK : 2])
+        gather_keys(True, 1, 0)
+        gather_keys(True, 1, 1, 0, N // 2)
+        gather_keys(False, 1, 1, N // 2, N)
+        relu(0, scores0)
+        turned0 = square_and_turn(0, scores0)
+        gather_keys(False, 1, 2)
+        gather_keys(False, 1, 3, 0, N // 2)
+        gather_keys(True, 1, 3, N // 2, N)
+        nc.scalar.activation(total_and_one[0][:], total[0][:, 0:1], IDENTITY, bias=1.0)
+        finish_keys(1)
+        scores1 = score(1)
+        w0_in = later("w0_in", 0, [P, NQ * PACK], BF16)
+        w_in[0] = w0_in[:]
+        v_got[0][0] = keep.tile([P, N], BF16, name="squares0", align_bytes=64)
+        for b, h, kib in ((0, 1, 15), (1, 0, 17)):
+            v_got[b][h] = later("v_got%d%d" % (b, h), kib, [P, N], BF16)
+        gather_values(True, 0, 0)
+        gather_values(True, 0, 1, 0, N // 2)
+        gather_values(False, 0, 1, N // 2, N)
+        weigh(0, turned0)
+        nc.vector.reciprocal(recip[0][:], total_and_one[0][:])
+        turned_v = {}
+        turned_v[0, 0] = psum.tile([P, 2, P], F32, name="turn_v0")
+        turn_values(0, 0, turned_v[0, 0])
+        positive1 = later("positive1", 8, [P, N], F32)
+        positive[1] = [positive1[:, 0 : N // 2], positive1[:, N // 2 : N]]
+        relu(1, scores1)
+        turned_v[0, 1] = psum.tile([P, 2, P], F32, name="product0")
+        turn_values(0, 1, turned_v[0, 1])
+        turned1 = square_and_turn(1, scores1)
+        gather_values(False, 1, 0)
+        quantize(second_codes[0][:, DV:wide], second_scales[0][:, DV:wide], w_in[0])
+        v_got[1][1] = later("v_got11", 9, [P, N], BF16)
+        gather_values(False, 1, 1, 0, N // 2)
+        gather_values(True, 1, 1, N // 2, N)
+        v0_in = later("v0_in", 11, [P, DV * PACK], BF16)
+        v1_in = later("v1_in", 5, [P, DV * PACK], BF16)
+        w1_in = later("w1_in", 2, [P, NQ * PACK], BF16)
+        w_in[1] = w1_in[:]
+        v_in = [v0_in[:], v1_in[:]]
 
-        weigh(1, early_in[:, w_at[1] : w_at[1] + NQ, :], turned_squares[1], scale_cols)
-        weigh(0, late_in[:, HALF : HALF + NQ, :], turned_squares[0], scale_cols)
-        nc.vector.reciprocal(recip[:], total_and_one[:])
-        quantize(second_codes[:, 0:early], second_scales[:, 0:early], early_flat[:])
-        late = slice(early, B * (NQ + DV))
-        quantize(second_codes[:, late], second_scales[:, late], late_flat[:])
+        def settle(b, h):
+            pairs = v_in[b][:, h * HALF * PACK : (h + 1) * HALF * PACK].bitcast(F32)
+            nc.scalar.copy(pairs.rearrange("s (e u) -> s e u", u=2), turned_v[b, h][:].rearrange("s u e -> s e u"))
 
-        sums = {}
-        for b in order:
-            w_cols, v_cols = slice(w_at[b], w_at[b] + NQ), slice(v_at[b], v_at[b] + DV)
-            sums[b] = product(
-                "product%d" % b, DV,
-                second_codes[:, w_cols], second_scales[:, w_cols], second_codes[:, v_cols], second_scales[:, v_cols],
-            )
-        for b, queue in zip(order, (nc.sync, nc.scalar)):
-            nc.scalar.activation(y_sb[b][:], sums[b][:], COPY, scale=recip[:, b : b + 1])
-            queue.dma_start(out[b], y_sb[b][:])
+        settle(0, 0)
+        settle(0, 1)
+        nc.vector.scalar_tensor_tensor(total_and_one[1][:], total[1][:, 0:1], 1.0, total[1][:, 1:2], ADD, ADD)
+        weigh(1, turned1)
+        nc.vector.reciprocal(recip[1][:], total_and_one[1][:])
+        quantize(second_codes[0][:, 0:DV], second_scales[0][:, 0:DV], v_in[0])
+        for h, tag in enumerate(("turn_v1", "turn_scales")):
+            turned_v[1, h] = psum.tile([P, 2, P], F32, name=tag)
+            turn_values(1, h, turned_v[1, h])
+            settle(1, h)
+        quantize(second_codes[1][:, DV:wide], second_scales[1][:, DV:wide], w_in[1])
+        finish(0, nc.sync)
+        quantize(second_codes[1][:, 0:DV], second_scales[1][:, 0:DV], v_in[1])
+        finish(1, nc.scalar)

@@ -45,24 +45,25 @@ def tile_attend_relu2_seg_kernel(tc, qT, kT, vT, vs, offs, out):
         k_in = [keep.tile([P, N * PACK], BF16, name="k_in%d" % b, align_bytes=64) for b in range(B)]
         k_codes = [keep.tile([P, N], U32, name="k_codes%d" % b, align_bytes=64) for b in range(B)]
         k_scales = [keep.tile([P, N], U8, name="k_scales%d" % b, align_bytes=64) for b in range(B)]
-        v_tab = [[keep.tile([P, (b + 1) * SEG], F32, name="v_tab%d%d" % (b, h)) for h in range(2)] for b in range(B)]
+        shared = ctx.enter_context(tc.tile_pool(name="shared", bufs=1))
+        v_tab = [[keep.tile([P, (b + 1) * SEG], F32, name="v_tab%d%d" % (b, h)) for h in range(2 - b)] for b in range(B)]
+        v_tab[1].append(shared.tile([P, T], F32, name="v_tab11", offset=0, align_bytes=64))
         wide = NQ + DV
         second_codes = [keep.tile([P, wide], U32, name="second_codes%d" % b, align_bytes=64) for b in range(B)]
         second_scales = [keep.tile([P, wide], U8, name="second_scales%d" % b, align_bytes=64) for b in range(B)]
         squares = [keep.tile([P, N], F32, name="squares%d" % b, align_bytes=64) for b in range(B)]
         total = [keep.tile([P, 2], F32, name="total%d" % b) for b in range(B)]
-        total_and_one = [keep.tile([P, 1], F32, name="total_and_one%d" % b) for b in range(B)]
+        total_and_one = [None, None]
         recip = [keep.tile([P, 1], F32, name="recip%d" % b) for b in range(B)]
         y_sb = [keep.tile([P, DV], F32, name="y_sb%d" % b) for b in range(B)]
 
-        shared = ctx.enter_context(tc.tile_pool(name="shared", bufs=1))
-        work = shared.tile([P, 20 * P], F32, name="work", offset=0, align_bytes=64)
+        work = keep.tile([P, 20 * P], F32, name="work", align_bytes=64)
 
         def blocks(a0, a1):
             return work[:, a0 * P : a1 * P]
 
         planes = [blocks(4, 20), blocks(0, 16)]
-        positive = [[blocks(14, 18)], None]
+        positive = [None, None]
         v_got = [[None, None], [None, None]]
         scale_cols = [None]
         w_in = [None, None]
@@ -141,7 +142,7 @@ def tile_attend_relu2_seg_kernel(tc, qT, kT, vT, vs, offs, out):
 
         def turn_values(b, h, turned):
             for u in range(2):
-                nc.tensor.transpose(turned[:, u, :], v_got[b][h][:].bitcast(F32)[:, u : N // 2 : 2], ident[:])
+                nc.tensor.transpose(turned[:, u, :], v_got[b][h].bitcast(F32)[:, u : N // 2 : 2], ident[:])
 
         def finish(b, queue):
             sums = psum.tile([P, DV], F32, name="product%d" % b)
@@ -196,59 +197,56 @@ def tile_attend_relu2_seg_kernel(tc, qT, kT, vT, vs, offs, out):
         gather_keys(True, 1, 0)
         gather_keys(True, 1, 1, 0, N // 2)
         gather_keys(False, 1, 1, N // 2, N)
+        positive0 = keep.tile([P, N], F32, name="k_tab1")
+        positive[0] = [positive0[:]]
         relu(0, scores0)
         turned0 = square_and_turn(0, scores0)
         gather_keys(False, 1, 2)
         gather_keys(False, 1, 3, 0, N // 2)
         gather_keys(True, 1, 3, N // 2, N)
+        total_and_one[0] = keep.tile([P, 1], F32, name="k_tab3")
         nc.scalar.activation(total_and_one[0][:], total[0][:, 0:1], IDENTITY, bias=1.0)
         finish_keys(1)
         scores1 = score(1)
-        w0_in = later("w0_in", 0, [P, NQ * PACK], BF16)
-        w_in[0] = w0_in[:]
-        v_got[0][0] = keep.tile([P, N], BF16, name="squares0", align_bytes=64)
-        for b, h, kib in ((0, 1, 15), (1, 0, 17)):
-            v_got[b][h] = later("v_got%d%d" % (b, h), kib, [P, N], BF16)
+        for b in range(B):
+            for h in range(2):
+                got = keep.tile([P, N], BF16, name="v_got%d%d" % (b, h), align_bytes=64)
+                v_got[b][h] = got[:]
+        w_in[0] = k_in[1][:, 2 * N : 3 * N]
         gather_values(True, 0, 0)
-        gather_values(True, 0, 1, 0, N // 2)
-        gather_values(False, 0, 1, N // 2, N)
+        gather_values(True, 0, 1)
         weigh(0, turned0)
         nc.vector.reciprocal(recip[0][:], total_and_one[0][:])
-        turned_v = {}
-        turned_v[0, 0] = psum.tile([P, 2, P], F32, name="turn_v0")
-        turn_values(0, 0, turned_v[0, 0])
-        positive1 = later("positive1", 8, [P, N], F32)
+        turned_v0 = psum.tile([P, 2, 2, P], F32, name="turn_v0")
+        for h in range(2):
+            turn_values(0, h, turned_v0[:, h])
+        positive1 = keep.tile([P, N], F32, name="v_tab01")
         positive[1] = [positive1[:, 0 : N // 2], positive1[:, N // 2 : N]]
         relu(1, scores1)
-        turned_v[0, 1] = psum.tile([P, 2, P], F32, name="product0")
-        turn_values(0, 1, turned_v[0, 1])
         turned1 = square_and_turn(1, scores1)
-        gather_values(False, 1, 0)
         quantize(second_codes[0][:, DV:wide], second_scales[0][:, DV:wide], w_in[0])
-        v_got[1][1] = later("v_got11", 9, [P, N], BF16)
-        gather_values(False, 1, 1, 0, N // 2)
-        gather_values(True, 1, 1, N // 2, N)
-        v0_in = later("v0_in", 11, [P, DV * PACK], BF16)
-        v1_in = later("v1_in", 5, [P, DV * PACK], BF16)
-        w1_in = later("w1_in", 2, [P, NQ * PACK], BF16)
+        gather_values(False, 1, 0)
+        cut = 5 * N // 8
+        gather_values(False, 1, 1, 0, cut)
+        gather_values(True, 1, 1, cut, N)
+        v0_in = later("v0_in", 0, [P, DV * PACK], BF16)
+        v1_in = later("v1_in", 4, [P, DV * PACK], BF16)
+        w1_in = later("w1_in", 8, [P, NQ * PACK], BF16)
+        total_and_one[1] = later("total_and_one1", 10, [P, 1], F32)
         w_in[1] = w1_in[:]
-        v_in = [v0_in[:], v1_in[:]]
-
-        def settle(b, h):
-            pairs = v_in[b][:, h * HALF * PACK : (h + 1) * HALF * PACK].bitcast(F32)
-            nc.scalar.copy(pairs.rearrange("s (e u) -> s e u", u=2), turned_v[b, h][:].rearrange("s u e -> s e u"))
-
-        settle(0, 0)
-        settle(0, 1)
+        nc.scalar.copy(
+            v0_in[:].bitcast(F32).rearrange("s (h e u) -> s h e u", h=2, u=2), turned_v0[:].rearrange("s h u e -> s h e u")
+        )
         nc.vector.scalar_tensor_tensor(total_and_one[1][:], total[1][:, 0:1], 1.0, total[1][:, 1:2], ADD, ADD)
         weigh(1, turned1)
         nc.vector.reciprocal(recip[1][:], total_and_one[1][:])
-        quantize(second_codes[0][:, 0:DV], second_scales[0][:, 0:DV], v_in[0])
+        quantize(second_codes[0][:, 0:DV], second_scales[0][:, 0:DV], v0_in[:])
         for h, tag in enumerate(("turn_v1", "turn_scales")):
-            turned_v[1, h] = psum.tile([P, 2, P], F32, name=tag)
-            turn_values(1, h, turned_v[1, h])
-            settle(1, h)
+            turned = psum.tile([P, 2, P], F32, name=tag)
+            turn_values(1, h, turned)
+            pairs = v1_in[:, h * HALF * PACK : (h + 1) * HALF * PACK].bitcast(F32)
+            nc.scalar.copy(pairs.rearrange("s (e u) -> s e u", u=2), turned[:].rearrange("s u e -> s e u"))
         quantize(second_codes[1][:, DV:wide], second_scales[1][:, DV:wide], w_in[1])
         finish(0, nc.sync)
-        quantize(second_codes[1][:, 0:DV], second_scales[1][:, 0:DV], v_in[1])
+        quantize(second_codes[1][:, 0:DV], second_scales[1][:, 0:DV], v1_in[:])
         finish(1, nc.scalar)

@@ -17,7 +17,6 @@ U16 = mybir.dt.uint16
 U8 = mybir.dt.uint8
 FP8X4 = mybir.dt.float8_e4m3fn_x4
 COPY = mybir.ActivationFunctionType.Copy
-IDENTITY = mybir.ActivationFunctionType.Identity
 RELU = mybir.ActivationFunctionType.Relu
 SQUARE = mybir.ActivationFunctionType.Square
 MULT = mybir.AluOpType.mult
@@ -41,7 +40,9 @@ def tile_attend_relu2_seg_kernel(tc, qT, kT, vT, vs, offs, out):
         q_in = keep.tile([P, B * NQ * PACK], BF16, name="q_in", align_bytes=64)
         q_codes = keep.tile([P, B * NQ], U32, name="q_codes", align_bytes=64)
         q_scales = keep.tile([P, B * NQ], U8, name="q_scales", align_bytes=64)
-        k_tab = [keep.tile([P, T], F32, name="k_tab%d" % t) for t in range(PACK)]
+        first_two = keep.tile([P, 2 * T], F32, name="k_tab1")
+        k_tab = [first_two[:, 0:T], first_two[:, T : 2 * T]]
+        k_tab += [keep.tile([P, T], F32, name="k_tab%d" % t)[:] for t in (2, 3)]
         k_in = [keep.tile([P, N * PACK], BF16, name="k_in%d" % b, align_bytes=64) for b in range(B)]
         k_codes = [keep.tile([P, N], U32, name="k_codes%d" % b, align_bytes=64) for b in range(B)]
         k_scales = [keep.tile([P, N], U8, name="k_scales%d" % b, align_bytes=64) for b in range(B)]
@@ -49,12 +50,12 @@ def tile_attend_relu2_seg_kernel(tc, qT, kT, vT, vs, offs, out):
         v_tab = [[keep.tile([P, (b + 1) * SEG], F32, name="v_tab%d%d" % (b, h)) for h in range(2 - b)] for b in range(B)]
         v_tab[1].append(shared.tile([P, T], F32, name="v_tab11", offset=0, align_bytes=64))
         wide = NQ + DV
-        second_codes = [keep.tile([P, wide], U32, name="second_codes%d" % b, align_bytes=64) for b in range(B)]
+        second_codes = [None, keep.tile([P, wide], U32, name="second_codes1", align_bytes=64)]
         second_scales = [keep.tile([P, wide], U8, name="second_scales%d" % b, align_bytes=64) for b in range(B)]
-        squares = [keep.tile([P, N], F32, name="squares%d" % b, align_bytes=64) for b in range(B)]
+        squares0 = keep.tile([P, N], F32, name="squares0")
+        squares = [[squares0[:]], None]
         total = [keep.tile([P, 2], F32, name="total%d" % b) for b in range(B)]
-        total_and_one = [None, None]
-        recip = [keep.tile([P, 1], F32, name="recip%d" % b) for b in range(B)]
+        recip = keep.tile([P, B], F32, name="recip")
         y_sb = [keep.tile([P, DV], F32, name="y_sb%d" % b) for b in range(B)]
 
         work = keep.tile([P, 20 * P], F32, name="work", align_bytes=64)
@@ -128,11 +129,11 @@ def tile_attend_relu2_seg_kernel(tc, qT, kT, vT, vs, offs, out):
         def square_and_turn(b, banks):
             width = N // len(banks)
             for i in range(len(banks)):
-                cols = slice(i * width, (i + 1) * width)
-                nc.scalar.activation(squares[b][:, cols], positive[b][i], SQUARE, accum_out=total[b][:, i : i + 1])
+                nc.scalar.activation(squares[b][i], positive[b][i], SQUARE, accum_out=total[b][:, i : i + 1])
             turned = psum.tile([P, PACK, P], F32, name="turn_p%d" % b)
             for t in range(PACK):
-                nc.tensor.transpose(turned[:, t, :], squares[b][:, t * P : (t + 1) * P], ident[:])
+                i, first = divmod(t * P, width)
+                nc.tensor.transpose(turned[:, t, :], squares[b][i][:, first : first + P], ident[:])
             return turned
 
         def weigh(b, turned):
@@ -144,15 +145,14 @@ def tile_attend_relu2_seg_kernel(tc, qT, kT, vT, vs, offs, out):
             for u in range(2):
                 nc.tensor.transpose(turned[:, u, :], v_got[b][h].bitcast(F32)[:, u : N // 2 : 2], ident[:])
 
-        def finish(b, queue):
-            sums = psum.tile([P, DV], F32, name="product%d" % b)
+        def finish(b, e0, e1, tag):
+            sums = psum.tile([P, e1 - e0], F32, name=tag)
             product(
                 sums[:],
                 second_codes[b][:, DV:wide], second_scales[b][:, DV:wide],
-                second_codes[b][:, 0:DV], second_scales[b][:, 0:DV],
+                second_codes[b][:, e0:e1], second_scales[b][:, e0:e1],
             )
-            nc.scalar.activation(y_sb[b][:], sums[:], COPY, scale=recip[b][:])
-            queue.dma_start(out[b], y_sb[b][:])
+            nc.scalar.activation(y_sb[b][:, e0:e1], sums[:], COPY, scale=recip[:, b : b + 1])
 
         nc.vector.memset(vs_tab[0 : P - 1, :], 0.0)
         nc.sync.dma_start(offsets[:], offs)
@@ -161,7 +161,8 @@ def tile_attend_relu2_seg_kernel(tc, qT, kT, vT, vs, offs, out):
         for h in range(2):
             nc.gpsimd.memset(v_tab[1][h][:, 0:SEG], 0.0)
 
-        for t in range(PACK):
+        nc.sync.dma_start(first_two[:].rearrange("p (t n) -> p t n", t=2)[:, :, 0:SEG], key_rows[:, 0:2, 0:SEG])
+        for t in (2, 3):
             nc.sync.dma_start(k_tab[t][:, 0:SEG], key_rows[:, t, 0:SEG])
         nc.sync.dma_start(q_raw[:], qT.rearrange("b (p j) q -> p b (j q)", j=PACK))
         for t in range(PACK):
@@ -171,7 +172,8 @@ def tile_attend_relu2_seg_kernel(tc, qT, kT, vT, vs, offs, out):
                 nc.sync.dma_start(v_tab[b][h][:, b * SEG : (b + 1) * SEG], vT[h * P : (h + 1) * P, b * SEG : (b + 1) * SEG])
 
         gather(False, vs_got[:, 0:N].rearrange("p (t s) -> p s t", t=PACK), vs_tab[:], 0, 0, N)
-        gather(True, vs_got[:, N : B * N], vs_tab[:], 1, 0, N)
+        gather(False, vs_got[:, N : N + N // 2], vs_tab[:], 1, 0, N // 2)
+        gather(True, vs_got[:, N + N // 2 : B * N], vs_tab[:], 1, N // 2, N)
         turned_scales = psum.tile([P, PACK, P], F32, name="turn_scales")
         turned_flat = turned_scales[:].rearrange("s t e -> s (t e)")
         for k in reversed(range(B * PACK)):
@@ -181,7 +183,8 @@ def tile_attend_relu2_seg_kernel(tc, qT, kT, vT, vs, offs, out):
 
         gather_keys(False, 0, 0)
         gather_keys(True, 0, 1)
-        gather_keys(False, 0, 2)
+        gather_keys(False, 0, 2, 0, N // 2)
+        gather_keys(True, 0, 2, N // 2, N)
         gather_keys(False, 0, 3, 0, N // 2)
         gather_keys(True, 0, 3, N // 2, N)
         nc.scalar.activation(
@@ -204,8 +207,6 @@ def tile_attend_relu2_seg_kernel(tc, qT, kT, vT, vs, offs, out):
         gather_keys(False, 1, 2)
         gather_keys(False, 1, 3, 0, N // 2)
         gather_keys(True, 1, 3, N // 2, N)
-        total_and_one[0] = keep.tile([P, 1], F32, name="k_tab3")
-        nc.scalar.activation(total_and_one[0][:], total[0][:, 0:1], IDENTITY, bias=1.0)
         finish_keys(1)
         scores1 = score(1)
         for b in range(B):
@@ -216,30 +217,33 @@ def tile_attend_relu2_seg_kernel(tc, qT, kT, vT, vs, offs, out):
         gather_values(True, 0, 0)
         gather_values(True, 0, 1)
         weigh(0, turned0)
-        nc.vector.reciprocal(recip[0][:], total_and_one[0][:])
         turned_v0 = psum.tile([P, 2, 2, P], F32, name="turn_v0")
         for h in range(2):
             turn_values(0, h, turned_v0[:, h])
         positive1 = keep.tile([P, N], F32, name="v_tab01")
         positive[1] = [positive1[:, 0 : N // 2], positive1[:, N // 2 : N]]
         relu(1, scores1)
-        turned1 = square_and_turn(1, scores1)
-        quantize(second_codes[0][:, DV:wide], second_scales[0][:, DV:wide], w_in[0])
         gather_values(False, 1, 0)
-        cut = 5 * N // 8
+        halves = [keep.tile([P, N // 2], F32, name=tag) for tag in ("squares1", "v_tab10")]
+        squares[1] = [half[:] for half in halves]
+        turned1 = square_and_turn(1, scores1)
+        cut = 3 * N // 4
         gather_values(False, 1, 1, 0, cut)
         gather_values(True, 1, 1, cut, N)
+        second_codes[0] = later("codes0", 11, [P, wide], U32)
+        quantize(second_codes[0][:, DV:wide], second_scales[0][:, DV:wide], w_in[0])
         v0_in = later("v0_in", 0, [P, DV * PACK], BF16)
         v1_in = later("v1_in", 4, [P, DV * PACK], BF16)
         w1_in = later("w1_in", 8, [P, NQ * PACK], BF16)
-        total_and_one[1] = later("total_and_one1", 10, [P, 1], F32)
+        total_and_one = later("total_and_one", 10, [P, B], F32)
         w_in[1] = w1_in[:]
         nc.scalar.copy(
             v0_in[:].bitcast(F32).rearrange("s (h e u) -> s h e u", h=2, u=2), turned_v0[:].rearrange("s h u e -> s h e u")
         )
-        nc.vector.scalar_tensor_tensor(total_and_one[1][:], total[1][:, 0:1], 1.0, total[1][:, 1:2], ADD, ADD)
+        nc.vector.tensor_scalar_add(total_and_one[:, 0:1], total[0][:, 0:1], 1.0)
+        nc.vector.scalar_tensor_tensor(total_and_one[:, 1:2], total[1][:, 0:1], 1.0, total[1][:, 1:2], ADD, ADD)
         weigh(1, turned1)
-        nc.vector.reciprocal(recip[1][:], total_and_one[1][:])
+        nc.vector.reciprocal(recip[:], total_and_one[:])
         quantize(second_codes[0][:, 0:DV], second_scales[0][:, 0:DV], v0_in[:])
         for h, tag in enumerate(("turn_v1", "turn_scales")):
             turned = psum.tile([P, 2, P], F32, name=tag)
@@ -247,6 +251,10 @@ def tile_attend_relu2_seg_kernel(tc, qT, kT, vT, vs, offs, out):
             pairs = v1_in[:, h * HALF * PACK : (h + 1) * HALF * PACK].bitcast(F32)
             nc.scalar.copy(pairs.rearrange("s (e u) -> s e u", u=2), turned[:].rearrange("s u e -> s e u"))
         quantize(second_codes[1][:, DV:wide], second_scales[1][:, DV:wide], w_in[1])
-        finish(0, nc.sync)
-        quantize(second_codes[1][:, 0:DV], second_scales[1][:, 0:DV], v1_in[:])
-        finish(1, nc.scalar)
+        finish(0, 0, DV, "product0")
+        nc.sync.dma_start(out[0], y_sb[0][:])
+        for h, tag in enumerate(("product1", "turn_p0")):
+            cols = slice(h * HALF, (h + 1) * HALF)
+            quantize(second_codes[1][:, cols], second_scales[1][:, cols], v1_in[:, h * HALF * PACK : (h + 1) * HALF * PACK])
+            finish(1, h * HALF, (h + 1) * HALF, tag)
+        nc.scalar.dma_start(out[1], y_sb[1][:])

@@ -143,7 +143,9 @@ def tile_attend_relu2_seg_kernel(tc, qT, kT, vT, vs, offs, out):
 
         def turn_values(b, h, turned):
             for u in range(2):
-                nc.tensor.transpose(turned[:, u, :], v_got[b][h].bitcast(F32)[:, u : N // 2 : 2], ident[:])
+                words = v_got[b][h].bitcast(F32)
+                source = words[:, u * P : (u + 1) * P] if (b, h) == (1, 0) else words[:, u : N // 2 : 2]
+                nc.tensor.transpose(turned[:, u, :], source, ident[:])
 
         def finish(b, e0, e1, tag):
             sums = psum.tile([P, e1 - e0], F32, name=tag)
@@ -223,11 +225,12 @@ def tile_attend_relu2_seg_kernel(tc, qT, kT, vT, vs, offs, out):
         positive1 = keep.tile([P, N], F32, name="v_tab01")
         positive[1] = [positive1[:, 0 : N // 2], positive1[:, N // 2 : N]]
         relu(1, scores1)
-        gather_values(False, 1, 0)
-        halves = [keep.tile([P, N // 2], F32, name=tag) for tag in ("squares1", "v_tab10")]
+        dealt = v_got[1][0].rearrange("p (u s e) -> p s u e", u=2, e=2)
+        gather(False, dealt, v_tab[1][0][:], 1, 0, N)
+        halves = [keep.tile([P, N // 2], F32, name=tag) for tag in ("squares1a", "squares1b")]
         squares[1] = [half[:] for half in halves]
         turned1 = square_and_turn(1, scores1)
-        cut = 3 * N // 4
+        cut = 5 * N // 8
         gather_values(False, 1, 1, 0, cut)
         gather_values(True, 1, 1, cut, N)
         second_codes[0] = later("codes0", 11, [P, wide], U32)

@@ -53,8 +53,8 @@ def tile_attend_relu2_seg_kernel(tc, qT, kT, vT, vs, offs, out):
         second_codes = [None, keep.tile([P, wide], U32, name="second_codes1", align_bytes=64)]
         second_scales = [keep.tile([P, wide], U8, name="second_scales%d" % b, align_bytes=64) for b in range(B)]
         squares0 = keep.tile([P, N], F32, name="squares0")
-        squares = [[squares0[:]], None]
-        total = [keep.tile([P, 2], F32, name="total%d" % b) for b in range(B)]
+        squares = [[squares0[:, 0 : N // 2], squares0[:, N // 2 : N]], None]
+        total = keep.tile([P, 2, B], F32, name="total")
         recip = keep.tile([P, B], F32, name="recip")
         y_sb = [keep.tile([P, DV], F32, name="y_sb%d" % b) for b in range(B)]
 
@@ -112,7 +112,7 @@ def tile_attend_relu2_seg_kernel(tc, qT, kT, vT, vs, offs, out):
             )
 
         def score(b):
-            parts = b + 1
+            parts = 2
             width = N // parts
             banks = []
             for i in range(parts):
@@ -129,7 +129,7 @@ def tile_attend_relu2_seg_kernel(tc, qT, kT, vT, vs, offs, out):
         def square_and_turn(b, banks):
             width = N // len(banks)
             for i in range(len(banks)):
-                nc.scalar.activation(squares[b][i], positive[b][i], SQUARE, accum_out=total[b][:, i : i + 1])
+                nc.scalar.activation(squares[b][i], positive[b][i], SQUARE, accum_out=total[:, i, b : b + 1])
             turned = psum.tile([P, PACK, P], F32, name="turn_p%d" % b)
             for t in range(PACK):
                 i, first = divmod(t * P, width)
@@ -200,13 +200,13 @@ def tile_attend_relu2_seg_kernel(tc, qT, kT, vT, vs, offs, out):
         scale_cols[0] = keep.tile([P, B * PACK], F32, name="k_in0", align_bytes=64)
         nc.vector.tensor_copy(scale_cols[0][:], turned_flat[:, P - 1 : P - 1 + 2 * B * PACK : 2])
         gather_keys(True, 1, 0)
-        gather_keys(True, 1, 1, 0, N // 2)
-        gather_keys(False, 1, 1, N // 2, N)
-        positive0 = keep.tile([P, N], F32, name="k_tab1")
-        positive[0] = [positive0[:]]
+        gather_keys(False, 1, 1)
+        positive0 = keep.tile([P, N], F32, name="positive0")
+        positive[0] = [positive0[:, 0 : N // 2], positive0[:, N // 2 : N]]
         relu(0, scores0)
         turned0 = square_and_turn(0, scores0)
-        gather_keys(False, 1, 2)
+        gather_keys(False, 1, 2, 0, 3 * N // 4)
+        gather_keys(True, 1, 2, 3 * N // 4, N)
         gather_keys(False, 1, 3, 0, N // 2)
         gather_keys(True, 1, 3, N // 2, N)
         finish_keys(1)
@@ -243,8 +243,7 @@ def tile_attend_relu2_seg_kernel(tc, qT, kT, vT, vs, offs, out):
         nc.scalar.copy(
             v0_in[:].bitcast(F32).rearrange("s (h e u) -> s h e u", h=2, u=2), turned_v0[:].rearrange("s h u e -> s h e u")
         )
-        nc.vector.tensor_scalar_add(total_and_one[:, 0:1], total[0][:, 0:1], 1.0)
-        nc.vector.scalar_tensor_tensor(total_and_one[:, 1:2], total[1][:, 0:1], 1.0, total[1][:, 1:2], ADD, ADD)
+        nc.vector.scalar_tensor_tensor(total_and_one[:], total[:, 0, :], 1.0, total[:, 1, :], ADD, ADD)
         weigh(1, turned1)
         nc.vector.reciprocal(recip[:], total_and_one[:])
         quantize(second_codes[0][:, 0:DV], second_scales[0][:, 0:DV], v0_in[:])

@@ -157,6 +157,7 @@ def tile_attend_relu2_seg_kernel(tc, qT, kT, vT, vs, offs, out):
             nc.scalar.activation(y_sb[b][:, e0:e1], sums[:], COPY, scale=recip[:, b : b + 1])
 
         nc.vector.memset(vs_tab[0 : P - 1, :], 0.0)
+        nc.vector.memset(total[:, 1, 0:1], 0.0)
         nc.sync.dma_start(offsets[:], offs)
         nc.sync.dma_start(vs_tab[P - 1 : P, :], vs[0:1, :])
         make_identity(nc, ident[:])
@@ -196,29 +197,54 @@ def tile_attend_relu2_seg_kernel(tc, qT, kT, vT, vs, offs, out):
         )
         finish_keys(0)
         quantize(q_codes[:], q_scales[:], q_in[:])
-        scores0 = score(0)
+        scores0 = []
+        for i in range(2):
+            sums = psum.tile([P, 2, NQ], F32, name="product%d" % i)
+            for r in range(2):
+                cols = slice((2 * i + r) * P, (2 * i + r + 1) * P)
+                product(sums[:, r, :], k_codes[0][:, cols], k_scales[0][:, cols], q_codes[:, 0:NQ], q_scales[:, 0:NQ])
+            scores0.append(sums)
         scale_cols[0] = keep.tile([P, B * PACK], F32, name="k_in0", align_bytes=64)
         nc.vector.tensor_copy(scale_cols[0][:], turned_flat[:, P - 1 : P - 1 + 2 * B * PACK : 2])
         gather_keys(True, 1, 0)
         gather_keys(False, 1, 1)
         positive0 = keep.tile([P, N], F32, name="positive0")
         positive[0] = [positive0[:, 0 : N // 2], positive0[:, N // 2 : N]]
-        relu(0, scores0)
-        turned0 = square_and_turn(0, scores0)
+        for i in range(2):
+            nc.scalar.activation(positive[0][i], scores0[i][:].rearrange("s r q -> s (r q)"), RELU)
+        for i in range(2):
+            nc.scalar.activation(squares[0][i], positive[0][i], SQUARE)
+        w0_in = keep.tile([P, NQ * PACK], BF16, name="w0_in", align_bytes=64)
+        spread = scale_cols[0][:, 0:PACK].unsqueeze(1).unsqueeze(3).to_broadcast([P, NQ // PACK, PACK, PACK])
+        nc.gpsimd.tensor_tensor(
+            w0_in[:].rearrange("s (c i t) -> s c t i", i=PACK, t=PACK),
+            squares0[:].rearrange("s (t c i) -> s c t i", t=PACK, i=PACK),
+            spread,
+            MULT,
+        )
+        summed = psum.tile([P, P], F32, name="turn_p0")
+        for t in range(PACK):
+            nc.tensor.matmul(
+                summed[:], squares0[:, t * P : (t + 1) * P], ident[:],
+                start=(t == 0), stop=(t == PACK - 1), is_transpose=True,
+            )
         gather_keys(False, 1, 2, 0, 3 * N // 4)
         gather_keys(True, 1, 2, 3 * N // 4, N)
         gather_keys(False, 1, 3, 0, N // 2)
         gather_keys(True, 1, 3, N // 2, N)
+        by_slot = keep.tile([P, P], F32, name="k_tab3")
+        nc.scalar.activation(by_slot[:], summed[:], COPY, accum_out=total[:, 0, 0:1])
         finish_keys(1)
         scores1 = score(1)
         for b in range(B):
             for h in range(2):
                 got = keep.tile([P, N], BF16, name="v_got%d%d" % (b, h), align_bytes=64)
                 v_got[b][h] = got[:]
-        w_in[0] = k_in[1][:, 2 * N : 3 * N]
+        second_codes[0] = keep.tile([P, wide], U32, name="work", align_bytes=64)
+        quantize(second_codes[0][:, DV:wide], second_scales[0][:, DV:wide], w0_in[:])
         gather_values(True, 0, 0)
-        gather_values(True, 0, 1)
-        weigh(0, turned0)
+        gather_values(False, 0, 1, 0, N // 4)
+        gather_values(True, 0, 1, N // 4, N)
         turned_v0 = psum.tile([P, 2, 2, P], F32, name="turn_v0")
         for h in range(2):
             turn_values(0, h, turned_v0[:, h])
@@ -233,8 +259,6 @@ def tile_attend_relu2_seg_kernel(tc, qT, kT, vT, vs, offs, out):
         cut = 5 * N // 8
         gather_values(False, 1, 1, 0, cut)
         gather_values(True, 1, 1, cut, N)
-        second_codes[0] = later("codes0", 11, [P, wide], U32)
-        quantize(second_codes[0][:, DV:wide], second_scales[0][:, DV:wide], w_in[0])
         v0_in = later("v0_in", 0, [P, DV * PACK], BF16)
         v1_in = later("v1_in", 4, [P, DV * PACK], BF16)
         w1_in = later("w1_in", 8, [P, NQ * PACK], BF16)

@@ -214,14 +214,6 @@ def tile_attend_relu2_seg_kernel(tc, qT, kT, vT, vs, offs, out):
             nc.scalar.activation(positive[0][i], scores0[i][:].rearrange("s r q -> s (r q)"), RELU)
         for i in range(2):
             nc.scalar.activation(squares[0][i], positive[0][i], SQUARE)
-        w0_in = keep.tile([P, NQ * PACK], BF16, name="w0_in", align_bytes=64)
-        spread = scale_cols[0][:, 0:PACK].unsqueeze(1).unsqueeze(3).to_broadcast([P, NQ // PACK, PACK, PACK])
-        nc.gpsimd.tensor_tensor(
-            w0_in[:].rearrange("s (c i t) -> s c t i", i=PACK, t=PACK),
-            squares0[:].rearrange("s (t c i) -> s c t i", t=PACK, i=PACK),
-            spread,
-            MULT,
-        )
         summed = psum.tile([P, P], F32, name="turn_p0")
         for t in range(PACK):
             nc.tensor.matmul(
@@ -240,11 +232,17 @@ def tile_attend_relu2_seg_kernel(tc, qT, kT, vT, vs, offs, out):
             for h in range(2):
                 got = keep.tile([P, N], BF16, name="v_got%d%d" % (b, h), align_bytes=64)
                 v_got[b][h] = got[:]
-        second_codes[0] = keep.tile([P, wide], U32, name="work", align_bytes=64)
-        quantize(second_codes[0][:, DV:wide], second_scales[0][:, DV:wide], w0_in[:])
+        w0_in = k_in[1][:, 2 * N : 3 * N]
+        spread = scale_cols[0][:, 0:PACK].unsqueeze(1).unsqueeze(3).to_broadcast([P, NQ // PACK, PACK, PACK])
+        nc.gpsimd.tensor_tensor(
+            w0_in.rearrange("s (c i t) -> s c t i", i=PACK, t=PACK),
+            squares0[:].rearrange("s (t c i) -> s c t i", t=PACK, i=PACK),
+            spread,
+            MULT,
+        )
         gather_values(True, 0, 0)
-        gather_values(False, 0, 1, 0, N // 4)
-        gather_values(True, 0, 1, N // 4, N)
+        gather_values(False, 0, 1, 0, 3 * N // 8)
+        gather_values(True, 0, 1, 3 * N // 8, N)
         turned_v0 = psum.tile([P, 2, 2, P], F32, name="turn_v0")
         for h in range(2):
             turn_values(0, h, turned_v0[:, h])
@@ -259,6 +257,8 @@ def tile_attend_relu2_seg_kernel(tc, qT, kT, vT, vs, offs, out):
         cut = 5 * N // 8
         gather_values(False, 1, 1, 0, cut)
         gather_values(True, 1, 1, cut, N)
+        second_codes[0] = later("codes0", 11, [P, wide], U32)
+        quantize(second_codes[0][:, DV:wide], second_scales[0][:, DV:wide], w0_in)
         v0_in = later("v0_in", 0, [P, DV * PACK], BF16)
         v1_in = later("v1_in", 4, [P, DV * PACK], BF16)
         w1_in = later("w1_in", 8, [P, NQ * PACK], BF16)

@@ -54,7 +54,7 @@ def tile_attend_relu2_seg_kernel(tc, qT, kT, vT, vs, offs, out):
         second_scales = [keep.tile([P, wide], U8, name="second_scales%d" % b, align_bytes=64) for b in range(B)]
         squares0 = keep.tile([P, N], F32, name="squares0")
         squares = [[squares0[:, 0 : N // 2], squares0[:, N // 2 : N]], None]
-        total = keep.tile([P, 2, B], F32, name="total")
+        total = keep.tile([P, 2], F32, name="total")
         recip = keep.tile([P, B], F32, name="recip")
         y_sb = [keep.tile([P, DV], F32, name="y_sb%d" % b) for b in range(B)]
 
@@ -129,7 +129,7 @@ def tile_attend_relu2_seg_kernel(tc, qT, kT, vT, vs, offs, out):
         def square_and_turn(b, banks):
             width = N // len(banks)
             for i in range(len(banks)):
-                nc.scalar.activation(squares[b][i], positive[b][i], SQUARE, accum_out=total[:, i, b : b + 1])
+                nc.scalar.activation(squares[b][i], positive[b][i], SQUARE, accum_out=total[:, i : i + 1])
             turned = psum.tile([P, PACK, P], F32, name="turn_p%d" % b)
             for t in range(PACK):
                 i, first = divmod(t * P, width)
@@ -157,7 +157,6 @@ def tile_attend_relu2_seg_kernel(tc, qT, kT, vT, vs, offs, out):
             nc.scalar.activation(y_sb[b][:, e0:e1], sums[:], COPY, scale=recip[:, b : b + 1])
 
         nc.vector.memset(vs_tab[0 : P - 1, :], 0.0)
-        nc.vector.memset(total[:, 1, 0:1], 0.0)
         nc.sync.dma_start(offsets[:], offs)
         nc.sync.dma_start(vs_tab[P - 1 : P, :], vs[0:1, :])
         make_identity(nc, ident[:])
@@ -224,10 +223,10 @@ def tile_attend_relu2_seg_kernel(tc, qT, kT, vT, vs, offs, out):
         gather_keys(True, 1, 2, 3 * N // 4, N)
         gather_keys(False, 1, 3, 0, N // 2)
         gather_keys(True, 1, 3, N // 2, N)
-        by_slot = keep.tile([P, P], F32, name="k_tab3")
-        nc.scalar.activation(by_slot[:], summed[:], COPY, accum_out=total[:, 0, 0:1])
         finish_keys(1)
         scores1 = score(1)
+        total0 = k_in[1][:, 0:2].bitcast(F32)
+        nc.vector.tensor_reduce(total0, summed[:], mybir.AxisListType.X, ADD)
         for b in range(B):
             for h in range(2):
                 got = keep.tile([P, N], BF16, name="v_got%d%d" % (b, h), align_bytes=64)
@@ -241,9 +240,9 @@ def tile_attend_relu2_seg_kernel(tc, qT, kT, vT, vs, offs, out):
             MULT,
         )
         gather_values(True, 0, 0)
-        gather_values(False, 0, 1, 0, 3 * N // 8)
-        gather_values(True, 0, 1, 3 * N // 8, N)
-        turned_v0 = psum.tile([P, 2, 2, P], F32, name="turn_v0")
+        gather_values(False, 0, 1, 0, N // 4)
+        gather_values(True, 0, 1, N // 4, N)
+        turned_v0 = psum.tile([P, 2, 2, P], F32, name="turn_p0")
         for h in range(2):
             turn_values(0, h, turned_v0[:, h])
         positive1 = keep.tile([P, N], F32, name="v_tab01")
@@ -267,7 +266,8 @@ def tile_attend_relu2_seg_kernel(tc, qT, kT, vT, vs, offs, out):
         nc.scalar.copy(
             v0_in[:].bitcast(F32).rearrange("s (h e u) -> s h e u", h=2, u=2), turned_v0[:].rearrange("s h u e -> s h e u")
         )
-        nc.vector.scalar_tensor_tensor(total_and_one[:], total[:, 0, :], 1.0, total[:, 1, :], ADD, ADD)
+        nc.vector.tensor_scalar_add(total_and_one[:, 0:1], total0, 1.0)
+        nc.vector.scalar_tensor_tensor(total_and_one[:, 1:2], total[:, 0:1], 1.0, total[:, 1:2], ADD, ADD)
         weigh(1, turned1)
         nc.vector.reciprocal(recip[:], total_and_one[:])
         quantize(second_codes[0][:, 0:DV], second_scales[0][:, 0:DV], v0_in[:])
@@ -279,7 +279,7 @@ def tile_attend_relu2_seg_kernel(tc, qT, kT, vT, vs, offs, out):
         quantize(second_codes[1][:, DV:wide], second_scales[1][:, DV:wide], w_in[1])
         finish(0, 0, DV, "product0")
         nc.sync.dma_start(out[0], y_sb[0][:])
-        for h, tag in enumerate(("product1", "turn_p0")):
+        for h, tag in enumerate(("product1", "product2")):
             cols = slice(h * HALF, (h + 1) * HALF)
             quantize(second_codes[1][:, cols], second_scales[1][:, cols], v1_in[:, h * HALF * PACK : (h + 1) * HALF * PACK])
             finish(1, h * HALF, (h + 1) * HALF, tag)

@@ -212,15 +212,15 @@ def tile_attend_relu2_seg_kernel(tc, qT, kT, vT, vs, offs, out):
         for i in range(2):
             nc.scalar.activation(positive[0][i], scores0[i][:].rearrange("s r q -> s (r q)"), RELU)
         for i in range(2):
-            nc.scalar.activation(squares[0][i], positive[0][i], SQUARE)
+            nc.gpsimd.tensor_tensor(squares[0][i], positive[0][i], positive[0][i], MULT)
         summed = psum.tile([P, P], F32, name="turn_p0")
         for t in range(PACK):
             nc.tensor.matmul(
                 summed[:], squares0[:, t * P : (t + 1) * P], ident[:],
                 start=(t == 0), stop=(t == PACK - 1), is_transpose=True,
             )
-        gather_keys(False, 1, 2, 0, 3 * N // 4)
-        gather_keys(True, 1, 2, 3 * N // 4, N)
+        gather_keys(False, 1, 2, 0, N // 2)
+        gather_keys(True, 1, 2, N // 2, N)
         gather_keys(False, 1, 3, 0, N // 2)
         gather_keys(True, 1, 3, N // 2, N)
         finish_keys(1)

@@ -37,12 +37,12 @@ def tile_attend_relu2_seg_kernel(tc, qT, kT, vT, vs, offs, out):
         vs_got = keep.tile([P, B * N], F32, name="vs_got")
         ident = keep.tile([P, P], F32, name="ident")
         q_raw = keep.tile([P, B, PACK * NQ], F32, name="q_raw")
-        q_in = keep.tile([P, B * NQ * PACK], BF16, name="q_in", align_bytes=64)
-        q_codes = keep.tile([P, B * NQ], U32, name="q_codes", align_bytes=64)
+        q0_in = keep.tile([P, NQ * PACK], BF16, name="q0_in", align_bytes=64)
+        q_codes = [keep.tile([P, NQ], U32, name="q_codes0", align_bytes=64)]
         q_scales = keep.tile([P, B * NQ], U8, name="q_scales", align_bytes=64)
-        first_two = keep.tile([P, 2 * T], F32, name="k_tab1")
+        first_two = keep.tile([P, 2 * T], F32, name="k_tab1", align_bytes=64)
         k_tab = [first_two[:, 0:T], first_two[:, T : 2 * T]]
-        k_tab += [keep.tile([P, T], F32, name="k_tab%d" % t)[:] for t in (2, 3)]
+        k_tab += [keep.tile([P, T], F32, name="k_tab%d" % t, align_bytes=64)[:] for t in (2, 3)]
         k_in = [keep.tile([P, N * PACK], BF16, name="k_in%d" % b, align_bytes=64) for b in range(B)]
         k_codes = [keep.tile([P, N], U32, name="k_codes%d" % b, align_bytes=64) for b in range(B)]
         k_scales = [keep.tile([P, N], U8, name="k_scales%d" % b, align_bytes=64) for b in range(B)]
@@ -118,7 +118,7 @@ def tile_attend_relu2_seg_kernel(tc, qT, kT, vT, vs, offs, out):
             for i in range(parts):
                 sums = psum.tile([P, width], F32, name="product%d" % i)
                 cols = slice(i * width, (i + 1) * width)
-                product(sums[:], q_codes[:, b * NQ : (b + 1) * NQ], q_scales[:, b * NQ : (b + 1) * NQ], k_codes[b][:, cols], k_scales[b][:, cols])
+                product(sums[:], q_codes[b][:], q_scales[:, b * NQ : (b + 1) * NQ], k_codes[b][:, cols], k_scales[b][:, cols])
                 banks.append(sums)
             return banks
 
@@ -189,24 +189,27 @@ def tile_attend_relu2_seg_kernel(tc, qT, kT, vT, vs, offs, out):
         gather_keys(True, 0, 2, N // 2, N)
         gather_keys(False, 0, 3, 0, N // 2)
         gather_keys(True, 0, 3, N // 2, N)
-        nc.scalar.activation(
-            q_in[:].rearrange("p (b q j) -> p b q j", b=B, j=PACK),
-            q_raw[:].rearrange("p b (j q) -> p b q j", j=PACK),
-            COPY,
-        )
+        q_rows = q_raw[:].rearrange("p b (j c i) -> p b c j i", i=PACK, j=PACK)
+        nc.scalar.activation(q0_in[:].rearrange("p (c i j) -> p c j i", i=PACK, j=PACK), q_rows[:, 0], COPY)
         finish_keys(0)
-        quantize(q_codes[:], q_scales[:], q_in[:])
+        quantize(q_codes[0][:], q_scales[:, 0:NQ], q0_in[:])
+        q1_in = k_in[0][:, 3 * N : 4 * N]
+        nc.gpsimd.tensor_scalar(
+            q1_in.rearrange("p (c i j) -> p c j i", i=PACK, j=PACK), q_rows[:, 1], 1.0, 0.0, MULT, ADD
+        )
         scores0 = []
         for i in range(2):
             sums = psum.tile([P, 2, NQ], F32, name="product%d" % i)
             for r in range(2):
                 cols = slice((2 * i + r) * P, (2 * i + r + 1) * P)
-                product(sums[:, r, :], k_codes[0][:, cols], k_scales[0][:, cols], q_codes[:, 0:NQ], q_scales[:, 0:NQ])
+                product(sums[:, r, :], k_codes[0][:, cols], k_scales[0][:, cols], q_codes[0][:], q_scales[:, 0:NQ])
             scores0.append(sums)
-        scale_cols[0] = keep.tile([P, B * PACK], F32, name="k_in0", align_bytes=64)
-        nc.vector.tensor_copy(scale_cols[0][:], turned_flat[:, P - 1 : P - 1 + 2 * B * PACK : 2])
+        scale_cols[0] = k_in[0][:, 0 : 2 * B * PACK].bitcast(F32)
+        nc.vector.tensor_copy(scale_cols[0], turned_flat[:, P - 1 : P - 1 + 2 * B * PACK : 2])
         gather_keys(True, 1, 0)
         gather_keys(False, 1, 1)
+        q_codes.append(keep.tile([P, NQ], U32, name="k_tab1", align_bytes=64))
+        quantize(q_codes[1][:], q_scales[:, NQ : B * NQ], q1_in)
         positive0 = keep.tile([P, N], F32, name="positive0")
         positive[0] = [positive0[:, 0 : N // 2], positive0[:, N // 2 : N]]
         for i in range(2):
@@ -219,8 +222,8 @@ def tile_attend_relu2_seg_kernel(tc, qT, kT, vT, vs, offs, out):
                 summed[:], squares0[:, t * P : (t + 1) * P], ident[:],
                 start=(t == 0), stop=(t == PACK - 1), is_transpose=True,
             )
-        gather_keys(False, 1, 2, 0, N // 2)
-        gather_keys(True, 1, 2, N // 2, N)
+        gather_keys(False, 1, 2, 0, 3 * N // 8)
+        gather_keys(True, 1, 2, 3 * N // 8, N)
         gather_keys(False, 1, 3, 0, N // 2)
         gather_keys(True, 1, 3, N // 2, N)
         finish_keys(1)

@@ -55,7 +55,6 @@ def tile_attend_relu2_seg_kernel(tc, qT, kT, vT, vs, offs, out):
         squares0 = keep.tile([P, N], F32, name="squares0")
         squares = [[squares0[:, 0 : N // 2], squares0[:, N // 2 : N]], None]
         total = keep.tile([P, 2], F32, name="total")
-        recip = keep.tile([P, B], F32, name="recip")
         y_sb = [keep.tile([P, DV], F32, name="y_sb%d" % b) for b in range(B)]
 
         work = keep.tile([P, 20 * P], F32, name="work", align_bytes=64)
@@ -94,8 +93,11 @@ def tile_attend_relu2_seg_kernel(tc, qT, kT, vT, vs, offs, out):
         def finish_keys(b):
             laid = k_in[b][:].rearrange("p (r s t) -> p s t r", r=PACK, t=PACK)
             rows = planes[b].rearrange("p (t s r) -> p s t r", t=PACK, r=PACK)
-            for r0 in (0, 2):
-                nc.vector.tensor_copy(laid[:, :, :, r0 : r0 + 2], rows[:, :, :, r0 : r0 + 2])
+            cut = 5 * P // 8 if b else P
+            nc.vector.tensor_copy(laid[:, :, :, 0:2], rows[:, :, :, 0:2])
+            nc.vector.tensor_copy(laid[:, 0:cut, :, 2:4], rows[:, 0:cut, :, 2:4])
+            if cut < P:
+                nc.scalar.copy(laid[:, cut:P, :, 2:4], rows[:, cut:P, :, 2:4])
             for n0 in (0, N // 2):
                 n1 = n0 + N // 2
                 quantize(k_codes[b][:, n0:n1], k_scales[b][:, n0:n1], k_in[b][:, n0 * PACK : n1 * PACK])
@@ -147,7 +149,7 @@ def tile_attend_relu2_seg_kernel(tc, qT, kT, vT, vs, offs, out):
                 source = words[:, u * P : (u + 1) * P] if (b, h) == (1, 0) else words[:, u : N // 2 : 2]
                 nc.tensor.transpose(turned[:, u, :], source, ident[:])
 
-        def finish(b, e0, e1, tag):
+        def finish(b, e0, e1, tag, recip):
             sums = psum.tile([P, e1 - e0], F32, name=tag)
             product(
                 sums[:],
@@ -243,8 +245,8 @@ def tile_attend_relu2_seg_kernel(tc, qT, kT, vT, vs, offs, out):
             MULT,
         )
         gather_values(True, 0, 0)
-        gather_values(False, 0, 1, 0, N // 4)
-        gather_values(True, 0, 1, N // 4, N)
+        gather_values(False, 0, 1, 0, 3 * N // 8)
+        gather_values(True, 0, 1, 3 * N // 8, N)
         turned_v0 = psum.tile([P, 2, 2, P], F32, name="turn_p0")
         for h in range(2):
             turn_values(0, h, turned_v0[:, h])
@@ -264,13 +266,14 @@ def tile_attend_relu2_seg_kernel(tc, qT, kT, vT, vs, offs, out):
         v0_in = later("v0_in", 0, [P, DV * PACK], BF16)
         v1_in = later("v1_in", 4, [P, DV * PACK], BF16)
         w1_in = later("w1_in", 8, [P, NQ * PACK], BF16)
-        total_and_one = later("total_and_one", 10, [P, B], F32)
+        total_and_one = keep.tile([P, B], F32, name="total_and_one")
+        recip = later("recip", 10, [P, B], F32)
         w_in[1] = w1_in[:]
         nc.scalar.copy(
             v0_in[:].bitcast(F32).rearrange("s (h e u) -> s h e u", h=2, u=2), turned_v0[:].rearrange("s h u e -> s h e u")
         )
-        nc.vector.tensor_scalar_add(total_and_one[:, 0:1], total0, 1.0)
-        nc.vector.scalar_tensor_tensor(total_and_one[:, 1:2], total[:, 0:1], 1.0, total[:, 1:2], ADD, ADD)
+        nc.gpsimd.tensor_scalar_add(total_and_one[:, 0:1], total0, 1.0)
+        nc.gpsimd.tensor_scalar(total_and_one[:, 1:2], total[:, 0:1], 1.0, total[:, 1:2], ADD, ADD)
         weigh(1, turned1)
         nc.vector.reciprocal(recip[:], total_and_one[:])
         quantize(second_codes[0][:, 0:DV], second_scales[0][:, 0:DV], v0_in[:])
@@ -280,10 +283,10 @@ def tile_attend_relu2_seg_kernel(tc, qT, kT, vT, vs, offs, out):
             pairs = v1_in[:, h * HALF * PACK : (h + 1) * HALF * PACK].bitcast(F32)
             nc.scalar.copy(pairs.rearrange("s (e u) -> s e u", u=2), turned[:].rearrange("s u e -> s e u"))
         quantize(second_codes[1][:, DV:wide], second_scales[1][:, DV:wide], w_in[1])
-        finish(0, 0, DV, "product0")
+        finish(0, 0, DV, "product0", recip)
         nc.sync.dma_start(out[0], y_sb[0][:])
         for h, tag in enumerate(("product1", "product2")):
             cols = slice(h * HALF, (h + 1) * HALF)
             quantize(second_codes[1][:, cols], second_scales[1][:, cols], v1_in[:, h * HALF * PACK : (h + 1) * HALF * PACK])
-            finish(1, h * HALF, (h + 1) * HALF, tag)
-        nc.scalar.dma_start(out[1], y_sb[1][:])
+            finish(1, h * HALF, (h + 1) * HALF, tag, recip)
+        nc.sync.dma_start(out[1], y_sb[1][:])

@@ -153,14 +153,14 @@ def tile_attend_relu2_seg_kernel(tc, qT, kT, vT, vs, offs, out):
             sums = psum.tile([P, e1 - e0], F32, name=tag)
             product(
                 sums[:],
-                second_codes[b][:, DV:wide], second_scales[b][:, DV:wide],
-                second_codes[b][:, e0:e1], second_scales[b][:, e0:e1],
+                second_codes[b][:, 0:NQ], second_scales[b][:, 0:NQ],
+                second_codes[b][:, NQ + e0 : NQ + e1], second_scales[b][:, NQ + e0 : NQ + e1],
             )
             nc.scalar.activation(y_sb[b][:, e0:e1], sums[:], COPY, scale=recip[:, b : b + 1])
 
         nc.vector.memset(vs_tab[0 : P - 1, :], 0.0)
         nc.sync.dma_start(offsets[:], offs)
-        nc.sync.dma_start(vs_tab[P - 1 : P, :], vs[0:1, :])
+        nc.scalar.dma_start(vs_tab[P - 1 : P, :], vs[0:1, :])
         make_identity(nc, ident[:])
         for h in range(2):
             nc.gpsimd.memset(v_tab[1][h][:, 0:SEG], 0.0)
@@ -262,13 +262,13 @@ def tile_attend_relu2_seg_kernel(tc, qT, kT, vT, vs, offs, out):
         gather_values(False, 1, 1, 0, cut)
         gather_values(True, 1, 1, cut, N)
         second_codes[0] = later("codes0", 11, [P, wide], U32)
-        quantize(second_codes[0][:, DV:wide], second_scales[0][:, DV:wide], w0_in)
+        quantize(second_codes[0][:, 0:NQ], second_scales[0][:, 0:NQ], w0_in)
         v0_in = later("v0_in", 0, [P, DV * PACK], BF16)
-        v1_in = later("v1_in", 4, [P, DV * PACK], BF16)
-        w1_in = later("w1_in", 8, [P, NQ * PACK], BF16)
+        both_in = later("both_in", 4, [P, wide * PACK], BF16)
+        w1_in, v1_in = both_in[:, 0 : NQ * PACK], both_in[:, NQ * PACK : wide * PACK]
         total_and_one = keep.tile([P, B], F32, name="total_and_one")
         recip = later("recip", 10, [P, B], F32)
-        w_in[1] = w1_in[:]
+        w_in[1] = w1_in
         nc.scalar.copy(
             v0_in[:].bitcast(F32).rearrange("s (h e u) -> s h e u", h=2, u=2), turned_v0[:].rearrange("s h u e -> s h e u")
         )
@@ -276,17 +276,16 @@ def tile_attend_relu2_seg_kernel(tc, qT, kT, vT, vs, offs, out):
         nc.gpsimd.tensor_scalar(total_and_one[:, 1:2], total[:, 0:1], 1.0, total[:, 1:2], ADD, ADD)
         weigh(1, turned1)
         nc.vector.reciprocal(recip[:], total_and_one[:])
-        quantize(second_codes[0][:, 0:DV], second_scales[0][:, 0:DV], v0_in[:])
+        quantize(second_codes[0][:, NQ:wide], second_scales[0][:, NQ:wide], v0_in[:])
         for h, tag in enumerate(("turn_v1", "turn_scales")):
             turned = psum.tile([P, 2, P], F32, name=tag)
             turn_values(1, h, turned)
             pairs = v1_in[:, h * HALF * PACK : (h + 1) * HALF * PACK].bitcast(F32)
             nc.scalar.copy(pairs.rearrange("s (e u) -> s e u", u=2), turned[:].rearrange("s u e -> s e u"))
-        quantize(second_codes[1][:, DV:wide], second_scales[1][:, DV:wide], w_in[1])
         finish(0, 0, DV, "product0", recip)
         nc.sync.dma_start(out[0], y_sb[0][:])
         for h, tag in enumerate(("product1", "product2")):
-            cols = slice(h * HALF, (h + 1) * HALF)
-            quantize(second_codes[1][:, cols], second_scales[1][:, cols], v1_in[:, h * HALF * PACK : (h + 1) * HALF * PACK])
+            c0, c1 = (NQ + HALF) * h, NQ + HALF * (h + 1)
+            quantize(second_codes[1][:, c0:c1], second_scales[1][:, c0:c1], both_in[:, c0 * PACK : c1 * PACK])
             finish(1, h * HALF, (h + 1) * HALF, tag, recip)
         nc.sync.dma_start(out[1], y_sb[1][:])

from contextlib import ExitStack

import concourse.mybir as mybir
from concourse.masks import make_identity

B, NQ, N, T, D, DV = 2, 128, 512, 2048, 512, 256
P = 128
PACK = 4
SEG = T // B
HALF = DV // 2
LIST_ROWS = 16

F32 = mybir.dt.float32
BF16 = mybir.dt.bfloat16
U32 = mybir.dt.uint32
U16 = mybir.dt.uint16
U8 = mybir.dt.uint8
FP8X4 = mybir.dt.float8_e4m3fn_x4
COPY = mybir.ActivationFunctionType.Copy
RELU = mybir.ActivationFunctionType.Relu
SQUARE = mybir.ActivationFunctionType.Square
MULT = mybir.AluOpType.mult
ADD = mybir.AluOpType.add

FLOPS = 2 * B * NQ * N * (D + DV)
BYTES = 4 * (B * D * NQ + D * T + DV * T + T + B * NQ * DV) + 2 * P * (B * N // LIST_ROWS)


def tile_attend_relu2_seg_kernel(tc, qT, kT, vT, vs, offs, out):
    nc = tc.nc
    with ExitStack() as ctx:
        keep = ctx.enter_context(tc.tile_pool(name="keep", bufs=1))
        psum = ctx.enter_context(tc.psum_pool(name="psum", bufs=1))

        offsets = keep.tile([P, B * N // LIST_ROWS], U16, name="offsets")
        vs_tab = keep.tile([P, T], F32, name="vs_tab")
        vs_got = keep.tile([P, B * N], F32, name="vs_got")
        ident = keep.tile([P, P], F32, name="ident")
        q_raw = keep.tile([P, B, PACK * NQ], F32, name="q_raw")
        q0_in = keep.tile([P, NQ * PACK], BF16, name="q0_in", align_bytes=64)
        q_codes = [keep.tile([P, NQ], U32, name="q_codes0", align_bytes=64)]
        q_scales = keep.tile([P, B * NQ], U8, name="q_scales", align_bytes=64)
        first_two = keep.tile([P, 2 * T], F32, name="k_tab1", align_bytes=64)
        k_tab = [first_two[:, 0:T], first_two[:, T : 2 * T]]
        k_tab += [keep.tile([P, T], F32, name="k_tab%d" % t, align_bytes=64)[:] for t in (2, 3)]
        k_in = [keep.tile([P, N * PACK], BF16, name="k_in%d" % b, align_bytes=64) for b in range(B)]
        k_codes = [keep.tile([P, N], U32, name="k_codes%d" % b, align_bytes=64) for b in range(B)]
        k_scales = [keep.tile([P, N], U8, name="k_scales%d" % b, align_bytes=64) for b in range(B)]
        shared = ctx.enter_context(tc.tile_pool(name="shared", bufs=1))
        v_tab = [[keep.tile([P, (b + 1) * SEG], F32, name="v_tab%d%d" % (b, h)) for h in range(2 - b)] for b in range(B)]
        v_tab[1].append(shared.tile([P, T], F32, name="v_tab11", offset=0, align_bytes=64))
        wide = NQ + DV
        second_codes = [None, keep.tile([P, wide], U32, name="second_codes1", align_bytes=64)]
        second_scales = [keep.tile([P, wide], U8, name="second_scales%d" % b, align_bytes=64) for b in range(B)]
        squares0 = keep.tile([P, N], F32, name="squares0")
        squares = [[squares0[:, 0 : N // 2], squares0[:, N // 2 : N]], None]
        total = keep.tile([P, 2], F32, name="total")
        y_sb = [keep.tile([P, DV], F32, name="y_sb%d" % b) for b in range(B)]

        work = keep.tile([P, 20 * P], F32, name="work", align_bytes=64)

        def blocks(a0, a1):
            return work[:, a0 * P : a1 * P]

        planes = [blocks(4, 20), blocks(0, 16)]
        positive = [None, None]
        v_got = [[None, None], [None, None]]
        scale_cols = [None]
        w_in = [None, None]

        def later(name, kib, shape, dtype):
            return shared.tile(shape, dtype, name=name, offset=kib * 512, align_bytes=64)

        key_rows = kT.rearrange("(p j) n -> p j n", j=PACK)

        def gather(on_scalar, target, window, b, n0, n1):
            first = (b * N + n0) // LIST_ROWS
            picked = window.indirect(offsets[:, first : first + (n1 - n0) // LIST_ROWS])
            if on_scalar:
                nc.scalar.activation(target, picked, COPY)
            else:
                nc.vector.tensor_copy(target, picked)

        def gather_keys(on_scalar, b, t, n0=0, n1=N):
            gather(on_scalar, planes[b][:, t * N + n0 : t * N + n1], k_tab[t][:, 0 : (b + 1) * SEG], b, n0, n1)

        def gather_values(on_scalar, b, h, n0=0, n1=N):
            gather(on_scalar, v_got[b][h][:, n0:n1], v_tab[b][h][:], b, n0, n1)

        def quantize(codes, scales, source):
            nc.vector.quantize_mx(out=codes.bitcast(FP8X4), scales=scales, in_=source)

        def finish_keys(b):
            laid = k_in[b][:].rearrange("p (r s t) -> p s t r", r=PACK, t=PACK)
            rows = planes[b].rearrange("p (t s r) -> p s t r", t=PACK, r=PACK)
            cut = 5 * P // 8 if b else P
            nc.vector.tensor_copy(laid[:, :, :, 0:2], rows[:, :, :, 0:2])
            nc.vector.tensor_copy(laid[:, 0:cut, :, 2:4], rows[:, 0:cut, :, 2:4])
            if cut < P:
                nc.scalar.copy(laid[:, cut:P, :, 2:4], rows[:, cut:P, :, 2:4])
            for n0 in (0, N // 2):
                n1 = n0 + N // 2
                quantize(k_codes[b][:, n0:n1], k_scales[b][:, n0:n1], k_in[b][:, n0 * PACK : n1 * PACK])

        def product(sums, left_codes, left_scales, right_codes, right_scales):
            nc.tensor.matmul_mx(
                out=sums,
                lhsT=left_codes.bitcast(FP8X4),
                lhsT_scale=left_scales,
                rhs=right_codes.bitcast(FP8X4),
                rhs_scale=right_scales,
                start=True,
                stop=True,
            )

        def score(b):
            parts = 2
            width = N // parts
            banks = []
            for i in range(parts):
                sums = psum.tile([P, width], F32, name="product%d" % i)
                cols = slice(i * width, (i + 1) * width)
                product(sums[:], q_codes[b][:], q_scales[:, b * NQ : (b + 1) * NQ], k_codes[b][:, cols], k_scales[b][:, cols])
                banks.append(sums)
            return banks

        def relu(b, banks):
            for i, sums in enumerate(banks):
                nc.scalar.activation(positive[b][i], sums[:], RELU)

        def square_and_turn(b, banks):
            width = N // len(banks)
            for i in range(len(banks)):
                nc.scalar.activation(squares[b][i], positive[b][i], SQUARE, accum_out=total[:, i : i + 1])
            turned = psum.tile([P, PACK, P], F32, name="turn_p%d" % b)
            for t in range(PACK):
                i, first = divmod(t * P, width)
                nc.tensor.transpose(turned[:, t, :], squares[b][i][:, first : first + P], ident[:])
            return turned

        def weigh(b, turned):
            target = w_in[b].rearrange("s (q t) -> s q t", t=PACK)
            spread = scale_cols[0][:, b * PACK : (b + 1) * PACK].unsqueeze(1).to_broadcast([P, NQ, PACK])
            nc.vector.tensor_tensor(target, turned[:].rearrange("s t q -> s q t"), spread, MULT)

        def turn_values(b, h, turned):
            for u in range(2):
                words = v_got[b][h].bitcast(F32)
                source = words[:, u * P : (u + 1) * P] if (b, h) == (1, 0) else words[:, u : N // 2 : 2]
                nc.tensor.transpose(turned[:, u, :], source, ident[:])

        def finish(b, e0, e1, tag, recip):
            sums = psum.tile([P, e1 - e0], F32, name=tag)
            product(
                sums[:],
                second_codes[b][:, 0:NQ], second_scales[b][:, 0:NQ],
                second_codes[b][:, NQ + e0 : NQ + e1], second_scales[b][:, NQ + e0 : NQ + e1],
            )
            nc.scalar.activation(y_sb[b][:, e0:e1], sums[:], COPY, scale=recip[:, b : b + 1])

        nc.vector.memset(vs_tab[0 : P - 1, :], 0.0)
        nc.sync.dma_start(offsets[:], offs)
        nc.scalar.dma_start(vs_tab[P - 1 : P, :], vs[0:1, :])
        make_identity(nc, ident[:])
        for h in range(2):
            nc.gpsimd.memset(v_tab[1][h][:, 0:SEG], 0.0)

        nc.sync.dma_start(first_two[:].rearrange("p (t n) -> p t n", t=2)[:, :, 0:SEG], key_rows[:, 0:2, 0:SEG])
        for t in (2, 3):
            nc.sync.dma_start(k_tab[t][:, 0:SEG], key_rows[:, t, 0:SEG])
        nc.sync.dma_start(q_raw[:], qT.rearrange("b (p j) q -> p b (j q)", j=PACK))
        for t in range(PACK):
            nc.sync.dma_start(k_tab[t][:, SEG:T], key_rows[:, t, SEG:T])
        for b in range(B):
            for h in range(2):
                nc.sync.dma_start(v_tab[b][h][:, b * SEG : (b + 1) * SEG], vT[h * P : (h + 1) * P, b * SEG : (b + 1) * SEG])

        gather(False, vs_got[:, 0:N].rearrange("p (t s) -> p s t", t=PACK), vs_tab[:], 0, 0, N)
        gather(False, vs_got[:, N : N + N // 2], vs_tab[:], 1, 0, N // 2)
        gather(True, vs_got[:, N + N // 2 : B * N], vs_tab[:], 1, N // 2, N)
        turned_scales = psum.tile([P, PACK, P], F32, name="turn_scales")
        turned_flat = turned_scales[:].rearrange("s t e -> s (t e)")
        for k in reversed(range(B * PACK)):
            b, t = divmod(k, PACK)
            source = vs_got[:, N + t : B * N : PACK] if b else vs_got[:, t * P : (t + 1) * P]
            nc.tensor.transpose(turned_flat[:, 2 * k : 2 * k + P], source, ident[:])

        gather_keys(False, 0, 0)
        gather_keys(True, 0, 1)
        gather_keys(False, 0, 2, 0, N // 2)
        gather_keys(True, 0, 2, N // 2, N)
        gather_keys(False, 0, 3, 0, N // 2)
        gather_keys(True, 0, 3, N // 2, N)
        q_rows = q_raw[:].rearrange("p b (j c i) -> p b c j i", i=PACK, j=PACK)
        nc.scalar.activation(q0_in[:].rearrange("p (c i j) -> p c j i", i=PACK, j=PACK), q_rows[:, 0], COPY)
        finish_keys(0)
        quantize(q_codes[0][:], q_scales[:, 0:NQ], q0_in[:])
        q1_in = k_in[0][:, 3 * N : 4 * N]
        nc.gpsimd.tensor_scalar(
            q1_in.rearrange("p (c i j) -> p c j i", i=PACK, j=PACK), q_rows[:, 1], 1.0, 0.0, MULT, ADD
        )
        scores0 = []
        for i in range(2):
            sums = psum.tile([P, 2, NQ], F32, name="product%d" % i)
            for r in range(2):
                cols = slice((2 * i + r) * P, (2 * i + r + 1) * P)
                product(sums[:, r, :], k_codes[0][:, cols], k_scales[0][:, cols], q_codes[0][:], q_scales[:, 0:NQ])
            scores0.append(sums)
        scale_cols[0] = k_in[0][:, 0 : 2 * B * PACK].bitcast(F32)
        nc.vector.tensor_copy(scale_cols[0], turned_flat[:, P - 1 : P - 1 + 2 * B * PACK : 2])
        gather_keys(True, 1, 0)
        gather_keys(False, 1, 1)
        q_codes.append(keep.tile([P, NQ], U32, name="k_tab1", align_bytes=64))
        quantize(q_codes[1][:], q_scales[:, NQ : B * NQ], q1_in)
        positive0 = keep.tile([P, N], F32, name="positive0")
        positive[0] = [positive0[:, 0 : N // 2], positive0[:, N // 2 : N]]
        for i in range(2):
            nc.scalar.activation(positive[0][i], scores0[i][:].rearrange("s r q -> s (r q)"), RELU)
        for i in range(2):
            nc.gpsimd.tensor_tensor(squares[0][i], positive[0][i], positive[0][i], MULT)
        summed = psum.tile([P, P], F32, name="turn_p0")
        for t in range(PACK):
            nc.tensor.matmul(
                summed[:], squares0[:, t * P : (t + 1) * P], ident[:],
                start=(t == 0), stop=(t == PACK - 1), is_transpose=True,
            )
        gather_keys(False, 1, 2, 0, 3 * N // 8)
        gather_keys(True, 1, 2, 3 * N // 8, N)
        gather_keys(False, 1, 3, 0, N // 2)
        gather_keys(True, 1, 3, N // 2, N)
        finish_keys(1)
        scores1 = score(1)
        total0 = k_in[1][:, 0:2].bitcast(F32)
        nc.vector.tensor_reduce(total0, summed[:], mybir.AxisListType.X, ADD)
        for b in range(B):
            for h in range(2):
                got = keep.tile([P, N], BF16, name="v_got%d%d" % (b, h), align_bytes=64)
                v_got[b][h] = got[:]
        w0_in = k_in[1][:, 2 * N : 3 * N]
        spread = scale_cols[0][:, 0:PACK].unsqueeze(1).unsqueeze(3).to_broadcast([P, NQ // PACK, PACK, PACK])
        nc.gpsimd.tensor_tensor(
            w0_in.rearrange("s (c i t) -> s c t i", i=PACK, t=PACK),
            squares0[:].rearrange("s (t c i) -> s c t i", t=PACK, i=PACK),
            spread,
            MULT,
        )
        gather_values(True, 0, 0)
        gather_values(False, 0, 1, 0, 3 * N // 8)
        gather_values(True, 0, 1, 3 * N // 8, N)
        turned_v0 = psum.tile([P, 2, 2, P], F32, name="turn_p0")
        for h in range(2):
            turn_values(0, h, turned_v0[:, h])
        positive1 = keep.tile([P, N], F32, name="v_tab01")
        positive[1] = [positive1[:, 0 : N // 2], positive1[:, N // 2 : N]]
        relu(1, scores1)
        dealt = v_got[1][0].rearrange("p (u s e) -> p s u e", u=2, e=2)
        gather(False, dealt, v_tab[1][0][:], 1, 0, N)
        halves = [keep.tile([P, N // 2], F32, name=tag) for tag in ("squares1a", "squares1b")]
        squares[1] = [half[:] for half in halves]
        turned1 = square_and_turn(1, scores1)
        cut = 5 * N // 8
        gather_values(False, 1, 1, 0, cut)
        gather_values(True, 1, 1, cut, N)
        second_codes[0] = later("codes0", 11, [P, wide], U32)
        quantize(second_codes[0][:, 0:NQ], second_scales[0][:, 0:NQ], w0_in)
        v0_in = later("v0_in", 0, [P, DV * PACK], BF16)
        both_in = later("both_in", 4, [P, wide * PACK], BF16)
        w1_in, v1_in = both_in[:, 0 : NQ * PACK], both_in[:, NQ * PACK : wide * PACK]
        total_and_one = keep.tile([P, B], F32, name="total_and_one")
        recip = later("recip", 10, [P, B], F32)
        w_in[1] = w1_in
        nc.scalar.copy(
            v0_in[:].bitcast(F32).rearrange("s (h e u) -> s h e u", h=2, u=2), turned_v0[:].rearrange("s h u e -> s h e u")
        )
        nc.gpsimd.tensor_scalar_add(total_and_one[:, 0:1], total0, 1.0)
        nc.gpsimd.tensor_scalar(total_and_one[:, 1:2], total[:, 0:1], 1.0, total[:, 1:2], ADD, ADD)
        weigh(1, turned1)
        nc.vector.reciprocal(recip[:], total_and_one[:])
        quantize(second_codes[0][:, NQ:wide], second_scales[0][:, NQ:wide], v0_in[:])
        for h, tag in enumerate(("turn_v1", "turn_scales")):
            turned = psum.tile([P, 2, P], F32, name=tag)
            turn_values(1, h, turned)
            pairs = v1_in[:, h * HALF * PACK : (h + 1) * HALF * PACK].bitcast(F32)
            nc.scalar.copy(pairs.rearrange("s (e u) -> s e u", u=2), turned[:].rearrange("s u e -> s e u"))
        finish(0, 0, DV, "product0", recip)
        nc.sync.dma_start(out[0], y_sb[0][:])
        for h, tag in enumerate(("product1", "product2")):
            c0, c1 = (NQ + HALF) * h, NQ + HALF * (h + 1)
            quantize(second_codes[1][:, c0:c1], second_scales[1][:, c0:c1], both_in[:, c0 * PACK : c1 * PACK])
            finish(1, h * HALF, (h + 1) * HALF, tag, recip)
        nc.sync.dma_start(out[1], y_sb[1][:])
